import numpy as np, ml_dtypes
CORES = [10,34,74,98]
N = 4
BF = ml_dtypes.bfloat16
W, S, H, R, CAP, HOP, ST = 2048, 256, 2048, 4, 256, 3, 341
P, E = W + R * S, S // N
AT = np.arange(W)
def hashed(u, lo, A):
    m = (61 * np.arange(16) + 7)[:, None]; u = u[:, :, None, :]
    return lo + (((u * u >> 5) + m * u + A[:, :, None, None]) & (W - 1))
def older(rng, *shape):
    return AT - 1 - np.minimum((AT * rng.random(shape + (W,)) ** 2).astype(np.int64), np.maximum(AT - 1, 0))
def parts(rng):
    off = rng.integers(-12, 9, (N, 8, 1, 1))
    X = np.clip(70 + rng.integers(-20, 21, (N, 8, 1, W)) + rng.integers(-60, 61, (N, 8, 16, W)), 0, 255)
    a = 2 * (70 + off + rng.integers(-20, 21, (N, 8, 1, S)) + rng.integers(-60, 61, (N, 8, 16, S))) + rng.integers(0, 2, (N, 8, 16, S))
    b = 80 + off + rng.integers(-50, 51, (N, 8, 1, (R - 1) * S)) + rng.integers(-100, 101, (N, 8, 16, (R - 1) * S))
    D = np.where(rng.random((N, 8, 16, W)) < 0.75, older(rng, N, 8, 16), -1); C = np.where(rng.random((N, 8, W)) < 0.9, older(rng, N, 8), -1)
    n = np.clip(W + S - 1 - ((W + S) * rng.random((N, 8, (R - 1) * S)) ** 2).astype(np.int64), 0, W + S - 1)
    return X, np.clip(np.concatenate([a, b], axis=3), 0, 255), D, C, n
def pack(X, a, D, C, n):
    return {"x0": X.reshape(N, 128, W).astype(np.float32).astype(BF), "come": a.reshape(N, 128, R * S).astype(np.float32).astype(BF),
            "dl0": np.ascontiguousarray(D[..., W - H:]).reshape(N, 128, H).astype(np.int32), "cd0": C.astype(np.int32), "age": n.astype(np.int32)}
def setup_inputs(rng):
    return pack(*parts(rng))
def setup_inputs_spread(rng):
    X = (256 * rng.random((N, 8, 16, W)) * np.exp2(-rng.integers(0, 7, (N, 8, 1, W)))).astype(np.int64)
    a = (256 * rng.random((N, 8, 16, R * S)) * np.exp2(-rng.integers(0, 5, (N, 8, 1, R * S)))).astype(np.int64)
    D = np.minimum(((AT + 1) * rng.random((N, 8, 16, W))).astype(np.int64), AT) - 1; C = np.minimum(((AT + 1) * rng.random((N, 8, W))).astype(np.int64), AT) - 1
    return pack(np.clip(X, 0, 255), np.clip(a, 0, 255), D, C, rng.integers(0, W + S, (N, 8, (R - 1) * S)))
def setup_inputs_ends(rng):
    X, a, D, C, n = parts(rng)
    def two(k):
        kind = rng.integers(0, 4, (N, 8, 1, k))
        return 255 * np.where(kind == 0, 0, np.where(kind == 1, 1, rng.integers(0, 2, (N, 8, 16, k))))
    X, a = two(W), two(R * S)
    r = rng.random(D.shape); D = np.where(r < 0.64, -1, np.where(r < 0.84, AT - 1, D))
    r = rng.random(C.shape); C = np.where(r < 0.64, -1, np.where(r < 0.84, AT - 1, C))
    n = (W + S - 1) * rng.integers(0, 2, n.shape)
    c = hashed(np.full((N, 8, 1), 16 * 127), 0, np.zeros((N, 8), np.int64))[0, 0, :, 0]
    X[..., c] = 255; C[..., c] = -1; X[:, 7, :, 0] = 255; X[:, 7, :, W - 1] = 255
    D[..., W - 1] = np.where(np.arange(16) % 2 == 0, W - 2, -1); C[:, ::2, W - 1] = -1; C[:, 1::2, W - 1] = W - 2
    last = np.arange(E - 1, S, E); a[..., last] = 255; a[..., S + last] = 255; n[..., last] = W + S - 1
    X[:, 5] = 0; X[:, 6] = 0; X[:, 6, :, W - 1] = 255; X[0, 7] = 0
    s = 4000 + np.array([11, 21, 27, 37, 43, 53, 59, 69]); h = hashed(np.zeros((N, 8, 8), np.int64) + s, S, np.zeros((N, 8), np.int64))[0, 0]
    good = h[15][h[15] < W]; half = 255 * (np.arange(16) % 2 == 0).astype(np.int64)[:, None]
    X4 = X[:, 4]; X4[:, :6] = 255; X4[..., h[h < W]] = half; X4[..., S] = half[:, 0]; X4[..., good] = 255
    C[:, 4, good] = -1; C[:, 4, int(np.min(good))] = S
    a[:, 4, :, :S] = 255; n[:, 4, :S] = W + S - 1; n[:, 4, S + 1:2 * S:2] = W + S - 1
    u = rng.integers(3841, 4075, (N, S)); u[:, 1::2] = s[np.arange(S // 2) & 7]; short = 4080 - u
    lack = (short >> 4)[:, None, :] + (((np.arange(16)[:, None] + np.arange(S)) & 15) < (short & 15)[:, None, :]).astype(np.int64)
    a[:, 4, :, S:2 * S] = 255 - 2 * lack
    a[:, 4, :6, 2 * S:] = 0; a[:, 4, :, 2 * S + 1:3 * S:2] = 255; a[:, 4, :6, 2 * S + 1:3 * S:2] = 253
    return pack(X, a, D, C, n)
def setup_inputs_corners(rng):
    X, a, D, C, n = parts(rng); X = 128 + (X >> 1); F = W // 8
    kind = rng.integers(0, 4, (N, 8, 1, W))
    D = np.where(kind == 0, -1, np.where(kind == 1, D[:, :, :1], D)); C[:, 1::3] = AT - 1
    edge = np.array([W - 1, ST - 1, ST])
    for q in range(N):
        for g in range(8):
            xg, dg, cg = X[q, g], D[q, g], C[q, g]
            dead = np.unique(np.append(rng.integers(1, F, 7), 0)); xg[:, dead] = 0
            cg[np.isin(cg, dead)] = -1
            k = (0, 1, CAP - 1, CAP, CAP + 1, W - F, CAP, CAP + 1)[(g + q) % 8]
            o = np.append(edge, rng.permutation(np.setdiff1d(np.arange(F, W), edge)))[:k]
            cg[o] = rng.choice(dead, len(o))
            gone = np.flatnonzero(kind[q, g, 0] == 2); gone = gone[gone >= F]; dg[:, gone] = rng.choice(dead, (16, len(gone)))
    x = a[..., :S] >> 1; c = hashed(np.add.reduce(x, axis=2), 0, np.zeros((N, 8), np.int64))
    live = np.max(X, axis=2) > 0; ok = np.take_along_axis(live, c.reshape(N, 8, 16 * S), 2).reshape(c.shape)
    up = np.max(np.where(ok, c, -1), axis=2); up2 = np.take_along_axis(C, np.maximum(up, 0), 2)
    y, y2 = W + S - 1 - up, W + S - 1 - up2
    n[..., :S] = np.clip(np.choose(rng.integers(0, 6, up.shape), [y, y - 1, y2, y2 - 1, 0 * y, 0 * y + W + S - 1]), 0, W + S - 1)
    return pack(X, a, D, C, n)
def setup_inputs_crowd(rng):
    X, a, D, C, n = parts(rng)
    for q in range(N):
        for g in range(8):
            k = (g + q) % 8; xg, ag, dg, cg = X[q, g], a[q, g], D[q, g], C[q, g]
            if k == 0: xg[:] = 0
            elif k == 1:
                xg[:] = 0; xg[:, int(rng.choice(np.array([0, 1, W - 2, W - 1])))] = 255
            elif k == 2 or k == 3:
                e = q & 1
                xg[:] = 128 + (xg >> 1); xg[:, e] = 0; xg[:, 1 - e] = 255; cg[1 + e:] = e; dg[:, 2:] = 1 - e
                if e == 1: cg[2:W >> 1] = -1
                if k == 3:
                    cg[W - 1] = -1; dg[:15, 2:] = -1
            elif k == 4:
                ag[:] = np.repeat(ag[:, ::S], S, axis=1); n[q, g] = W + S - 1
            elif k == 5:
                b = int(rng.integers(0, S)); us = rng.permutation(np.arange(400, 3600)); tab = np.zeros(S, np.int64)
                tab[(us * us >> 5) & (S - 1)] = us; u = tab[(b - AT) & (S - 1)]
                xg[:] = (u >> 4) + (np.arange(16)[:, None] < (u & 15)).astype(np.int64)
            elif k == 6:
                cg[:] = AT - 1; dg[:] = AT - 1
            else:
                xg[:] = 60 + (xg >> 2); ag[:, :S] = ag[:, :S] >> 2; ag[:, S:2 * S] = 254; ag[:, 2 * S:3 * S] = 0
                if q & 1: xg[:, int(rng.choice(np.array([S, W - 1])))] = 255
    return pack(X, a, D, C, n)
def setup_inputs_ties(rng):
    X, a, D, C, n = parts(rng)
    X = 60 + rng.integers(0, 2, (N, 8, 1, 1)) + rng.integers(0, 4, X.shape); a = 60 + rng.integers(0, 4, a.shape)
    a[..., :S] = 120 + rng.integers(0, 8, (N, 8, 16, S))
    o = np.argsort(rng.random((N, 2, 16, S)), axis=2); k = rng.integers(4, 8, (N, 2, 1, S))
    X[:, 2:4] = 62
    lower = 62 - (o[:, 0] < k[:, 0]).astype(np.int64)
    both = 62 + (o[:, 1] < k[:, 1]).astype(np.int64) - (o[:, 1] >= 10).astype(np.int64)
    a[:, 2, :, :S] = 2 * lower + rng.integers(0, 2, lower.shape); a[:, 3, :, :S] = 2 * both + rng.integers(0, 2, both.shape)
    return pack(X, a, D, C, n)
def check_inputs(d):
    bad = []
    for k, lo, hi in (("x0", 0, 255), ("come", 0, 255), ("dl0", -1, W - 2), ("cd0", -1, W - 2), ("age", 0, W + S - 1)):
        v = np.asarray(d[k]).astype(np.float64)
        if not np.all((v >= lo) & (v <= hi)): bad.append("range of " + k)
        elif not np.all(v == np.floor(v)): bad.append("whole numbers in " + k)
    if np.any(np.asarray(d["dl0"]) >= np.arange(W - H, W)): bad.append("the witnesses in dl0 are older places")
    if np.any(np.asarray(d["cd0"]) >= np.arange(W)): bad.append("the parents in cd0 are older places")
    return bad
def judge(X, live, c, y):
    k = c.shape[-1]; i = np.maximum(c, 0).reshape(N, 8, 16 * k)
    v = np.take_along_axis(X, i[:, :, None, :], 3).reshape(N, 8, 16, 16, k)
    more = np.add.reduce((v >= y[:, :, :, None, :]).astype(np.int32), axis=2)
    return (c >= 0) & (more >= 11) & np.take_along_axis(live, i, 2).reshape(N, 8, 16, k)
def reference(x0, come, dl0, cd0, age):
    X = np.zeros((N, 8, 16, P), np.int64); X[..., :W] = x0.astype(np.float32).astype(np.int64).reshape(N, 8, 16, W)
    D = np.full((N, 8, 16, P), -1, np.int64); D[..., W - H:W] = dl0.reshape(N, 8, 16, H)
    C = np.full((N, 8, P), -1, np.int64); C[..., :W] = cd0
    a = come.astype(np.float32).astype(np.int64).reshape(N, 8, 16, R, S); n = age.astype(np.int64).reshape(N, 8, R - 1, S)
    live = np.zeros((N, 8, P), bool); live[..., :W] = True
    z = np.zeros((N, 8, 16, S), np.int64); A = np.zeros((N, 8), np.int64)
    for t in range(R):
        lo = S * t; B = W + S * t
        live[..., :lo] = False
        x = (a[:, :, :, t] + z) >> 1; X[..., B:B + S] = x
        old = X[..., lo:B]; u = np.add.reduce(old, axis=2)
        who = ((u * u >> 5) + np.arange(lo, B)) & (S - 1)
        over = np.add.reduce((np.take_along_axis(x, who[:, :, None, :], 3) >= old).astype(np.int32), axis=2)
        die = live[..., lo:B] & (over >= 11); live[..., lo:B] = live[..., lo:B] & ~die
        c = hashed(np.add.reduce(x, axis=2), lo, A)
        c = np.where(judge(X, live, c, x), c, -1)
        D[..., B:B + S] = c; C[..., B:B + S] = np.max(c, axis=2); live[..., B:B + S] = True
        A = np.add.reduce(die.astype(np.int64), axis=2)
        cd = C[..., lo:B]
        orphan = live[..., lo:B] & (cd >= 0) & ~np.take_along_axis(live, np.maximum(cd, 0), 2)
        turn = np.roll(orphan, -ST * (t + 1), axis=2)
        turn = turn & (np.add.accumulate(turn.astype(np.int64), axis=2) <= CAP)
        taken = np.roll(turn, ST * (t + 1), axis=2)
        o = np.argsort(~taken, axis=2, kind="stable")[..., :CAP]; use = np.take_along_axis(taken, o, 2); o = o + lo
        y = np.take_along_axis(X, o[:, :, None, :], 3); d = np.take_along_axis(D, o[:, :, None, :], 3)
        left = np.where(judge(X, live, d, y), d, -1); b = np.max(left, axis=2)
        xb = np.take_along_axis(X, np.maximum(b, 0)[:, :, None, :], 3)
        y = np.where((use & (b >= 0))[:, :, None, :], (y + xb) >> 1, y)
        b = np.where(use, b, np.take_along_axis(C, o, 2)); d = np.where(use[:, :, None, :], left, d)
        np.put_along_axis(X, o[:, :, None, :], y, 3); np.put_along_axis(D, o[:, :, None, :], d, 3); np.put_along_axis(C, o, b, 2)
        if t < R - 1:
            w = np.zeros((N, 8, S), np.int64) + np.arange(B, B + S)
            for h in range(HOP):
                up = np.take_along_axis(C, w, 2)
                w = np.where((up >= 0) & (B + S - 1 - up <= n[:, :, t]), up, w)
            out = np.take_along_axis(X, w[:, :, None, :], 3).reshape(N, 8, 16, N, E)
            z = np.ascontiguousarray(out.transpose(3, 1, 2, 0, 4)).reshape(N, 8, 16, S)
    lo = S * (R - 1)
    return {"yx": np.ascontiguousarray(X[..., lo:]).reshape(N, 128, W + S).astype(np.float32).astype(BF), "yc": C[..., lo:].astype(np.float32), "ya": live[..., lo:].astype(np.float32)}

@@ -1,0 +1,726 @@
+from concourse.bass import DstId, RemoteDMATransfer
+from concourse.mybir import AluOpType as Op, ActivationFunctionType as Fn
+
+W, S, R, ST, N = 2048, 256, 4, 341, 4
+O = 528
+PW = O + W + R * S
+BF, F32, F16, I32, U16 = "bfloat16", "float32", "float16", "int32", "uint16"
+MAGIC = 12582912.0
+K3 = 65536.0
+CFG = {"ns4": 9, "ns5": 6, "dv": 52, "ov": 50, "cyc": 1.04, "pe": 0.55, "get": 1.56, "put": 3.8,
+       "wake": 70.0, "far": 3500.0, "turns": 5, "pin": 0, "pin2": 1}
+
+SCRATCH = {}
+
+
+def _sb(name, cols, dtype):
+    SCRATCH[name] = ("sbuf", [128] + (cols if isinstance(cols, list) else [cols]), dtype)
+
+
+for _n, _c, _d in [
+    ("X", PW, BF), ("XA", PW, BF), ("C", PW, F32), ("D", PW, I32), ("CM", R * S, BF),
+    ("cdi", 128, I32), ("cdf", 128, F32), ("cdh", 128, F16), ("agi", 48, I32),
+    ("cdn", 128, F32), ("cdm", 128, F32),
+    ("jrow", 256, F32), ("pi", 1, I32), ("pt", 4, I32), ("pc", 16, F32), ("jg", 128, F32), ("jm", 256, F32),
+    ("WS1", 144, BF), ("WSv", 144, BF), ("WSs", 144, BF), ("WSz", 144, BF), ("Wh", 144, F16), ("Ch", W, F16), ("CO", PW, F32),
+    ("BD", 128, BF), ("BD2", 128, BF), ("BDv", 128, BF), ("BDs", 128, BF), ("TL", 128, BF), ("TU", 128, BF), ("sv", 16, F32), ("Ub", 64, BF), ("lf", 130, F32),
+    ("Ip", 128, BF), ("In", 128, BF), ("Ih", 128, BF),
+    ("M0", 4 * 160, F16), ("M1", 4 * 160, F16), ("UWi", 2048, BF), ("UW", 2048, F16),
+    ("cV", 512, BF), ("cS", 512, BF), ("cH", 256, BF), ("cJ4", 256, BF), ("cJ5", 256, BF),
+    ("one", 256, F32), ("cap", 130, BF), ("segn", 256, F16), ("seg8", 128, F32), ("aw", 256, F32), ("mk", 256, F32),
+    ("p32", 128, F32), ("Kc", 256, F32), ("s16", [16, 16], BF), ("s1", 256, BF), ("sw", 16, F32),
+    ("L16", 16, U16), ("sq", 128, F32), ("wi", 128, I32), ("wj", 128, I32), ("who", 128, U16), ("lc", 130, U16),
+    ("Ed", W, BF), ("Gd", 1536, BF), ("Og", 2064, BF), ("E4", 4096, BF), ("E5", 4096, BF), ("junk", W, BF),
+    ("ua", 16, F32), ("uq", 16, F32), ("hi", 16, I32), ("hj", 16, I32), ("hA", 16, F32),
+    ("T1", 256, F32), ("T2", 256, I32), ("c4", 256, I32), ("o4", 256, U16), ("c5", 256, F32), ("o5", 256, U16),
+    ("F", 130, BF), ("Sb", 130, BF), ("cum", 130, F32), ("IB", [128, 16], BF), ("bs", 128, F32), ("lb", 16, U16),
+    ("E3", 256, BF), ("U", 144, F32), ("kp", 4, F32), ("ou", 16, F32), ("lo1", 16, U16), ("lo2", 16, U16), ("lx", 16, U16),
+    ("y", 256, BF), ("dg", 256, F16), ("ta", 256, F16), ("tb", 256, F16), ("tc", 256, F16),
+    ("v4", 256, F16), ("v5", 256, F16), ("tr", 256, F16), ("tq", 256, F16), ("m4", 16, F32), ("m5", 16, F32), ("mc", 32, F16),
+    ("cn", 256, F32), ("xb", 256, BF), ("av", 256, BF), ("dn", 256, F32),
+    ("thw", 48, F32), ("th", 192, F32), ("cc", 192, F32), ("fl", 64, F32), ("wq", 64, F32),
+    ("lh", 32, U16), ("hg", 512, F16), ("sc", 512, F16), ("lw", 16, U16),
+    ("zs", 3 * S, BF), ("Z", 3 * S, BF), ("ac", 16, F32),
+]:
+    _sb(_n, _c, _d)
+for _k in range(8):
+    SCRATCH["p%d" % _k] = ("psum", [128, 512], F32)
+
+DMA_SEMS = ["dx", "dc0", "dcm", "dcd", "dag", "ddl", "drep", "dya", "dyo", "dyx", "dyy", "dyc"]
+SEMAPHORES = ["eV", "eS", "eP", "eG"] + DMA_SEMS + ["arr0", "arr1", "arr2", "snt0", "snt1", "snt2"]
+
+
+def build(T, rank, topo, core):
+    ops = []
+    cyc = CFG["cyc"]
+
+    def view(a, name, lo, hi, n, tag=None):
+        where, _, dtype = SCRATCH[name]
+        return {"ap": a, "regs": [(name, lo, hi) if tag is None else (name, lo, hi, tag)], "rd": [], "n": n,
+                "two": dtype in (BF, F16, U16), "ps": where == "psum", "ind": False}
+
+    def A(n, a, b, st=1):
+        if st == 1:
+            return view(T[n][:, a:b], n, a, b, b - a)
+        return view(T[n][:, a:b:st], n, a, b, (b - a + st - 1) // st)
+
+    def lane(n, a, b, st):
+        return view(T[n][:, a:b:st], n, a - a % st, b, (b - a + st - 1) // st, a % st)
+
+    def ext(a):
+        return {"ap": a, "regs": [], "rd": [], "n": 0, "two": False, "ps": False, "ind": False}
+
+    def IND(w, o):
+        return dict(w, ap=w["ap"].indirect(o["ap"]), regs=w["regs"] + o["regs"], n=16 * o["n"], ind=True)
+
+    def SCT(w, o):
+        return dict(w, ap=w["ap"].indirect(o["ap"]), rd=o["regs"], n=16 * o["n"], ind=True)
+
+    def ap(x):
+        return x["ap"] if isinstance(x, dict) else x
+
+    def emit(e, f, out, ins, cost, lat=0.0, sem=None, arr=None):
+        rd = list(out["rd"])
+        for x in ins:
+            if isinstance(x, dict):
+                rd += x["regs"]
+        ops.append({"e": e, "f": f, "w": out["regs"], "r": rd, "sem": sem, "arr": arr, "c": cost, "lat": lat})
+
+    def vcost(out, full, both=False):
+        if out["ind"]:
+            return 50 + out["n"] * CFG["put"] * cyc
+        if full and full[0]["ind"]:
+            return 50 + out["n"] * CFG["get"] * cyc
+        k = 0.5 if out["two"] and all(x["two"] for x in full) else 1.0
+        if both and not any(x["ps"] for x in full):
+            k *= 2
+        return 40 + max(64, out["n"] * k) * cyc
+
+    def ts(out, a, s1, op0, s2=None, op1=None):
+        if op1 is None:
+            emit("V", lambda q: q.tensor_scalar(ap(out), ap(a), ap(s1), None, op0), out, [a, s1], vcost(out, [a]))
+        else:
+            emit("V", lambda q: q.tensor_scalar(ap(out), ap(a), ap(s1), ap(s2), op0, op1), out, [a, s1, s2], vcost(out, [a]))
+
+    def tt(out, a, b, op):
+        emit("V", lambda q: q.tensor_tensor(ap(out), ap(a), ap(b), op), out, [a, b], vcost(out, [a, b], True))
+
+    def cp(out, a):
+        emit("V", lambda q: q.tensor_copy(ap(out), ap(a)), out, [a], vcost(out, [a]))
+
+    def fill(out, v):
+        emit("V", lambda q: q.memset(ap(out), v), out, [], vcost(out, []))
+
+    def scan(out, d0, d1, op0, op1):
+        emit("V", lambda q: q.tensor_tensor_scan(ap(out), ap(d0), ap(d1), 0.0, op0, op1), out, [d0, d1], vcost(out, [d0, d1]))
+
+    def act(out, a, fn, bias=None, scale=None, acc=None):
+        kw = {}
+        if bias is not None:
+            kw["bias"] = ap(bias)
+        if scale is not None:
+            kw["scale"] = ap(scale)
+        o = out
+        if acc is not None:
+            kw["accum_out"] = ap(acc)
+            o = dict(out, regs=out["regs"] + acc["regs"])
+        cost = 65 + out["n"] * CFG["get"] * cyc if a["ind"] else 60 + max(64, out["n"]) * cyc
+        emit("S", lambda q: q.activation(ap(out), ap(a), fn, **kw), o, [a, bias, scale], cost)
+
+    def mm(out, l, r, start, stop, arr=None):
+        emit("P", lambda q: q.matmul(ap(out), ap(l), ap(r), start, stop), out, [l, r],
+             max(64, r["n"]) * CFG["pe"] * (1 if r["two"] else 4), 60.0, arr=arr)
+
+    def iota(out, pat, base, cm, flag=True):
+        cost = 130 + 2 * out["n"] * cyc
+        if flag:
+            emit("G", lambda q: q.iota(ap(out), pat, base, cm, allow_small_or_imprecise_dtypes=True), out, [], cost)
+        else:
+            emit("G", lambda q: q.iota(ap(out), pat, base, cm), out, [], cost)
+
+    def gfill(out, v):
+        iota(out, [[0, out["n"]]], v, 0)
+
+    def select(out, a, pat, op, base, cm, other=0.0):
+        emit("G", lambda q: q.affine_select(ap(out), ap(a), pat, op, other, base, cm), out, [a], 170 + 2 * out["n"] * cyc)
+
+    def dma(e, out, a, sem, kib):
+        emit(e, lambda q: q.dma_start(ap(out), ap(a)), out, [a], 60.0, 2000.0 + 5.6 * kib, sem=sem)
+
+    def chain(name):
+        ops[-1]["chain"] = name
+
+    def ws(n, r):
+        return A(n, 15 - r, 143 - r)
+
+    def wrap(out, n, rhs, start=True, stop=True):
+        for r in range(16):
+            mm(out, ws(n, r), rhs(r), start and r == 0, stop and r == 15)
+
+    def mshift(n, a, d):
+        return A(n, 160 * a + 16 - d, 160 * a + 144 - d)
+
+    def turn(bank, src, n, m, d):
+        k = n // 4
+        for a in range(4):
+            bk, at = bank(a) if not isinstance(bank, str) else (bank, k * a)
+            for b in range(4):
+                mm(A(bk, at, at + k), mshift(m, a, d * (b - a)), A(src, b, n, 4), b == 0, b == 3)
+
+    def back(bank, src, m, d):
+        for b in range(4):
+            for a in range(4):
+                mm(A(bank, b, 256, 4), mshift(m, b, d * (a - b)), A(src, 64 * a, 64 * a + 64), a == 0, a == 3)
+
+    def col(n, j):
+        return A(n, j, j + 1)
+
+    ns4, ns5, dv, ov = CFG["ns4"], CFG["ns5"], CFG["dv"], CFG["ov"]
+    nv4, nv5 = 16 - ns4, 14 - ns5
+    s16 = view(T.s16[:], "s16", 0, 256, 256)
+    dma("Y", A("X", O, O + W), ext(T.x0[:]), "dx", 512)
+    dma("S", A("CM", 0, S), ext(T.come[:, 0:S]), "dc0", 64)
+    dma("S", A("cdi", 0, 128), ext(T.cd0[:]), "dcd", 64)
+    dma("S", A("agi", 0, 48), ext(T.age[:]), "dag", 24)
+    dma("Y", A("D", O, O + W), ext(T.dl0[:]), "ddl", 1536)
+    dma("Y", A("CM", S, R * S), ext(T.come[:, S:R * S]), "dcm", 1728)
+    iota(A("pi", 0, 1), [[0, 1]], 0, 1, False)
+    iota(A("jrow", 0, 256), [[1, 256]], 0, 0)
+    iota(A("jg", 0, 128), [[16, 8], [0, 16]], 0, 0)
+    iota(A("Kc", 0, 256), [[61, 16], [0, 16]], 7, 0)
+    iota(s16, [[256, 16], [16, 16]], 0, 0)
+    iota(A("s1", 0, 256), [[1, 256]], 0, 0)
+    iota(A("jm", 0, 256), [[0, 16], [1, 16]], 0, 0)
+    gfill(A("UWi", 0, 2048), 1)
+    fill(A("cH", 0, 256), -0.5)
+    for h in (0, 256):
+        act(A("cV", h, h + 256), A("jrow", 0, 256), Fn.Identity, bias=10.5 * K3, scale=0.0)
+        act(A("cS", h, h + 256), A("jrow", 0, 256), Fn.Identity, bias=2.5 * K3, scale=0.0)
+    gfill(A("XA", 0, O - 1), 0)
+    gfill(A("XA", O - 1, O), -512)
+    gfill(A("X", 0, O), 0)
+    gfill(A("ac", 0, 16), 0)
+    gfill(A("C", 0, O), -1025)
+    iota(A("D", 0, O), [[0, O]], -1, 0, False)
+    gfill(A("one", 0, 256), 1)
+    gfill(A("cap", 0, 130), 256)
+    gfill(A("F", 0, 1), 0)
+    gfill(A("cJ4", 0, 16 * nv4), -43008)
+    gfill(A("cJ4", 16 * nv4, 256), -10240)
+    gfill(A("cJ5", 0, 16 * nv5), -43008)
+    gfill(A("cJ5", 16 * nv5, 224), -10240)
+    gfill(A("cJ5", 224, 256), -43008)
+    gfill(lane("th", 0, 192, 4), -1)
+    ts(col("pt", 0), col("pi", 0), 15, Op.bitwise_and)
+    ts(col("pt", 1), col("pi", 0), 112, Op.bitwise_and)
+    ts(col("pt", 2), col("pi", 0), 3, Op.bitwise_and)
+    ts(col("pt", 3), col("pi", 0), 12, Op.bitwise_and)
+    cp(col("pc", 0), col("pi", 0))
+    ts(col("pc", 4), col("pi", 0), 16.0, Op.add)
+    cp(A("pc", 1, 3), A("pt", 0, 2))
+    ts(col("pc", 3), col("pt", 1), 15.0, Op.add)
+    cp(A("pc", 5, 7), A("pt", 2, 4))
+    ts(col("pc", 7), col("pt", 0), 32.0, Op.mult)
+    ts(A("WS1", 0, 144), A("jrow", 0, 144), col("pc", 3), Op.is_equal)
+    ts(A("Ip", 0, 128), A("jrow", 0, 128), col("pc", 0), Op.is_equal)
+    ts(A("BD", 0, 128), A("jg", 0, 128), col("pc", 2), Op.is_equal)
+    act(A("p32", 0, 128), A("jrow", 0, 128), Fn.Identity, bias=col("pc", 7), scale=512.0)
+    act(A("sw", 0, 16), A("jrow", 0, 16), Fn.Identity, bias=col("pc", 1), scale=16.0)
+    for n, src, k, v in (("Ih", "Ip", 128, 0.5), ("In", "Ip", 128, -1.0), ("BDv", "BD", 128, -K3), ("BDs", "BD", 128, -K3 / 2),
+                         ("BD2", "BD", 128, 2.0), ("WSz", "WS1", 144, -512.0), ("WSv", "WS1", 144, 4096.0),
+                         ("WSs", "WS1", 144, 2048.0)):
+        act(A(n, 0, k), A(src, 0, k), Fn.Identity, scale=v)
+    ts(A("L16", 0, 16), A("jrow", 0, 16), 0.0, Op.mult, col("pc", 1), Op.add)
+    ts(A("pc", 8, 12), A("jrow", 0, 4), col("pc", 5), Op.is_equal)
+    ts(A("pc", 12, 16), A("jrow", 0, 16, 4), col("pc", 6), Op.is_equal)
+    for a in range(4):
+        ts(A("M0", 160 * a, 160 * a + 160), A("jrow", 0, 160), col("pc", 4), Op.is_equal, col("pc", 8 + a), Op.mult)
+        ts(A("M1", 160 * a, 160 * a + 160), A("jrow", 0, 160), col("pc", 4), Op.is_equal, col("pc", 12 + a), Op.mult)
+    select(A("TL", 0, 128), A("BD", 0, 128), [[1, 128]], Op.is_ge, 0, -1)
+    select(A("TU", 0, 128), A("BD", 0, 128), [[-1, 128]], Op.is_gt, 0, 1)
+    select(A("seg8", 0, 128), A("one", 0, 128), [[0, 16], [1, 8]], Op.is_gt, 0, 0)
+    act(A("sv", 0, 16), A("sw", 0, 16), Fn.Identity, bias=256.0)
+    select(A("segn", 0, 256), A("X", 0, 256), [[0, 16], [1, 16]], Op.not_equal, 0, 0, -60000.0)
+    ts(A("mk", 0, 256), A("jm", 0, 256), col("pc", 1), Op.not_equal, -48976.0, Op.mult)
+    ts(A("Wh", 0, 144), A("WS1", 0, 144), 0.0625, Op.mult)
+    gfill(A("CO", 0, O + S * (R - 1)), 0)
+    select(A("UW", 0, 2048), A("UWi", 0, 2048), [[1, 16], [16, 8], [0, 16]], Op.is_equal, 0, -1)
+    for t in range(R - 1):
+        act(lane("cc", 64 * t, 64 * t + 64, 4), A("sw", 0, 16), Fn.Identity, bias=float(W + S * t))
+    cp(A("cdh", 0, 128), A("cdi", 0, 128))
+    ts(A("cdf", 0, 128), A("cdi", 0, 128), -1024.0, Op.add)
+    for r in range(16):
+        dma("Y", view(T.C[r:128:16, O:O + W], "C", O, O + W, W, r), A("cdf", 0, 128), "drep", 64)
+    turn("p6", "cdh", 128, "M0", 1)
+    cp(A("ta", 0, 128), A("p6", 0, 128))
+    turn("p6", "ta", 128, "M1", 4)
+    ts(A("cdm", 0, 128), A("p6", 0, 128), 0.0, Op.is_lt)
+    tt(A("cdn", 0, 128), A("p6", 0, 128), A("cdm", 0, 128), Op.subtract)
+
+    def ages():
+        ts(A("tc", 0, 48), A("agi", 0, 48), -1024.0, Op.add)
+        turn("p0", "tc", 48, "M0", 1)
+        cp(A("tb", 0, 48), A("p0", 0, 48))
+        turn("p0", "tb", 48, "M1", 4)
+        for t in range(R - 1):
+            act(A("thw", 16 * t, 16 * t + 16), A("p0", 16 * t, 16 * t + 16), Fn.Identity,
+                bias=float(W + S * t + S - 1 - 1024), scale=-1.0)
+        for k in range(1, 4):
+            act(lane("th", k, 192, 4), A("thw", 0, 48), Fn.Identity)
+
+    def who(t):
+        lo = S * t
+        wrap(A("p7", 0, 128), "WS1", lambda r: A("X", O + lo + r, O + lo + W, 16))
+        act(A("sq", 0, 128), A("p7", 0, 128), Fn.Square)
+        tt(A("wi", 0, 128), A("sq", 0, 128), A("p32", 0, 128), Op.add)
+        ts(A("wj", 0, 128), A("wi", 0, 128), 5, Op.arith_shift_right, S - 1, Op.bitwise_and)
+        cp(A("who", 0, 128), A("wj", 0, 128))
+
+    def parent_list(t, src):
+        c0, r0 = divmod(ST * (t + 1), 16)
+        free = float(O - 2 if t == 0 else O - 1)
+        act(col("kp", 0), col("pc", 1), Fn.Sign, bias=0.5 - r0)
+        act(col("kp", 1), col("kp", 0), Fn.Relu)
+        act(col("kp", 2), col("kp", 0), Fn.Relu, scale=-1.0)
+        up = float(O if t == 0 else O + 1024)
+        act(A("lf", 1, 128 - c0), A(src, c0 + 1, 128), Fn.Identity, bias=up)
+        act(A("lf", 128 - c0, 128), A(src, 0, c0), Fn.Identity, bias=up)
+        act(col("kp", 3), col(src, c0), Fn.Identity, bias=up - free)
+        act(col("lf", 0), col("kp", 3), Fn.Identity, bias=free, scale=col("kp", 1))
+        act(col("lf", 128), col("kp", 3), Fn.Identity, bias=free, scale=col("kp", 2))
+        cp(A("lc", 0, 129), A("lf", 0, 129))
+
+    pieces = [("V", 0, 32, "p0"), ("S", dv, 32, "p4"), ("V", 32, dv - 32, "p1"), ("S", dv + 32, 32, "p5"),
+              ("S", dv + 64, 64 - dv, "p6")]
+
+    def pre_terms(t):
+        lo = S * t
+        mm(A("p3", 0, 256), A("Ih", 0, 128), A("CM", lo, lo + S), True, False)
+        mm(A("p3", 0, 256), A("Ih", 0, 128), A("cH", 0, 256), False, t == 0)
+
+    def judge_parts(E, off, yy, win, cj):
+        flip = [0]
+
+        def vrow(k):
+            tt(A(E, 256 * k, 256 * k + 256), IND(win, A(off, 16 * k, 16 * k + 16)), yy, Op.is_ge)
+            chain("V")
+
+        def srows(k0, k1):
+            todo = None
+            for k in list(range(k0, k1, 2)) + [None]:
+                if k is not None:
+                    n = min(2, k1 - k)
+                    h, pb = 512 * flip[0], ("p2", "p3", "p0")[flip[0]]
+                    flip[0] = (flip[0] + 1) % 3
+                    act(A("Gd", h, h + 256 * n), IND(win, A(off, 16 * k, 16 * (k + n))), Fn.Identity)
+                    chain("S")
+                    mm(A(pb, 0, 256 * n), A("Ip", 0, 128), A("Gd", h, h + 256 * n), True, False)
+                    for i in range(n):
+                        mm(A(pb, 256 * i, 256 * i + 256), A("In", 0, 128), yy, False, i == n - 1)
+                if todo is not None:
+                    act(A(E, 256 * todo[0], 256 * (todo[0] + todo[1])), A(todo[2], 0, 256 * todo[1]), Fn.Sign, bias=0.5)
+                    chain("S")
+                todo = None if k is None else (k, n, pb)
+
+        def const(bank, k0, k1):
+            mm(A(bank, 16 * k0, 16 * k1), A("Ip", 0, 128), A(cj, 16 * k0, 16 * k1), True, False)
+
+        def count(bank, k0, k1, m, stop=False):
+            wrap(A(bank, 16 * k0, 16 * k1), m, lambda r: A(E, 256 * k0 + r, 256 * k1, 16), False, stop)
+
+        return vrow, srows, const, count
+
+    def spread(m, j, lo, bank, out):
+        ts(A("mc", 16 * j, 16 * j + 16), A(m, 0, 16), float(-lo - 1), Op.max)
+        for r in range(16):
+            mm(A(bank, r, 256, 16), A("UW", 128 * r, 128 * r + 128), A("mc", 16 * j, 16 * j + 16), True, True)
+        act(out, A(bank, 0, 256), Fn.Identity, bias=float(lo if lo == S * (R - 1) else lo - 1024))
+
+    def chunks(a, b):
+        cut = list(range(a, max(b - 3, a + 1), 4)) + [b]
+        return list(zip(cut, cut[1:]))
+
+    peers = [(rank + k) % N for k in range(1, N)]
+
+    parent_list(0, "cdn")
+    pre_terms(0)
+
+    def places():
+        cp(A("hi", 0, 16), A("uq", 0, 16))
+        ts(A("hj", 0, 16), A("hi", 0, 16), 5, Op.arith_shift_right, W - 1, Op.bitwise_and)
+        ts(A("hA", 0, 16), A("hj", 0, 16), col("ac", 0), Op.add)
+        tt(A("T1", 0, 256), IND(A("ua", 0, 16), A("L16", 0, 16)), A("Kc", 0, 256), Op.mult)
+        tt(A("T2", 0, 256), IND(A("hA", 0, 16), A("L16", 0, 16)), A("T1", 0, 256), Op.add)
+        ts(A("c4", 0, 256), A("T2", 0, 256), W - 1, Op.bitwise_and)
+        ts(A("o4", 0, 256), A("c4", 0, 256), 16.0, Op.add)
+
+    for t in range(R):
+        lo, B = S * t, W + S * t
+        last = t == R - 1
+        c0, r0 = divmod(ST * (t + 1), 16)
+        xa = A("X", O + B, O + B + S)
+        if t > 0:
+            z0 = S * (t - 1)
+            for i, b in enumerate([rank] + peers):
+                src = A("zs" if b == rank else "Z", z0 + 64 * b, z0 + 64 * b + 64)
+                mm(A("p3", 64 * b, 64 * b + 64), A("Ih", 0, 128), src, False, i == N - 1, arr=t - 1 if i == 1 else None)
+        ts(xa, A("p3", 0, 256), MAGIC, Op.add, MAGIC, Op.subtract)
+        wrap(A("p7", 0, 16), "WS1", lambda r: A("X", O + B + r, O + B + S, 16))
+        act(A("ua", 0, 16), A("p7", 0, 16), Fn.Identity)
+        act(A("uq", 0, 16), A("p7", 0, 16), Fn.Square)
+        if t == 0:
+            places()
+            who(0)
+            ops[-1]["r"] += [("o4", 0, 256)]
+        for i, (e, k, n, bank) in enumerate(pieces):
+            a, m = O + lo + 16 * k, 16 * n
+            ed, got = A("Ed", 16 * k, 16 * k + m), IND(xa, A("who", k, k + n))
+            mm(A(bank, 0, m), A("Ip", 0, 128), A("cV" if e == "V" else "cS", 0, m), True, False)
+            known = min(m, O + B - S - a)
+            if t > 0 and known > 0:
+                mm(A(bank, 0, known), A("BD2", 0, 128), A("XA", a, a + known), False, False)
+            if e == "V":
+                tt(ed, got, A("X", a, a + m), Op.is_ge)
+            else:
+                h, pb = (512, "p3") if i == 3 else (0, "p2")
+                act(A("Gd", h, h + m), got, Fn.Identity)
+                mm(A(pb, 0, m), A("In", 0, 128), A("X", a, a + m), True, False)
+                mm(A(pb, 0, m), A("Ip", 0, 128), A("Gd", h, h + m), False, True)
+                act(ed, A(pb, 0, m), Fn.Sign, bias=0.5)
+            mm(A(bank, 0, m), A("BDv" if e == "V" else "BDs", 0, 128), ed, False, True)
+            tt(A("XA", a, a + m), A(bank, 0, m), A("X", a, a + m), Op.min)
+        if t > 0:
+            places()
+        ov = CFG["ov"] if t > 0 else 62
+        wall = A("XA", 0, O + B)
+        win = A("XA", lo + O - 16, O + B)
+        ts(A("Og", 0, 16 * ov), IND(wall, A("lc", 0, ov)), 0.0, Op.min, -1.0, Op.max)
+        if CFG["pin2"]:
+            ops[-1]["r"] += [("T1", 0, 256), ("hA", 0, 16)]
+        act(A("Og", 16 * ov, 1024), IND(wall, A("lc", ov, 64)), Fn.Sign, bias=0.5)
+        act(A("Og", 1024, 2064), IND(wall, A("lc", 64, 129)), Fn.Sign, bias=0.5)
+        mm(A("p6", 0, 129), A("Ip", 0, 128), A("cH", 0, 129), True, False)
+        wrap(A("p6", 0, 128 - c0), "WS1", lambda r: A("XA", O + lo + 16 * c0 + r, O + B, 16), False, False)
+        wrap(A("p6", 128 - c0, 129), "WS1", lambda r: A("XA", O + lo + r, O + lo + 16 * c0 + 16, 16), False, False)
+        wrap(A("p6", 0, 64), "WSz", lambda r: A("Og", r, 1024, 16), False, False)
+        wrap(A("p6", 64, 129), "WSz", lambda r: A("Og", 1024 + r, 2064, 16), False, True)
+        ts(A("F", 1, 130), A("p6", 0, 129), 6000.0, Op.is_ge)
+        mm(A("p6", 0, 129), A("BD", 0, 128), A("F", 1, 130), True, True)
+        mm(A("p7", 0, 129), A("TL", 0, 128), A("F", 1, 130), True, False)
+        mm(A("p7", 0, 129), A("TU", 0, 128), A("F", 0, 129), False, True)
+        scan(A("Sb", 0, 129), A("p6", 0, 129), A("cap", 0, 129), Op.add, Op.min)
+        wrap(A("p6", 0, 8), "WS1", lambda r: A("Sb", r, 128, 16))
+        scan(A("cum", 0, 129), A("one", 0, 129), A("p7", 0, 129), Op.mult, Op.add)
+        base = float(O + lo + 16 * c0)
+        ts(A("Ub", 0, 16), A("sw", 0, 16), col("Sb", 128), Op.is_ge, -(base + 16.0), Op.mult)
+        ts(A("Ub", 16, 32), A("sw", 0, 16), col("Sb", 127 - c0), Op.is_ge, -2048.0, Op.mult)
+        act(col("U", 0), col("Sb", 128), Fn.Identity, scale=-1.0)
+        act(A("Ub", 32, 48), A("sw", 0, 16), Fn.Relu, bias=col("U", 0))
+        for b in range(8):
+            ts(view(T.IB[:, b:128:8, :], "IB", 0, 2048, 256, b), s16, col("p6", b), Op.is_ge)
+        wrap(A("p7", 0, 128), "WS1", lambda r: view(T.IB[:, :, r], "IB", 0, 2048, 128))
+        scan(A("bs", 0, 128), A("seg8", 0, 128), A("p7", 0, 128), Op.mult, Op.add)
+        cp(A("lb", 0, 16), A("bs", 7, 128, 8))
+        tt(A("E3", 0, 256), IND(A("cum", 0, 129), A("lb", 0, 16)), A("s1", 0, 256), Op.is_le)
+        act(A("Ub", 48, 64), A("bs", 7, 128, 8), Fn.Identity, scale=16.0)
+        for i in range(4):
+            mm(A("p6", 0, 16), A("Ip", 0, 128), A("Ub", 16 * i, 16 * i + 16), i == 0, False)
+        wrap(A("p6", 0, 16), "WS1", lambda r: A("E3", r, 256, 16), False, True)
+        ts(A("lo1", 0, 16), A("p6", 0, 16), base, Op.add)
+        act(A("ou", 0, 16), A("p6", 0, 16), Fn.Identity, bias=base)
+        ts(A("dg", 0, 256), IND(A("D", 0, O + B), A("lo1", 0, 16)), float(-lo), Op.add, -1.0, Op.max)
+        act(A("y", 0, 256), IND(A("X", 0, O + B), A("lo1", 0, 16)), Fn.Identity)
+        turn("p7", "dg", 256, "M0", 1)
+        cp(A("ta", 0, 256), A("p7", 0, 256))
+        turn(lambda a: ("p6" if a < 2 else "p7", 64 * a), "ta", 256, "M1", 4)
+        ts(A("o5", 0, 128), A("p6", 0, 128), 16.0, Op.add)
+        ts(A("o5", 128, 256), A("p7", 128, 256), 16.0, Op.add)
+        act(A("c5", 0, 128), A("p6", 0, 128), Fn.Identity)
+        act(A("c5", 128, 256), A("p7", 128, 256), Fn.Identity)
+        vrow, srows, const, count = judge_parts("E4", "o4", xa, win, "cJ4")
+        const("p4", 0, 16)
+        for k in range(nv4):
+            vrow(k)
+        srows(nv4, 16)
+        for k0, k1 in chunks(nv4, 16):
+            count("p4", k0, k1, "WSs")
+        for k0, k1 in chunks(0, nv4):
+            count("p4", k0, k1, "WSv", k1 == nv4)
+        tt(A("v4", 0, 256), A("p4", 0, 256), A("c4", 0, 256), Op.min)
+        tt(A("tr", 0, 128), A("v4", 0, 128), A("v4", 128, 256), Op.max)
+        tt(A("tr", 128, 192), A("tr", 0, 64), A("tr", 64, 128), Op.max)
+        tt(A("tr", 192, 224), A("tr", 128, 160), A("tr", 160, 192), Op.max)
+        tt(A("m4", 0, 16), A("tr", 192, 208), A("tr", 208, 224), Op.max)
+        spread("m4", 0, lo, "p4", A("CO" if last else "C", O + B, O + B + S))
+        if t == 0:
+            ages()
+        if not last:
+            ts(A("lh", 0, 16), A("mc", 0, 16), float(lo + O), Op.add)
+            act(lane("cc", 64 * t + 1, 64 * t + 64, 4), A("m4", 0, 16), Fn.Identity, bias=float(lo))
+        yy = A("y", 0, 256)
+        vrow, srows, const, count = judge_parts("E5", "o5", yy, win, "cJ5")
+        const("p5", 0, 14)
+        const("p1", 14, 16)
+        for k in range(nv5):
+            vrow(k)
+        srows(nv5, 14)
+        cs = sorted(chunks(0, nv5) + chunks(nv5, 14), key=lambda x: (x[1] - nv5) / ns5 if x[0] >= nv5 else x[1] / (nv5 + 2))
+        for k0, k1 in cs:
+            count("p5", k0, k1, "WSv" if k0 < nv5 else "WSs", (k0, k1) == cs[-1])
+        vrow(14)
+        if CFG["pin"]:
+            ops[-1]["r"] += [("mc", 0, 16)]
+        vrow(15)
+        count("p1", 14, 16, "WSv", True)
+        tt(A("v5", 0, 224), A("p5", 0, 224), A("c5", 0, 224), Op.min)
+        tt(A("tq", 0, 112), A("v5", 0, 112), A("v5", 112, 224), Op.max)
+        tt(A("tq", 112, 176), A("tq", 0, 64), A("tq", 48, 112), Op.max)
+        tt(A("tq", 176, 208), A("tq", 112, 144), A("tq", 144, 176), Op.max)
+        tt(A("tq", 208, 224), A("tq", 176, 192), A("tq", 192, 208), Op.max)
+        tt(A("v5", 224, 256), A("p1", 224, 256), A("c5", 224, 256), Op.min)
+        tt(A("tq", 224, 240), A("v5", 224, 240), A("v5", 240, 256), Op.max)
+        tt(A("m5", 0, 16), A("tq", 208, 224), A("tq", 224, 240), Op.max)
+        ts(A("lx", 0, 16), A("m5", 0, 16), 16.0, Op.add)
+        spread("m5", 1, lo, "p6", A("cn", 0, 256))
+        mm(A("p7", 0, 256), A("Ih", 0, 128), yy, True, False)
+        mm(A("p7", 0, 256), A("Ih", 0, 128), A("cH", 0, 256), False, False)
+        act(A("xb", 0, 256), IND(win, A("lx", 0, 16)), Fn.Identity)
+        mm(A("p7", 0, 256), A("Ih", 0, 128), A("xb", 0, 256), False, True)
+        act(A("U", 16, 32), A("m5", 0, 16), Fn.Relu, scale=-2.0)
+        tt(A("U", 32, 48), A("ou", 0, 16), A("U", 16, 32), Op.subtract)
+        tt(A("U", 48, 64), A("U", 32, 48), A("sv", 0, 16), Op.max)
+        cp(A("lo2", 0, 16), A("U", 48, 64))
+        if last:
+            ts(A("av", 0, 256), A("p7", 0, 256), MAGIC, Op.add, MAGIC, Op.subtract)
+        else:
+            act(A("aw", 0, 256), A("p7", 0, 256), Fn.Identity, bias=MAGIC)
+            act(A("av", 0, 256), A("aw", 0, 256), Fn.Identity, bias=-MAGIC)
+        if last:
+            for r in range(16):
+                mm(A("p0", 0, 128), ws("WS1", r), A("XA", O + lo + 128 * r, O + lo + 128 * r + 128), r == 0, r == 15)
+            ts(A("cdf", 0, 128), A("p0", 0, 128), 0.0, Op.is_ge)
+            dma("Y", ext(T.ya[:, 0:W]), A("cdf", 0, 128), "dya", 64)
+            dma("Y", ext(T.ya[:, W:W + S]), view(T.one[0:8, 0:256], "one", 0, 256, 256), "dyo", 8)
+            dma("Y", ext(T.yx[:, W:W + S]), xa, "dyy", 64)
+            cp(SCT(A("X", 0, O + B), A("lo2", 0, 16)), A("av", 0, 256))
+            dma("Y", ext(T.yx[:, 0:W]), A("X", O + lo, O + B), "dyx", 512)
+            cp(SCT(A("CO", 0, O + B), A("lo1", 0, 16)), A("cn", 0, 256))
+            dma("S", ext(T.yc[:]), view(T.CO[0:128:16, O + lo:PW], "CO", O + lo, PW, W + S), "dyc", 72)
+            break
+        cp(SCT(A("C", 0, O + B), A("lo1", 0, 16)), A("cn", 0, 256))
+        cp(SCT(A("X", 0, O + B), A("lo2", 0, 16)), A("av", 0, 256))
+        cw = A("C", 0, O + B + S)
+        for h in range(2):
+            hg, sc = A("hg", 256 * h, 256 * h + 256), A("sc", 256 * h, 256 * h + 256)
+            tt(hg, IND(cw, A("lh", 16 * h, 16 * h + 16)), A("mk", 0, 256), Op.add)
+            scan(sc, A("segn", 0, 256), hg, Op.add, Op.max)
+            ends = A("sc", 256 * h + 15, 256 * h + 256, 16)
+            if h == 0:
+                ts(A("lh", 16, 32), ends, float(O + 1024), Op.add)
+            ts(lane("cc", 64 * t + 2 + h, 64 * t + 64, 4), ends, 1024.0, Op.add)
+        cc = A("cc", 64 * t, 64 * t + 64)
+        tt(A("fl", 0, 64), cc, A("th", 64 * t, 64 * t + 64), Op.is_lt)
+        scan(A("wq", 0, 64), A("fl", 0, 64), cc, Op.mult, Op.max)
+        ts(A("lw", 0, 16), A("wq", 3, 64, 4), float(O), Op.add)
+        cp(A("zs", lo, lo + S), IND(A("X", 0, O + B + S), A("lw", 0, 16)))
+
+        def send(q, t=t):
+            trs = []
+            free = topo.engines(core, T.cores[peers[0]])
+            for i, b in enumerate(peers):
+                dst = T.cores[b]
+                ok = [e for e in topo.engines(core, dst) if e in free][:4 if i == 0 else 2]
+                free = [e for e in free if e not in ok]
+                rid, pid, _ = topo.addr(dst)
+                trs.append(RemoteDMATransfer(
+                    dst_ids=[DstId(rid=rid, pnc=pid)], dma_engine_mask=sum(1 << e for e in ok),
+                    remote_sem=T.sem["arr%d" % t], src=T.zs[:, S * t + 64 * b:S * t + 64 * b + 64],
+                    dst=T.Z[:, S * t + 64 * rank:S * t + 64 * rank + 64]))
+            return q.remote_dma_fused(trs, local_sem=T.sem["snt%d" % t])
+        emit("G", send, ext(None), [A("zs", lo, lo + S)], 500.0)
+        ops[-1]["send"] = t
+        who(t + 1)
+        for h in range(0, W, 1024):
+            select(A("Ch", h, h + 1024), A("C", O + lo + S + h, O + lo + S + h + 1024), [[0, 1024]], Op.is_ge, 0, 0)
+            wrap(A("p6", h // 16, h // 16 + 64), "Wh", lambda r: A("Ch", h + r, h + 1024, 16))
+        parent_list(t + 1, "p6")
+        if t == R - 2:
+            for h in range(0, W, 512):
+                a = O + lo + S + h
+                act(A("CO", a, a + 512), A("C", a, a + 512), Fn.Identity, bias=1024.0)
+        act(A("junk", 0, 256), A("XA", O + lo, O + lo + S), Fn.Sign, bias=0.5, acc=col("ac", 2))
+        ops[-1]["r"] += [("E5", 256 * nv5, 256 * 14)]
+        for i in range(2):
+            a = S + 896 * i
+            act(A("junk", a, a + 896), A("XA", O + lo + a, O + lo + a + 896), Fn.Sign, bias=0.5, acc=col("ac", 8 + i))
+            ops[-1]["r"] += [("cn", 0, 256)]
+        act(col("ac", 4), col("ac", 8), Fn.Identity, bias=col("ac", 9))
+        act(col("ac", 3), col("ac", 2), Fn.Identity, bias=col("ac", 4))
+        act(col("ac", 0), col("ac", 3), Fn.Identity, bias=1024.0 if t == 0 else col("ac", 5), scale=-0.5)
+        act(col("ac", 5), col("ac", 4), Fn.Identity, bias=128.0, scale=0.5)
+        gfill(A("XA", O + lo, O + lo + S), -512)
+        if t == 0:
+            gfill(A("XA", O - 1, O), 0)
+        back("p0", "v4", "M1", 4)
+        cp(A("tb", 0, 256), A("p0", 0, 256))
+        back("p0", "tb", "M0", 1)
+        ts(A("D", O + B, O + B + S), A("p0", 0, 256), float(lo), Op.add)
+        back("p2", "v5", "M1", 4)
+        cp(A("tc", 0, 256), A("p2", 0, 256))
+        back("p2", "tc", "M0", 1)
+        act(A("dn", 0, 256), A("p2", 0, 256), Fn.Identity, bias=float(lo))
+        cp(SCT(A("D", 0, O + B), A("lo1", 0, 16)), A("dn", 0, 256))
+        pre_terms(t + 1)
+    return ops
+
+
+def _meet(a, b):
+    if a[2] <= b[1] or b[2] <= a[1]:
+        return False
+    return len(a) < 4 or len(b) < 4 or a[3] == b[3]
+
+
+def hazards(ops):
+    seen = {}
+    for i, o in enumerate(ops):
+        o["key"] = o["sem"] if o["sem"] is not None else o["e"]
+        follow, wait = set(), set()
+        for kind in ("r", "w"):
+            for reg in o[kind]:
+                psum = SCRATCH[reg[0]][0] == "psum"
+                for (j, k2, reg2) in seen.get(reg[0], []):
+                    other = ops[j]["key"] != o["key"]
+                    if psum:
+                        if other or o["e"] == "P":
+                            follow.add(j)
+                        if other:
+                            wait.add(j)
+                    elif (kind == "w" or k2 == "w") and _meet(reg, reg2):
+                        follow.add(j)
+                        if other or o["sem"] is None:
+                            wait.add(j)
+        for kind in ("r", "w"):
+            for reg in o[kind]:
+                old = seen.setdefault(reg[0], [])
+                if SCRATCH[reg[0]][0] == "psum" and o["e"] == "P":
+                    old[:] = []
+                old.append((i, kind, reg))
+        o["follow"], o["wait"] = follow, wait
+
+
+def schedule(ops):
+    hazards(ops)
+    n, wake = len(ops), CFG["wake"]
+    edges = [[] for _ in ops]
+    sends = {o["send"]: i for i, o in enumerate(ops) if "send" in o}
+    dmas = {}
+    for i, o in enumerate(ops):
+        pre = {j: (ops[j]["lat"] + wake if j in o["wait"] else 0.0) for j in o["follow"]}
+        if o["arr"] is not None:
+            pre[sends[o["arr"]]] = CFG["far"]
+        name = "dma" + o["e"] if o["sem"] is not None else o.get("chain")
+        if name is not None:
+            if name in dmas:
+                pre.setdefault(dmas[name], 0.0)
+            dmas[name] = i
+        o["pre"] = pre
+        for j, d in pre.items():
+            edges[j].append((i, d))
+    way = [0.0] * n
+    for i in range(n - 1, -1, -1):
+        way[i] = ops[i]["c"] + max([ops[i]["lat"]] + [d + way[j] for j, d in edges[i]])
+    before = [list(o["pre"].items()) for o in ops]
+
+    def place(rank, links, head):
+        end = [0.0] * n
+        busy = {e: ([], []) for e in "VSPGY"}
+        for i in sorted(range(n), key=rank):
+            c = ops[i]["c"]
+            at = max([head[i]] + [end[j] + d for j, d in links[i]])
+            starts, ends = busy[ops[i]["e"]]
+            a, b = 0, len(ends)
+            while a < b:
+                mid = (a + b) // 2
+                if ends[mid] <= at:
+                    a = mid + 1
+                else:
+                    b = mid
+            while a < len(starts) and starts[a] < at + c:
+                at = max(at, ends[a])
+                a += 1
+            starts.insert(a, at)
+            ends.insert(a, at + c)
+            end[i] = at + c
+        return end
+
+    lat, zero = [o["lat"] for o in ops], [0.0] * n
+    end = place(lambda i: (-way[i], i), before, zero)
+    best = None
+    for _ in range(CFG["turns"]):
+        rev = place(lambda i: (-end[i], -i), edges, lat)
+        end = place(lambda i: (-rev[i], i), before, zero)
+        span = max(end[i] + lat[i] for i in range(n))
+        if best is None or span < best[0]:
+            best = (span, end)
+    end = best[1]
+    return [ops[i] for i in sorted(range(n), key=lambda i: (end[i] - ops[i]["c"], i))]
+
+
+def order(ops):
+    hazards(ops)
+    known, count = {}, {}
+    for o in ops:
+        count[o["key"]] = count.get(o["key"], 0) + 1
+        o["idx"] = count[o["key"]]
+        kn = known.setdefault(o["e"], {})
+        need = {}
+        for j in o["wait"]:
+            p = ops[j]
+            if p["idx"] > kn.get(p["key"], 0) and p["idx"] > need.get(p["key"], (0, 0))[0]:
+                need[p["key"]] = (p["idx"], j)
+        waits = []
+        for key in sorted(need, key=lambda k: -need[k][1]):
+            idx, j = need[key]
+            if idx > kn.get(key, 0):
+                waits.append(j)
+                ops[j]["sig"] = True
+                kn[key] = idx if ops[j]["sem"] is None else 10 ** 6
+                for k2, v2 in ops[j]["vc"].items():
+                    if v2 > kn.get(k2, 0):
+                        kn[k2] = v2
+        o["waits"] = waits
+        o["vc"] = dict(kn)
+    return count
+
+
+def rank_program(g, core, T, topo):
+    rank = T.rank_of(core)
+    if rank is None:
+        return
+    ops = schedule(build(T, rank, topo, core))
+    count = order(ops)
+    queue = {"V": g.vector, "S": g.scalar, "P": g.tensor, "G": g, "Y": g.sync}
+    raised = {}
+    for o in ops:
+        if o["sem"] is None and o.get("sig"):
+            raised[o["e"]] = raised.get(o["e"], 0) + 1
+            o["val"] = raised[o["e"]]
+    for o in ops:
+        q = queue[o["e"]]
+        for j in o["waits"]:
+            p = ops[j]
+            if p["sem"] is None:
+                q.wait_ge(T.sem["e" + p["e"]], p["val"])
+            else:
+                q.wait_ge(T.sem[p["sem"]], 16 * count[p["sem"]])
+        if o["arr"] is not None:
+            q.wait_ge(T.sem["arr%d" % o["arr"]], 8)
+        ins = o["f"](q)
+        if o["sem"] is not None:
+            ins.then_inc(T.sem[o["sem"]], 16)
+        elif o.get("sig"):
+            ins.then_inc(T.sem["e" + o["e"]], 1)
+    for n in ("dya", "dyo", "dyy", "dyx", "dyc"):
+        g.wait_ge(T.sem[n], 16)
+    for t in range(R - 1):
+        g.wait_ge(T.sem["snt%d" % t], 8)

@@ -7,8 +7,8 @@ PW = O + W + R * S
 BF, F32, F16, I32, U16 = "bfloat16", "float32", "float16", "int32", "uint16"
 MAGIC = 12582912.0
 K3 = 65536.0
-CFG = {"ns4": 9, "ns5": 6, "dv": 52, "ov": 50, "cyc": 1.04, "pe": 0.55, "get": 1.56, "put": 3.8,
-       "wake": 70.0, "far": 3500.0, "turns": 5, "pin": 0, "pin2": 1}
+CFG = {"ns4": 9, "ns5": 5, "dv": 50, "ov": 56, "cyc": 0.9, "pe": 0.5, "get": 1.56, "put": 3.8,
+       "wake": 150.0, "far": 3500.0, "turns": 2, "late": 3, "at4": -1, "at5": 9, "pin2": 1, "v4": 0.9, "mid": 64, "mix": 1, "spread": 0.0}
 
 SCRATCH = {}
 
@@ -36,7 +36,7 @@ for _n, _c, _d in [
     ("F", 130, BF), ("Sb", 130, BF), ("cum", 130, F32), ("IB", [128, 16], BF), ("bs", 128, F32), ("lb", 16, U16),
     ("E3", 256, BF), ("U", 144, F32), ("kp", 4, F32), ("ou", 16, F32), ("lo1", 16, U16), ("lo2", 16, U16), ("lx", 16, U16),
     ("y", 256, BF), ("dg", 256, F16), ("ta", 256, F16), ("tb", 256, F16), ("tc", 256, F16),
-    ("v4", 256, F16), ("v5", 256, F16), ("tr", 256, F16), ("tq", 256, F16), ("m4", 16, F32), ("m5", 16, F32), ("mc", 32, F16),
+    ("v4", 256, F16), ("v5", 256, F16), ("tr", 256, F16), ("tq", 352, F16), ("KI", 2176, F16), ("m4", 16, F32), ("mc", 32, F16),
     ("cn", 256, F32), ("xb", 256, BF), ("av", 256, BF), ("dn", 256, F32),
     ("thw", 48, F32), ("th", 192, F32), ("cc", 192, F32), ("fl", 64, F32), ("wq", 64, F32),
     ("lh", 32, U16), ("hg", 512, F16), ("sc", 512, F16), ("lw", 16, U16),
@@ -46,7 +46,7 @@ for _n, _c, _d in [
 for _k in range(8):
     SCRATCH["p%d" % _k] = ("psum", [128, 512], F32)
 
-DMA_SEMS = ["dx", "dc0", "dcm", "dcd", "dag", "ddl", "drep", "dya", "dyo", "dyx", "dyy", "dyc"]
+DMA_SEMS = ["dx", "dx2", "dc0", "dcm", "dcd", "dag", "ddl", "drep", "dya", "dyo", "dyx", "dyy", "dyc"]
 SEMAPHORES = ["eV", "eS", "eP", "eG"] + DMA_SEMS + ["arr0", "arr1", "arr2", "snt0", "snt1", "snt2"]
 
 
@@ -176,9 +176,11 @@ def build(T, rank, topo, core):
         return A(n, j, j + 1)
 
     ns4, ns5, dv, ov = CFG["ns4"], CFG["ns5"], CFG["dv"], CFG["ov"]
-    nv4, nv5 = 16 - ns4, 14 - ns5
+    early = 16 - CFG["late"]
+    nv4, nv5 = 16 - ns4, early - ns5
     s16 = view(T.s16[:], "s16", 0, 256, 256)
-    dma("Y", A("X", O, O + W), ext(T.x0[:]), "dx", 512)
+    dma("Y", A("X", O, O + W // 2), ext(T.x0[:, 0:W // 2]), "dx", 256)
+    dma("Y", A("X", O + W // 2, O + W), ext(T.x0[:, W // 2:W]), "dx2", 512)
     dma("S", A("CM", 0, S), ext(T.come[:, 0:S]), "dc0", 64)
     dma("S", A("cdi", 0, 128), ext(T.cd0[:]), "dcd", 64)
     dma("S", A("agi", 0, 48), ext(T.age[:]), "dag", 24)
@@ -207,9 +209,8 @@ def build(T, rank, topo, core):
     gfill(A("F", 0, 1), 0)
     gfill(A("cJ4", 0, 16 * nv4), -43008)
     gfill(A("cJ4", 16 * nv4, 256), -10240)
-    gfill(A("cJ5", 0, 16 * nv5), -43008)
-    gfill(A("cJ5", 16 * nv5, 224), -10240)
-    gfill(A("cJ5", 224, 256), -43008)
+    gfill(A("cJ5", 0, 16 * ns5), -10240)
+    gfill(A("cJ5", 16 * ns5, 256), -43008)
     gfill(lane("th", 0, 192, 4), -1)
     ts(col("pt", 0), col("pi", 0), 15, Op.bitwise_and)
     ts(col("pt", 1), col("pi", 0), 112, Op.bitwise_and)
@@ -238,12 +239,14 @@ def build(T, rank, topo, core):
         ts(A("M1", 160 * a, 160 * a + 160), A("jrow", 0, 160), col("pc", 4), Op.is_equal, col("pc", 12 + a), Op.mult)
     select(A("TL", 0, 128), A("BD", 0, 128), [[1, 128]], Op.is_ge, 0, -1)
     select(A("TU", 0, 128), A("BD", 0, 128), [[-1, 128]], Op.is_gt, 0, 1)
-    select(A("seg8", 0, 128), A("one", 0, 128), [[0, 16], [1, 8]], Op.is_gt, 0, 0)
+    select(A("seg8", 0, 64), A("one", 0, 64), [[0, 16], [1, 4]], Op.is_gt, 0, 0)
     act(A("sv", 0, 16), A("sw", 0, 16), Fn.Identity, bias=256.0)
     select(A("segn", 0, 256), A("X", 0, 256), [[0, 16], [1, 16]], Op.not_equal, 0, 0, -60000.0)
     ts(A("mk", 0, 256), A("jm", 0, 256), col("pc", 1), Op.not_equal, -48976.0, Op.mult)
     ts(A("Wh", 0, 144), A("WS1", 0, 144), 0.0625, Op.mult)
-    gfill(A("CO", 0, O + S * (R - 1)), 0)
+    iota(A("CO", 0, 2048), [[61, 16], [0, 128]], 7, 0)
+    select(A("KI", 0, 2048), A("CO", 0, 2048), [[0, 16], [1, 128]], Op.is_equal, 0, -1)
+    select(A("KI", 2048, 2176), A("one", 0, 128), [[1, 128]], Op.is_equal, 0, -1)
     select(A("UW", 0, 2048), A("UWi", 0, 2048), [[1, 16], [16, 8], [0, 16]], Op.is_equal, 0, -1)
     for t in range(R - 1):
         act(lane("cc", 64 * t, 64 * t + 64, 4), A("sw", 0, 16), Fn.Identity, bias=float(W + S * t))
@@ -270,11 +273,12 @@ def build(T, rank, topo, core):
 
     def who(t):
         lo = S * t
-        wrap(A("p7", 0, 128), "WS1", lambda r: A("X", O + lo + r, O + lo + W, 16))
-        act(A("sq", 0, 128), A("p7", 0, 128), Fn.Square)
-        tt(A("wi", 0, 128), A("sq", 0, 128), A("p32", 0, 128), Op.add)
-        ts(A("wj", 0, 128), A("wi", 0, 128), 5, Op.arith_shift_right, S - 1, Op.bitwise_and)
-        cp(A("who", 0, 128), A("wj", 0, 128))
+        for a, b, bank in ([(0, 64, "p7"), (64, 128, "p2")] if t == 0 else [(0, 128, "p7")]):
+            wrap(A(bank, a, b), "WS1", lambda r: A("X", O + lo + 16 * a + r, O + lo + 16 * b, 16))
+            act(A("sq", a, b), A(bank, a, b), Fn.Square)
+            tt(A("wi", a, b), A("sq", a, b), A("p32", a, b), Op.add)
+            ts(A("wj", a, b), A("wi", a, b), 5, Op.arith_shift_right, S - 1, Op.bitwise_and)
+            cp(A("who", a, b), A("wj", a, b))
 
     def parent_list(t, src):
         c0, r0 = divmod(ST * (t + 1), 16)
@@ -290,7 +294,7 @@ def build(T, rank, topo, core):
         act(col("lf", 128), col("kp", 3), Fn.Identity, bias=free, scale=col("kp", 2))
         cp(A("lc", 0, 129), A("lf", 0, 129))
 
-    pieces = [("V", 0, 32, "p0"), ("S", dv, 32, "p4"), ("V", 32, dv - 32, "p1"), ("S", dv + 32, 32, "p5"),
+    pieces = [("V", 0, 32, "p0"), ("S", 32, 32, "p4"), ("V", 64, dv - 32, "p1"), ("S", dv + 32, 32, "p5"),
               ("S", dv + 64, 64 - dv, "p6")]
 
     def pre_terms(t):
@@ -331,10 +335,22 @@ def build(T, rank, topo, core):
         return vrow, srows, const, count
 
     def spread(m, j, lo, bank, out):
-        ts(A("mc", 16 * j, 16 * j + 16), A(m, 0, 16), float(-lo - 1), Op.max)
+        if m is not None:
+            ts(A("mc", 16 * j, 16 * j + 16), A(m, 0, 16), float(-lo - 1), Op.max)
         for r in range(16):
             mm(A(bank, r, 256, 16), A("UW", 128 * r, 128 * r + 128), A("mc", 16 * j, 16 * j + 16), True, True)
         act(out, A(bank, 0, 256), Fn.Identity, bias=float(lo if lo == S * (R - 1) else lo - 1024))
+
+    def tree(v, bank, c, k0, k1, tmp, at, out):
+        steps = [lambda: tt(A(v, 16 * k0, 16 * k1), A(bank, 16 * k0, 16 * k1), A(c, 16 * k0, 16 * k1), Op.min)]
+        src, a, n = v, 16 * k0, k1 - k0
+        top = A(src, a, a + 16)
+        while n > 1:
+            h = (n + 1) // 2
+            top = out if h == 1 and out is not None else A(tmp, at, at + 16 * h)
+            steps.append(lambda o=top, x=A(src, a, a + 16 * h), z=A(src, a + 16 * (n - h), a + 16 * n): tt(o, x, z, Op.max))
+            src, a, n, at = tmp, at, h, at + 16 * h
+        return steps, top
 
     def chunks(a, b):
         cut = list(range(a, max(b - 3, a + 1), 4)) + [b]
@@ -345,12 +361,19 @@ def build(T, rank, topo, core):
     parent_list(0, "cdn")
     pre_terms(0)
 
-    def places():
+    def places(t):
         cp(A("hi", 0, 16), A("uq", 0, 16))
         ts(A("hj", 0, 16), A("hi", 0, 16), 5, Op.arith_shift_right, W - 1, Op.bitwise_and)
-        ts(A("hA", 0, 16), A("hj", 0, 16), col("ac", 0), Op.add)
-        tt(A("T1", 0, 256), IND(A("ua", 0, 16), A("L16", 0, 16)), A("Kc", 0, 256), Op.mult)
-        tt(A("T2", 0, 256), IND(A("hA", 0, 16), A("L16", 0, 16)), A("T1", 0, 256), Op.add)
+        if t == 0:
+            cp(A("hA", 0, 16), A("hj", 0, 16))
+            tt(A("T1", 0, 256), IND(A("ua", 0, 16), A("L16", 0, 16)), A("Kc", 0, 256), Op.mult)
+            tt(A("T2", 0, 256), IND(A("hA", 0, 16), A("L16", 0, 16)), A("T1", 0, 256), Op.add)
+        else:
+            ts(A("tq", 336, 352), A("hj", 0, 16), col("ac", 0), Op.add, -2048.0, Op.add)
+            for m in range(16):
+                mm(A("p7", 16 * m, 16 * m + 16), A("KI", 128 * m, 128 * m + 128), A("tq", 320, 336), True, False)
+                mm(A("p7", 16 * m, 16 * m + 16), A("KI", 2048, 2176), A("tq", 336, 352), False, True)
+            ts(A("T2", 0, 256), A("p7", 0, 256), 4194304.0, Op.add)
         ts(A("c4", 0, 256), A("T2", 0, 256), W - 1, Op.bitwise_and)
         ts(A("o4", 0, 256), A("c4", 0, 256), 16.0, Op.add)
 
@@ -366,12 +389,13 @@ def build(T, rank, topo, core):
                 mm(A("p3", 64 * b, 64 * b + 64), A("Ih", 0, 128), src, False, i == N - 1, arr=t - 1 if i == 1 else None)
         ts(xa, A("p3", 0, 256), MAGIC, Op.add, MAGIC, Op.subtract)
         wrap(A("p7", 0, 16), "WS1", lambda r: A("X", O + B + r, O + B + S, 16))
-        act(A("ua", 0, 16), A("p7", 0, 16), Fn.Identity)
         act(A("uq", 0, 16), A("p7", 0, 16), Fn.Square)
-        if t == 0:
-            places()
+        if t > 0:
+            ts(A("tq", 320, 336), A("p7", 0, 16), -2048.0, Op.add)
+        else:
+            act(A("ua", 0, 16), A("p7", 0, 16), Fn.Identity)
+            places(0)
             who(0)
-            ops[-1]["r"] += [("o4", 0, 256)]
         for i, (e, k, n, bank) in enumerate(pieces):
             a, m = O + lo + 16 * k, 16 * n
             ed, got = A("Ed", 16 * k, 16 * k + m), IND(xa, A("who", k, k + n))
@@ -390,20 +414,24 @@ def build(T, rank, topo, core):
             mm(A(bank, 0, m), A("BDv" if e == "V" else "BDs", 0, 128), ed, False, True)
             tt(A("XA", a, a + m), A(bank, 0, m), A("X", a, a + m), Op.min)
         if t > 0:
-            places()
+            places(t)
         ov = CFG["ov"] if t > 0 else 62
         wall = A("XA", 0, O + B)
         win = A("XA", lo + O - 16, O + B)
-        ts(A("Og", 0, 16 * ov), IND(wall, A("lc", 0, ov)), 0.0, Op.min, -1.0, Op.max)
+        cut = 128 - ov
+        ts(A("Og", 16 * cut, 2064), IND(wall, A("lc", cut, 129)), 0.0, Op.min, -1.0, Op.max)
         if CFG["pin2"]:
-            ops[-1]["r"] += [("T1", 0, 256), ("hA", 0, 16)]
-        act(A("Og", 16 * ov, 1024), IND(wall, A("lc", ov, 64)), Fn.Sign, bias=0.5)
-        act(A("Og", 1024, 2064), IND(wall, A("lc", 64, 129)), Fn.Sign, bias=0.5)
+            ops[-1]["r"] += [("T2", 0, 256) if CFG["pin2"] == 1 else ("o4", 0, 256)]
+        mid = min(CFG["mid"], cut - 2)
+        act(A("Og", 0, 16 * mid), IND(wall, A("lc", 0, mid)), Fn.Sign, bias=0.5)
+        chain("S")
+        act(A("Og", 16 * mid, 16 * cut), IND(wall, A("lc", mid, cut)), Fn.Sign, bias=0.5)
+        chain("S")
         mm(A("p6", 0, 129), A("Ip", 0, 128), A("cH", 0, 129), True, False)
         wrap(A("p6", 0, 128 - c0), "WS1", lambda r: A("XA", O + lo + 16 * c0 + r, O + B, 16), False, False)
         wrap(A("p6", 128 - c0, 129), "WS1", lambda r: A("XA", O + lo + r, O + lo + 16 * c0 + 16, 16), False, False)
-        wrap(A("p6", 0, 64), "WSz", lambda r: A("Og", r, 1024, 16), False, False)
-        wrap(A("p6", 64, 129), "WSz", lambda r: A("Og", 1024 + r, 2064, 16), False, True)
+        wrap(A("p6", 0, mid), "WSz", lambda r: A("Og", r, 16 * mid, 16), False, False)
+        wrap(A("p6", mid, 129), "WSz", lambda r: A("Og", 16 * mid + r, 2064, 16), False, True)
         ts(A("F", 1, 130), A("p6", 0, 129), 6000.0, Op.is_ge)
         mm(A("p6", 0, 129), A("BD", 0, 128), A("F", 1, 130), True, True)
         mm(A("p7", 0, 129), A("TL", 0, 128), A("F", 1, 130), True, False)
@@ -416,13 +444,17 @@ def build(T, rank, topo, core):
         ts(A("Ub", 16, 32), A("sw", 0, 16), col("Sb", 127 - c0), Op.is_ge, -2048.0, Op.mult)
         act(col("U", 0), col("Sb", 128), Fn.Identity, scale=-1.0)
         act(A("Ub", 32, 48), A("sw", 0, 16), Fn.Relu, bias=col("U", 0))
-        for b in range(8):
-            ts(view(T.IB[:, b:128:8, :], "IB", 0, 2048, 256, b), s16, col("p6", b), Op.is_ge)
-        wrap(A("p7", 0, 128), "WS1", lambda r: view(T.IB[:, :, r], "IB", 0, 2048, 128))
-        scan(A("bs", 0, 128), A("seg8", 0, 128), A("p7", 0, 128), Op.mult, Op.add)
-        cp(A("lb", 0, 16), A("bs", 7, 128, 8))
+        for h in range(2):
+            for b in range(4):
+                ts(view(T.IB[:, 64 * h + b:64 * h + 64:4, :], "IB", 1024 * h, 1024 * h + 1024, 256, b), s16,
+                   col("p6", 4 * h + b), Op.is_ge)
+                chain("IB")
+            wrap(A("p7", 0, 64), "WS1", lambda r: view(T.IB[:, 64 * h:64 * h + 64, r], "IB", 1024 * h, 1024 * h + 1024, 64),
+                 h == 0, h == 1)
+        scan(A("bs", 0, 64), A("seg8", 0, 64), A("p7", 0, 64), Op.mult, Op.add)
+        cp(A("lb", 0, 16), A("bs", 3, 64, 4))
         tt(A("E3", 0, 256), IND(A("cum", 0, 129), A("lb", 0, 16)), A("s1", 0, 256), Op.is_le)
-        act(A("Ub", 48, 64), A("bs", 7, 128, 8), Fn.Identity, scale=16.0)
+        act(A("Ub", 48, 64), A("bs", 3, 64, 4), Fn.Identity, scale=16.0)
         for i in range(4):
             mm(A("p6", 0, 16), A("Ip", 0, 128), A("Ub", 16 * i, 16 * i + 16), i == 0, False)
         wrap(A("p6", 0, 16), "WS1", lambda r: A("E3", r, 256, 16), False, True)
@@ -442,52 +474,56 @@ def build(T, rank, topo, core):
         for k in range(nv4):
             vrow(k)
         srows(nv4, 16)
-        for k0, k1 in chunks(nv4, 16):
-            count("p4", k0, k1, "WSs")
-        for k0, k1 in chunks(0, nv4):
-            count("p4", k0, k1, "WSv", k1 == nv4)
-        tt(A("v4", 0, 256), A("p4", 0, 256), A("c4", 0, 256), Op.min)
-        tt(A("tr", 0, 128), A("v4", 0, 128), A("v4", 128, 256), Op.max)
-        tt(A("tr", 128, 192), A("tr", 0, 64), A("tr", 64, 128), Op.max)
-        tt(A("tr", 192, 224), A("tr", 128, 160), A("tr", 160, 192), Op.max)
-        tt(A("m4", 0, 16), A("tr", 192, 208), A("tr", 208, 224), Op.max)
+        cs = sorted(chunks(0, nv4) + chunks(nv4, 16), key=lambda x: CFG["v4"] * x[1] / nv4 if x[0] < nv4 else (x[1] - nv4) / ns4)
+        for k0, k1 in cs:
+            count("p4", k0, k1, "WSv" if k0 < nv4 else "WSs", (k0, k1) == cs[-1])
+        steps4, _ = tree("v4", "p4", "c4", 0, 16, "tr", 0, A("m4", 0, 16))
+        yy = A("y", 0, 256)
+        vrow, srows, const, count = judge_parts("E5", "o5", yy, win, "cJ5")
+        const("p5", 0, early)
+        const("p1", early, 16)
+        if CFG["at4"] < 0:
+            while steps4:
+                steps4.pop(0)()
+        for k in range(ns5, early):
+            vrow(k)
+            if k - ns5 >= CFG["at4"] and steps4:
+                steps4.pop(0)()
+                chain("V")
+        for step in steps4:
+            step()
         spread("m4", 0, lo, "p4", A("CO" if last else "C", O + B, O + B + S))
         if t == 0:
             ages()
         if not last:
             ts(A("lh", 0, 16), A("mc", 0, 16), float(lo + O), Op.add)
             act(lane("cc", 64 * t + 1, 64 * t + 64, 4), A("m4", 0, 16), Fn.Identity, bias=float(lo))
-        yy = A("y", 0, 256)
-        vrow, srows, const, count = judge_parts("E5", "o5", yy, win, "cJ5")
-        const("p5", 0, 14)
-        const("p1", 14, 16)
-        for k in range(nv5):
-            vrow(k)
-        srows(nv5, 14)
-        cs = sorted(chunks(0, nv5) + chunks(nv5, 14), key=lambda x: (x[1] - nv5) / ns5 if x[0] >= nv5 else x[1] / (nv5 + 2))
+        srows(0, ns5)
+        cs = sorted(chunks(0, ns5) + chunks(ns5, early), key=lambda x: x[1] / ns5 if x[0] < ns5 else (x[1] - ns5) / (16 - ns5))
         for k0, k1 in cs:
-            count("p5", k0, k1, "WSv" if k0 < nv5 else "WSs", (k0, k1) == cs[-1])
-        vrow(14)
-        if CFG["pin"]:
-            ops[-1]["r"] += [("mc", 0, 16)]
-        vrow(15)
-        count("p1", 14, 16, "WSv", True)
-        tt(A("v5", 0, 224), A("p5", 0, 224), A("c5", 0, 224), Op.min)
-        tt(A("tq", 0, 112), A("v5", 0, 112), A("v5", 112, 224), Op.max)
-        tt(A("tq", 112, 176), A("tq", 0, 64), A("tq", 48, 112), Op.max)
-        tt(A("tq", 176, 208), A("tq", 112, 144), A("tq", 144, 176), Op.max)
-        tt(A("tq", 208, 224), A("tq", 176, 192), A("tq", 192, 208), Op.max)
-        tt(A("v5", 224, 256), A("p1", 224, 256), A("c5", 224, 256), Op.min)
-        tt(A("tq", 224, 240), A("v5", 224, 240), A("v5", 240, 256), Op.max)
-        tt(A("m5", 0, 16), A("tq", 208, 224), A("tq", 224, 240), Op.max)
-        ts(A("lx", 0, 16), A("m5", 0, 16), 16.0, Op.add)
-        spread("m5", 1, lo, "p6", A("cn", 0, 256))
+            count("p5", k0, k1, "WSs" if k0 < ns5 else "WSv", (k0, k1) == cs[-1])
+        steps5, top = tree("v5", "p5", "c5", 0, early, "tq", 0, None)
+        steps5.append(lambda: ts(A("tq", 240, 256), top, float(-lo - 1), Op.max))
+        for k in range(early, 16):
+            vrow(k)
+            if k >= early + CFG["at5"]:
+                steps5.pop(0)()
+                chain("V")
+        count("p1", early, 16, "WSv", True)
+        for step in steps5:
+            step()
+        steps5, top = tree("v5", "p1", "c5", early, 16, "tq", 256, None)
+        for step in steps5:
+            step()
+        tt(A("mc", 16, 32), A("tq", 240, 256), top, Op.max)
+        ts(A("lx", 0, 16), A("mc", 16, 32), 16.0, Op.add)
+        spread(None, 1, lo, "p6", A("cn", 0, 256))
         mm(A("p7", 0, 256), A("Ih", 0, 128), yy, True, False)
         mm(A("p7", 0, 256), A("Ih", 0, 128), A("cH", 0, 256), False, False)
         act(A("xb", 0, 256), IND(win, A("lx", 0, 16)), Fn.Identity)
         mm(A("p7", 0, 256), A("Ih", 0, 128), A("xb", 0, 256), False, True)
-        act(A("U", 16, 32), A("m5", 0, 16), Fn.Relu, scale=-2.0)
-        tt(A("U", 32, 48), A("ou", 0, 16), A("U", 16, 32), Op.subtract)
+        ts(A("U", 16, 32), A("mc", 16, 32), 0.0, Op.min, 8192.0, Op.mult)
+        tt(A("U", 32, 48), A("ou", 0, 16), A("U", 16, 32), Op.add)
         tt(A("U", 48, 64), A("U", 32, 48), A("sv", 0, 16), Op.max)
         cp(A("lo2", 0, 16), A("U", 48, 64))
         if last:
@@ -549,7 +585,7 @@ def build(T, rank, topo, core):
                 a = O + lo + S + h
                 act(A("CO", a, a + 512), A("C", a, a + 512), Fn.Identity, bias=1024.0)
         act(A("junk", 0, 256), A("XA", O + lo, O + lo + S), Fn.Sign, bias=0.5, acc=col("ac", 2))
-        ops[-1]["r"] += [("E5", 256 * nv5, 256 * 14)]
+        ops[-1]["r"] += [("E5", 0, 256 * ns5)]
         for i in range(2):
             a = S + 896 * i
             act(A("junk", a, a + 896), A("XA", O + lo + a, O + lo + a + 896), Fn.Sign, bias=0.5, acc=col("ac", 8 + i))
@@ -614,7 +650,10 @@ def schedule(ops):
     edges = [[] for _ in ops]
     sends = {o["send"]: i for i, o in enumerate(ops) if "send" in o}
     dmas = {}
+    mix = CFG["mix"]
     for i, o in enumerate(ops):
+        mix = (mix * 1103515245 + 12345) % 2147483648
+        o["c"] *= 1 + CFG["spread"] * (mix / 2147483648 - 0.5)
         pre = {j: (ops[j]["lat"] + wake if j in o["wait"] else 0.0) for j in o["follow"]}
         if o["arr"] is not None:
             pre[sends[o["arr"]]] = CFG["far"]

@@ -3,44 +3,47 @@ from concourse.mybir import AluOpType as Op, ActivationFunctionType as Fn
 
 W, S, R, ST, N = 2048, 256, 4, 341, 4
 O = 528
+Y0 = 256
 PW = O + W + R * S
 BF, F32, F16, I32, U16 = "bfloat16", "float32", "float16", "int32", "uint16"
 MAGIC = 12582912.0
 K3 = 65536.0
-CFG = {"ns4": 9, "ns5": 5, "dv": 50, "ov": 56, "cyc": 0.9, "pe": 0.5, "get": 1.56, "put": 3.8,
-       "wake": 150.0, "far": 3500.0, "turns": 2, "late": 3, "at4": -1, "at5": 9, "pin2": 1, "v4": 0.9, "mid": 64, "mix": 1, "spread": 0.0}
+CFG = {"ns4": 9, "ns5": 5, "late": 3, "own": "VVSS", "og": "SSSV", "v4": 0.9, "calls": 2, "pre": 2,
+       "tries": 12, "turns": 2, "spread": 0.3, "mix": 1, "shakes": 3000, "span": 2000.0, "heat": 100.0}
+PACE = [(0.83, 1.56, 3.8, 0.42, 110.0, 4200.0), (1.15, 1.8, 5.0, 0.58, 90.0, 4200.0),
+        (0.88, 1.2, 2.5, 0.44, 190.0, 5500.0), (1.04, 1.5, 3.5, 0.52, 130.0, 3300.0)]
 
 SCRATCH = {}
 
 
 def _sb(name, cols, dtype):
-    SCRATCH[name] = ("sbuf", [128] + (cols if isinstance(cols, list) else [cols]), dtype)
+    SCRATCH[name] = ("sbuf", [128, cols], dtype)
 
 
 for _n, _c, _d in [
-    ("X", PW, BF), ("XA", PW, BF), ("C", PW, F32), ("D", PW, I32), ("CM", R * S, BF),
-    ("cdi", 128, I32), ("cdf", 128, F32), ("cdh", 128, F16), ("agi", 48, I32),
-    ("cdn", 128, F32), ("cdm", 128, F32),
+    ("X", PW, BF), ("XA", PW, BF), ("XF", PW, F32), ("C", PW, F32), ("D", PW, I32), ("CM", R * S, BF),
+    ("cdi", 128, I32), ("cdf", 128, F32), ("cdh", 128, F16), ("agi", 48, I32), ("cdm", 128, BF),
     ("jrow", 256, F32), ("pi", 1, I32), ("pt", 4, I32), ("pc", 16, F32), ("jg", 128, F32), ("jm", 256, F32),
     ("WS1", 144, BF), ("WSv", 144, BF), ("WSs", 144, BF), ("WSz", 144, BF), ("Wh", 144, F16), ("Ch", W, F16), ("CO", PW, F32),
-    ("BD", 128, BF), ("BD2", 128, BF), ("BDv", 128, BF), ("BDs", 128, BF), ("TL", 128, BF), ("TU", 128, BF), ("sv", 16, F32), ("Ub", 64, BF), ("lf", 130, F32),
-    ("Ip", 128, BF), ("In", 128, BF), ("Ih", 128, BF),
-    ("M0", 4 * 160, F16), ("M1", 4 * 160, F16), ("UWi", 2048, BF), ("UW", 2048, F16),
-    ("cV", 512, BF), ("cS", 512, BF), ("cH", 256, BF), ("cJ4", 256, BF), ("cJ5", 256, BF),
-    ("one", 256, F32), ("cap", 130, BF), ("segn", 256, F16), ("seg8", 128, F32), ("aw", 256, F32), ("mk", 256, F32),
-    ("p32", 128, F32), ("Kc", 256, F32), ("s16", [16, 16], BF), ("s1", 256, BF), ("sw", 16, F32),
-    ("L16", 16, U16), ("sq", 128, F32), ("wi", 128, I32), ("wj", 128, I32), ("who", 128, U16), ("lc", 130, U16),
-    ("Ed", W, BF), ("Gd", 1536, BF), ("Og", 2064, BF), ("E4", 4096, BF), ("E5", 4096, BF), ("junk", W, BF),
-    ("ua", 16, F32), ("uq", 16, F32), ("hi", 16, I32), ("hj", 16, I32), ("hA", 16, F32),
+    ("BD", 128, BF), ("BD2", 128, BF), ("BDv", 128, BF), ("BDs", 128, BF), ("TL", 128, BF), ("TLn", 128, BF), ("Ub", 48, BF),
+    ("Ip", 128, BF), ("In", 128, BF), ("Ih", 128, BF), ("If", 128, F16),
+    ("M0", 4 * 160, F16), ("M1", 4 * 160, F16), ("UWi", 2048, BF), ("UW", 2048, F16), ("KI", 2048, F16),
+    ("cV", 512, BF), ("cS", 512, BF), ("cH", 256, BF), ("cJ4", 256, BF), ("cJ5", 256, BF), ("cF", 144 * R, BF),
+    ("one", 256, F32), ("inc", 256, BF), ("cJb", 144, F16), ("vv", 144, F32), ("Tw", 2352, F32), ("off", 144, F16),
+    ("fb", 16 * R, F16), ("segn", 256, F16), ("aw", 256, F32), ("ax", 256, F32), ("mk", 256, F32),
+    ("p32", 128, F32), ("Kc", 256, F32), ("s1", 144, BF), ("sw", 16, F32),
+    ("L16", 16, U16), ("sq", 128, F32), ("wi", 128, I32), ("wj", 128, I32), ("who", 128, U16), ("lc", 128, U16),
+    ("Ed", W, BF), ("Gd", 1536, BF), ("Og", W, BF), ("E4", 4096, BF), ("E5", 4096, BF), ("junk", W, BF),
+    ("ua", 16, F32), ("uq", 16, F32), ("hi", 16, I32), ("hj", 16, I32), ("hA", 16, F32), ("uh", 32, F16),
     ("T1", 256, F32), ("T2", 256, I32), ("c4", 256, I32), ("o4", 256, U16), ("c5", 256, F32), ("o5", 256, U16),
-    ("F", 130, BF), ("Sb", 130, BF), ("cum", 130, F32), ("IB", [128, 16], BF), ("bs", 128, F32), ("lb", 16, U16),
-    ("E3", 256, BF), ("U", 144, F32), ("kp", 4, F32), ("ou", 16, F32), ("lo1", 16, U16), ("lo2", 16, U16), ("lx", 16, U16),
-    ("y", 256, BF), ("dg", 256, F16), ("ta", 256, F16), ("tb", 256, F16), ("tc", 256, F16),
-    ("v4", 256, F16), ("v5", 256, F16), ("tr", 256, F16), ("tq", 352, F16), ("KI", 2176, F16), ("m4", 16, F32), ("mc", 32, F16),
-    ("cn", 256, F32), ("xb", 256, BF), ("av", 256, BF), ("dn", 256, F32),
-    ("thw", 48, F32), ("th", 192, F32), ("cc", 192, F32), ("fl", 64, F32), ("wq", 64, F32),
+    ("F", 130, BF), ("Sb", 144, F32), ("lb", 16, U16),
+    ("E3", 256, F16), ("U", 1, F32), ("lo1", 16, U16), ("lx", 16, U16), ("sm", 256, F16), ("avi", 256, I32),
+    ("dg", 256, F16), ("ta", 256, F16), ("tb", 256, F16), ("tc", 256, F16),
+    ("v4", 256, F16), ("v5", 256, F16), ("tr", 256, F16), ("tq", 320, F16), ("m4", 16, F32), ("mc", 32, F16),
+    ("cn", 256, F32), ("xb", 256, BF), ("dn", 256, F32),
+    ("th1", 48, F32), ("th2", 48, F32), ("cc", 192, F32), ("fl", 64, F32), ("wq", 64, F32),
     ("lh", 32, U16), ("hg", 512, F16), ("sc", 512, F16), ("lw", 16, U16),
-    ("zs", 3 * S, BF), ("Z", 3 * S, BF), ("ac", 16, F32),
+    ("zs", 3 * S, BF), ("Z", 3 * S, BF), ("ac", 8, F32),
 ]:
     _sb(_n, _c, _d)
 for _k in range(8):
@@ -52,7 +55,6 @@ SEMAPHORES = ["eV", "eS", "eP", "eG"] + DMA_SEMS + ["arr0", "arr1", "arr2", "snt
 
 def build(T, rank, topo, core):
     ops = []
-    cyc = CFG["cyc"]
 
     def view(a, name, lo, hi, n, tag=None):
         where, _, dtype = SCRATCH[name]
@@ -79,40 +81,43 @@ def build(T, rank, topo, core):
     def ap(x):
         return x["ap"] if isinstance(x, dict) else x
 
-    def emit(e, f, out, ins, cost, lat=0.0, sem=None, arr=None):
+    def emit(e, f, out, ins, cost, lat=0.0, sem=None):
         rd = list(out["rd"])
         for x in ins:
             if isinstance(x, dict):
                 rd += x["regs"]
-        ops.append({"e": e, "f": f, "w": out["regs"], "r": rd, "sem": sem, "arr": arr, "c": cost, "lat": lat})
+        ops.append({"e": e, "f": f, "w": list(out["regs"]), "r": rd, "sem": sem, "arr": None, "c": cost, "lat": lat,
+                    "after": []})
+        return len(ops) - 1
 
     def vcost(out, full, both=False):
         if out["ind"]:
-            return 50 + out["n"] * CFG["put"] * cyc
+            return (50, out["n"], 2)
         if full and full[0]["ind"]:
-            return 50 + out["n"] * CFG["get"] * cyc
+            return (50, out["n"], 1)
         k = 0.5 if out["two"] and all(x["two"] for x in full) else 1.0
         if both and not any(x["ps"] for x in full):
             k *= 2
-        return 40 + max(64, out["n"] * k) * cyc
+        return (40, max(64, out["n"] * k), 0)
 
     def ts(out, a, s1, op0, s2=None, op1=None):
         if op1 is None:
-            emit("V", lambda q: q.tensor_scalar(ap(out), ap(a), ap(s1), None, op0), out, [a, s1], vcost(out, [a]))
-        else:
-            emit("V", lambda q: q.tensor_scalar(ap(out), ap(a), ap(s1), ap(s2), op0, op1), out, [a, s1, s2], vcost(out, [a]))
+            return emit("V", lambda q: q.tensor_scalar(ap(out), ap(a), ap(s1), None, op0), out, [a, s1], vcost(out, [a]))
+        return emit("V", lambda q: q.tensor_scalar(ap(out), ap(a), ap(s1), ap(s2), op0, op1), out, [a, s1, s2],
+                    vcost(out, [a]))
 
     def tt(out, a, b, op):
-        emit("V", lambda q: q.tensor_tensor(ap(out), ap(a), ap(b), op), out, [a, b], vcost(out, [a, b], True))
+        return emit("V", lambda q: q.tensor_tensor(ap(out), ap(a), ap(b), op), out, [a, b], vcost(out, [a, b], True))
 
     def cp(out, a):
-        emit("V", lambda q: q.tensor_copy(ap(out), ap(a)), out, [a], vcost(out, [a]))
+        return emit("V", lambda q: q.tensor_copy(ap(out), ap(a)), out, [a], vcost(out, [a]))
 
     def fill(out, v):
-        emit("V", lambda q: q.memset(ap(out), v), out, [], vcost(out, []))
+        return emit("V", lambda q: q.memset(ap(out), v), out, [], vcost(out, []))
 
     def scan(out, d0, d1, op0, op1):
-        emit("V", lambda q: q.tensor_tensor_scan(ap(out), ap(d0), ap(d1), 0.0, op0, op1), out, [d0, d1], vcost(out, [d0, d1]))
+        return emit("V", lambda q: q.tensor_tensor_scan(ap(out), ap(d0), ap(d1), 0.0, op0, op1), out, [d0, d1],
+                    vcost(out, [d0, d1]))
 
     def act(out, a, fn, bias=None, scale=None, acc=None):
         kw = {}
@@ -124,61 +129,68 @@ def build(T, rank, topo, core):
         if acc is not None:
             kw["accum_out"] = ap(acc)
             o = dict(out, regs=out["regs"] + acc["regs"])
-        cost = 65 + out["n"] * CFG["get"] * cyc if a["ind"] else 60 + max(64, out["n"]) * cyc
-        emit("S", lambda q: q.activation(ap(out), ap(a), fn, **kw), o, [a, bias, scale], cost)
+        cost = (65, out["n"], 2) if out["ind"] else (65, out["n"], 1) if a["ind"] else (60, max(64, out["n"]), 0)
+        return emit("S", lambda q: q.activation(ap(out), ap(a), fn, **kw), o, [a, bias, scale], cost)
 
-    def mm(out, l, r, start, stop, arr=None):
-        emit("P", lambda q: q.matmul(ap(out), ap(l), ap(r), start, stop), out, [l, r],
-             max(64, r["n"]) * CFG["pe"] * (1 if r["two"] else 4), 60.0, arr=arr)
+    def mms(calls):
+        def run(q):
+            return [q.matmul(ap(o), ap(l), ap(r), a, z) for o, l, r, a, z in calls][-1]
+        out = dict(calls[0][0], regs=sorted(set(c[0]["regs"][0] for c in calls)))
+        return emit("P", run, out, [x for c in calls for x in c[1:3]], (0, sum(max(64, c[2]["n"]) for c in calls), 3), 60.0)
+
+    def mm(out, l, r, start, stop):
+        return mms([(out, l, r, start, stop)])
 
     def iota(out, pat, base, cm, flag=True):
-        cost = 130 + 2 * out["n"] * cyc
+        cost = (130, 2 * out["n"], 0)
         if flag:
-            emit("G", lambda q: q.iota(ap(out), pat, base, cm, allow_small_or_imprecise_dtypes=True), out, [], cost)
-        else:
-            emit("G", lambda q: q.iota(ap(out), pat, base, cm), out, [], cost)
+            return emit("G", lambda q: q.iota(ap(out), pat, base, cm, allow_small_or_imprecise_dtypes=True), out, [], cost)
+        return emit("G", lambda q: q.iota(ap(out), pat, base, cm), out, [], cost)
 
     def gfill(out, v):
-        iota(out, [[0, out["n"]]], v, 0)
+        return iota(out, [[0, out["n"]]], v, 0)
 
     def select(out, a, pat, op, base, cm, other=0.0):
-        emit("G", lambda q: q.affine_select(ap(out), ap(a), pat, op, other, base, cm), out, [a], 170 + 2 * out["n"] * cyc)
+        return emit("G", lambda q: q.affine_select(ap(out), ap(a), pat, op, other, base, cm), out, [a], (170, 2 * out["n"], 0))
 
     def dma(e, out, a, sem, kib):
-        emit(e, lambda q: q.dma_start(ap(out), ap(a)), out, [a], 60.0, 2000.0 + 5.6 * kib, sem=sem)
+        return emit(e, lambda q: q.dma_start(ap(out), ap(a)), out, [a], (60, 0, 0), 2000.0 + 5.6 * kib, sem=sem)
 
     def chain(name):
         ops[-1]["chain"] = name
+
+    def after(i):
+        ops[-1]["after"].append(i)
 
     def ws(n, r):
         return A(n, 15 - r, 143 - r)
 
     def wrap(out, n, rhs, start=True, stop=True):
-        for r in range(16):
-            mm(out, ws(n, r), rhs(r), start and r == 0, stop and r == 15)
+        return mms([(out, ws(n, r), rhs(r), start and r == 0, stop and r == 15) for r in range(16)])
+
+    def unwrap(bank, src):
+        return mms([(A(bank, r, 256, 16), A("UW", 128 * r, 128 * r + 128), src, True, True) for r in range(16)])
 
     def mshift(n, a, d):
         return A(n, 160 * a + 16 - d, 160 * a + 144 - d)
 
-    def turn(bank, src, n, m, d):
+    def turn(bank, src, n, m, d, part=range(4)):
         k = n // 4
-        for a in range(4):
-            bk, at = bank(a) if not isinstance(bank, str) else (bank, k * a)
-            for b in range(4):
-                mm(A(bk, at, at + k), mshift(m, a, d * (b - a)), A(src, b, n, 4), b == 0, b == 3)
+        mms([(A(bank, k * a, k * a + k), mshift(m, a, d * (b - a)), A(src, b, n, 4), b == 0, b == 3)
+             for a in part for b in range(4)])
 
     def back(bank, src, m, d):
-        for b in range(4):
-            for a in range(4):
-                mm(A(bank, b, 256, 4), mshift(m, b, d * (a - b)), A(src, 64 * a, 64 * a + 64), a == 0, a == 3)
+        mms([(A(bank, b, 256, 4), mshift(m, b, d * (a - b)), A(src, 64 * a, 64 * a + 64), a == 0, a == 3)
+             for b in range(4) for a in range(4)])
 
     def col(n, j):
         return A(n, j, j + 1)
 
-    ns4, ns5, dv, ov = CFG["ns4"], CFG["ns5"], CFG["dv"], CFG["ov"]
+    ns4, ns5 = CFG["ns4"], CFG["ns5"]
     early = 16 - CFG["late"]
-    nv4, nv5 = 16 - ns4, early - ns5
-    s16 = view(T.s16[:], "s16", 0, 256, 256)
+    nv4 = 16 - ns4
+    Ip, In, Ih, If = A("Ip", 0, 128), A("In", 0, 128), A("Ih", 0, 128), A("If", 0, 128)
+    sw = A("sw", 0, 16)
     dma("Y", A("X", O, O + W // 2), ext(T.x0[:, 0:W // 2]), "dx", 256)
     dma("Y", A("X", O + W // 2, O + W), ext(T.x0[:, W // 2:W]), "dx2", 512)
     dma("S", A("CM", 0, S), ext(T.come[:, 0:S]), "dc0", 64)
@@ -190,28 +202,31 @@ def build(T, rank, topo, core):
     iota(A("jrow", 0, 256), [[1, 256]], 0, 0)
     iota(A("jg", 0, 128), [[16, 8], [0, 16]], 0, 0)
     iota(A("Kc", 0, 256), [[61, 16], [0, 16]], 7, 0)
-    iota(s16, [[256, 16], [16, 16]], 0, 0)
-    iota(A("s1", 0, 256), [[1, 256]], 0, 0)
+    iota(A("s1", 0, 144), [[1, 144]], 0, 0)
     iota(A("jm", 0, 256), [[0, 16], [1, 16]], 0, 0)
-    gfill(A("UWi", 0, 2048), 1)
+    fill(A("UWi", 0, 2048), 1.0)
     fill(A("cH", 0, 256), -0.5)
-    for h in (0, 256):
-        act(A("cV", h, h + 256), A("jrow", 0, 256), Fn.Identity, bias=10.5 * K3, scale=0.0)
-        act(A("cS", h, h + 256), A("jrow", 0, 256), Fn.Identity, bias=2.5 * K3, scale=0.0)
+    fill(A("cV", 0, 512), 10.5 * K3)
+    fill(A("cS", 0, 512), 2.5 * K3)
     gfill(A("XA", 0, O - 1), 0)
     gfill(A("XA", O - 1, O), -512)
     gfill(A("X", 0, O), 0)
-    gfill(A("ac", 0, 16), 0)
     gfill(A("C", 0, O), -1025)
     iota(A("D", 0, O), [[0, O]], -1, 0, False)
     gfill(A("one", 0, 256), 1)
-    gfill(A("cap", 0, 130), 256)
-    gfill(A("F", 0, 1), 0)
+    gfill(A("Sb", 0, 144), 0)
+    gfill(A("cF", 0, 144 * R), 0)
+    gfill(A("fl", 0, 64), 0)
+    gfill(A("inc", 0, 256), 1)
+    act(A("inc", 0, 256), A("inc", 0, 256), Fn.Identity, scale=1.0 / 1024)
+    fill(A("vv", 129, 144), 1024 + 129.125)
+    iota(A("cJb", 0, 129), [[2, 129]], 2050, 0)
+    gfill(A("cJb", 129, 130), -1)
+    iota(A("cJb", 130, 144), [[2, 14]], 2310, 0)
     gfill(A("cJ4", 0, 16 * nv4), -43008)
     gfill(A("cJ4", 16 * nv4, 256), -10240)
     gfill(A("cJ5", 0, 16 * ns5), -10240)
     gfill(A("cJ5", 16 * ns5, 256), -43008)
-    gfill(lane("th", 0, 192, 4), -1)
     ts(col("pt", 0), col("pi", 0), 15, Op.bitwise_and)
     ts(col("pt", 1), col("pi", 0), 112, Op.bitwise_and)
     ts(col("pt", 2), col("pi", 0), 3, Op.bitwise_and)
@@ -221,15 +236,17 @@ def build(T, rank, topo, core):
     cp(A("pc", 1, 3), A("pt", 0, 2))
     ts(col("pc", 3), col("pt", 1), 15.0, Op.add)
     cp(A("pc", 5, 7), A("pt", 2, 4))
-    ts(col("pc", 7), col("pt", 0), 32.0, Op.mult)
+    act(col("pc", 7), col("pc", 1), Fn.Identity, scale=32.0)
     ts(A("WS1", 0, 144), A("jrow", 0, 144), col("pc", 3), Op.is_equal)
-    ts(A("Ip", 0, 128), A("jrow", 0, 128), col("pc", 0), Op.is_equal)
+    ts(Ip, A("jrow", 0, 128), col("pc", 0), Op.is_equal)
     ts(A("BD", 0, 128), A("jg", 0, 128), col("pc", 2), Op.is_equal)
     act(A("p32", 0, 128), A("jrow", 0, 128), Fn.Identity, bias=col("pc", 7), scale=512.0)
-    act(A("sw", 0, 16), A("jrow", 0, 16), Fn.Identity, bias=col("pc", 1), scale=16.0)
+    act(sw, A("jrow", 0, 16), Fn.Identity, bias=col("pc", 1), scale=16.0)
     for n, src, k, v in (("Ih", "Ip", 128, 0.5), ("In", "Ip", 128, -1.0), ("BDv", "BD", 128, -K3), ("BDs", "BD", 128, -K3 / 2),
                          ("BD2", "BD", 128, 2.0), ("WSz", "WS1", 144, -512.0), ("WSv", "WS1", 144, 4096.0),
-                         ("WSs", "WS1", 144, 2048.0)):
+                         ("WSs", "WS1", 144, 2048.0), ("TLn", "TL", 128, -1.0 / 1024)):
+        if n == "TLn":
+            select(A("TL", 0, 128), A("BD", 0, 128), [[1, 128]], Op.is_ge, 0, -1)
         act(A(n, 0, k), A(src, 0, k), Fn.Identity, scale=v)
     ts(A("L16", 0, 16), A("jrow", 0, 16), 0.0, Op.mult, col("pc", 1), Op.add)
     ts(A("pc", 8, 12), A("jrow", 0, 4), col("pc", 5), Op.is_equal)
@@ -237,19 +254,23 @@ def build(T, rank, topo, core):
     for a in range(4):
         ts(A("M0", 160 * a, 160 * a + 160), A("jrow", 0, 160), col("pc", 4), Op.is_equal, col("pc", 8 + a), Op.mult)
         ts(A("M1", 160 * a, 160 * a + 160), A("jrow", 0, 160), col("pc", 4), Op.is_equal, col("pc", 12 + a), Op.mult)
-    select(A("TL", 0, 128), A("BD", 0, 128), [[1, 128]], Op.is_ge, 0, -1)
-    select(A("TU", 0, 128), A("BD", 0, 128), [[-1, 128]], Op.is_gt, 0, 1)
-    select(A("seg8", 0, 64), A("one", 0, 64), [[0, 16], [1, 4]], Op.is_gt, 0, 0)
-    act(A("sv", 0, 16), A("sw", 0, 16), Fn.Identity, bias=256.0)
+    for t in range(R):
+        r0 = ST * (t + 1) % 16
+        ts(A("fb", 16 * t, 16 * t + 16), sw, float(Y0 - O - S * t), Op.add)
+        act(col("cF", 144 * t), col("pc", 1), Fn.Relu, bias=8192.0 * r0, scale=-8192.0)
+        act(col("cF", 144 * t + 128), col("pc", 1), Fn.Relu, bias=8192.0 * (1 - r0), scale=8192.0)
+    for h in range(0, W, 512):
+        act(A("XF", O + h, O + h + 512), A("X", O + h, O + h + 512), Fn.Identity, scale=16.0)
     select(A("segn", 0, 256), A("X", 0, 256), [[0, 16], [1, 16]], Op.not_equal, 0, 0, -60000.0)
     ts(A("mk", 0, 256), A("jm", 0, 256), col("pc", 1), Op.not_equal, -48976.0, Op.mult)
     ts(A("Wh", 0, 144), A("WS1", 0, 144), 0.0625, Op.mult)
-    iota(A("CO", 0, 2048), [[61, 16], [0, 128]], 7, 0)
-    select(A("KI", 0, 2048), A("CO", 0, 2048), [[0, 16], [1, 128]], Op.is_equal, 0, -1)
-    select(A("KI", 2048, 2176), A("one", 0, 128), [[1, 128]], Op.is_equal, 0, -1)
-    select(A("UW", 0, 2048), A("UWi", 0, 2048), [[1, 16], [16, 8], [0, 16]], Op.is_equal, 0, -1)
+    select(If, Ip, [[0, 128]], Op.is_ge, 0, 0)
+    for h in range(0, W, 512):
+        iota(A("CO", h, h + 512), [[61, 4], [0, 128]], 7 + 61 * (h // 128), 0)
+        select(A("KI", h, h + 512), A("CO", h, h + 512), [[0, 4], [1, 128]], Op.is_equal, 0, -1)
+        select(A("UW", h, h + 512), A("UWi", h, h + 512), [[1, 4], [16, 8], [0, 16]], Op.is_equal, h // 128, -1)
     for t in range(R - 1):
-        act(lane("cc", 64 * t, 64 * t + 64, 4), A("sw", 0, 16), Fn.Identity, bias=float(W + S * t))
+        act(lane("cc", 64 * t, 64 * t + 64, 4), sw, Fn.Identity, bias=float(W + S * t))
     cp(A("cdh", 0, 128), A("cdi", 0, 128))
     ts(A("cdf", 0, 128), A("cdi", 0, 128), -1024.0, Op.add)
     for r in range(16):
@@ -257,19 +278,18 @@ def build(T, rank, topo, core):
     turn("p6", "cdh", 128, "M0", 1)
     cp(A("ta", 0, 128), A("p6", 0, 128))
     turn("p6", "ta", 128, "M1", 4)
-    ts(A("cdm", 0, 128), A("p6", 0, 128), 0.0, Op.is_lt)
-    tt(A("cdn", 0, 128), A("p6", 0, 128), A("cdm", 0, 128), Op.subtract)
+    ts(A("lc", 0, 128), A("p6", 0, 128), float(O), Op.add)
+    ts(A("cdm", 0, 128), A("p6", 0, 128), 0.0, Op.is_lt, 32768.0, Op.mult)
 
     def ages():
         ts(A("tc", 0, 48), A("agi", 0, 48), -1024.0, Op.add)
-        turn("p0", "tc", 48, "M0", 1)
-        cp(A("tb", 0, 48), A("p0", 0, 48))
-        turn("p0", "tb", 48, "M1", 4)
+        turn("p1", "tc", 48, "M0", 1)
+        cp(A("tb", 0, 48), A("p1", 0, 48))
+        turn("p1", "tb", 48, "M1", 4)
         for t in range(R - 1):
-            act(A("thw", 16 * t, 16 * t + 16), A("p0", 16 * t, 16 * t + 16), Fn.Identity,
-                bias=float(W + S * t + S - 1 - 1024), scale=-1.0)
-        for k in range(1, 4):
-            act(lane("th", k, 192, 4), A("thw", 0, 48), Fn.Identity)
+            oldest = W + S * t + S - 1 - 1024
+            for n, less in (("th1", S * t), ("th2", 1024)):
+                act(A(n, 16 * t, 16 * t + 16), A("p1", 16 * t, 16 * t + 16), Fn.Identity, bias=float(oldest - less), scale=-1.0)
 
     def who(t):
         lo = S * t
@@ -280,27 +300,9 @@ def build(T, rank, topo, core):
             ts(A("wj", a, b), A("wi", a, b), 5, Op.arith_shift_right, S - 1, Op.bitwise_and)
             cp(A("who", a, b), A("wj", a, b))
 
-    def parent_list(t, src):
-        c0, r0 = divmod(ST * (t + 1), 16)
-        free = float(O - 2 if t == 0 else O - 1)
-        act(col("kp", 0), col("pc", 1), Fn.Sign, bias=0.5 - r0)
-        act(col("kp", 1), col("kp", 0), Fn.Relu)
-        act(col("kp", 2), col("kp", 0), Fn.Relu, scale=-1.0)
-        up = float(O if t == 0 else O + 1024)
-        act(A("lf", 1, 128 - c0), A(src, c0 + 1, 128), Fn.Identity, bias=up)
-        act(A("lf", 128 - c0, 128), A(src, 0, c0), Fn.Identity, bias=up)
-        act(col("kp", 3), col(src, c0), Fn.Identity, bias=up - free)
-        act(col("lf", 0), col("kp", 3), Fn.Identity, bias=free, scale=col("kp", 1))
-        act(col("lf", 128), col("kp", 3), Fn.Identity, bias=free, scale=col("kp", 2))
-        cp(A("lc", 0, 129), A("lf", 0, 129))
-
-    pieces = [("V", 0, 32, "p0"), ("S", 32, 32, "p4"), ("V", 64, dv - 32, "p1"), ("S", dv + 32, 32, "p5"),
-              ("S", dv + 64, 64 - dv, "p6")]
-
     def pre_terms(t):
         lo = S * t
-        mm(A("p3", 0, 256), A("Ih", 0, 128), A("CM", lo, lo + S), True, False)
-        mm(A("p3", 0, 256), A("Ih", 0, 128), A("cH", 0, 256), False, t == 0)
+        mms([(A("p3", 0, 256), Ih, A("CM", lo, lo + S), True, False), (A("p3", 0, 256), Ih, A("cH", 0, 256), False, t == 0)])
 
     def judge_parts(E, off, yy, win, cj):
         flip = [0]
@@ -318,48 +320,35 @@ def build(T, rank, topo, core):
                     flip[0] = (flip[0] + 1) % 3
                     act(A("Gd", h, h + 256 * n), IND(win, A(off, 16 * k, 16 * (k + n))), Fn.Identity)
                     chain("S")
-                    mm(A(pb, 0, 256 * n), A("Ip", 0, 128), A("Gd", h, h + 256 * n), True, False)
-                    for i in range(n):
-                        mm(A(pb, 256 * i, 256 * i + 256), A("In", 0, 128), yy, False, i == n - 1)
+                    mms([(A(pb, 0, 256 * n), Ip, A("Gd", h, h + 256 * n), True, False)] +
+                        [(A(pb, 256 * i, 256 * i + 256), In, yy, False, i == n - 1) for i in range(n)])
                 if todo is not None:
                     act(A(E, 256 * todo[0], 256 * (todo[0] + todo[1])), A(todo[2], 0, 256 * todo[1]), Fn.Sign, bias=0.5)
                     chain("S")
                 todo = None if k is None else (k, n, pb)
 
         def const(bank, k0, k1):
-            mm(A(bank, 16 * k0, 16 * k1), A("Ip", 0, 128), A(cj, 16 * k0, 16 * k1), True, False)
+            mm(A(bank, 16 * k0, 16 * k1), Ip, A(cj, 16 * k0, 16 * k1), True, False)
 
         def count(bank, k0, k1, m, stop=False):
             wrap(A(bank, 16 * k0, 16 * k1), m, lambda r: A(E, 256 * k0 + r, 256 * k1, 16), False, stop)
 
         return vrow, srows, const, count
 
-    def spread(m, j, lo, bank, out):
-        if m is not None:
-            ts(A("mc", 16 * j, 16 * j + 16), A(m, 0, 16), float(-lo - 1), Op.max)
-        for r in range(16):
-            mm(A(bank, r, 256, 16), A("UW", 128 * r, 128 * r + 128), A("mc", 16 * j, 16 * j + 16), True, True)
-        act(out, A(bank, 0, 256), Fn.Identity, bias=float(lo if lo == S * (R - 1) else lo - 1024))
-
     def tree(v, bank, c, k0, k1, tmp, at, out):
-        steps = [lambda: tt(A(v, 16 * k0, 16 * k1), A(bank, 16 * k0, 16 * k1), A(c, 16 * k0, 16 * k1), Op.min)]
+        tt(A(v, 16 * k0, 16 * k1), A(bank, 16 * k0, 16 * k1), A(c, 16 * k0, 16 * k1), Op.min)
         src, a, n = v, 16 * k0, k1 - k0
         top = A(src, a, a + 16)
         while n > 1:
             h = (n + 1) // 2
             top = out if h == 1 and out is not None else A(tmp, at, at + 16 * h)
-            steps.append(lambda o=top, x=A(src, a, a + 16 * h), z=A(src, a + 16 * (n - h), a + 16 * n): tt(o, x, z, Op.max))
+            tt(top, A(src, a, a + 16 * h), A(src, a + 16 * (n - h), a + 16 * n), Op.max)
             src, a, n, at = tmp, at, h, at + 16 * h
-        return steps, top
+        return top
 
     def chunks(a, b):
         cut = list(range(a, max(b - 3, a + 1), 4)) + [b]
         return list(zip(cut, cut[1:]))
-
-    peers = [(rank + k) % N for k in range(1, N)]
-
-    parent_list(0, "cdn")
-    pre_terms(0)
 
     def places(t):
         cp(A("hi", 0, 16), A("uq", 0, 16))
@@ -369,106 +358,107 @@ def build(T, rank, topo, core):
             tt(A("T1", 0, 256), IND(A("ua", 0, 16), A("L16", 0, 16)), A("Kc", 0, 256), Op.mult)
             tt(A("T2", 0, 256), IND(A("hA", 0, 16), A("L16", 0, 16)), A("T1", 0, 256), Op.add)
         else:
-            ts(A("tq", 336, 352), A("hj", 0, 16), col("ac", 0), Op.add, -2048.0, Op.add)
-            for m in range(16):
-                mm(A("p7", 16 * m, 16 * m + 16), A("KI", 128 * m, 128 * m + 128), A("tq", 320, 336), True, False)
-                mm(A("p7", 16 * m, 16 * m + 16), A("KI", 2048, 2176), A("tq", 336, 352), False, True)
+            ts(A("uh", 16, 32), A("hj", 0, 16), col("ac", 0), Op.add, -2048.0, Op.add)
+            mms([c for m in range(16) for c in (
+                (A("p7", 16 * m, 16 * m + 16), A("KI", 128 * m, 128 * m + 128), A("uh", 0, 16), True, False),
+                (A("p7", 16 * m, 16 * m + 16), If, A("uh", 16, 32), False, True))])
             ts(A("T2", 0, 256), A("p7", 0, 256), 4194304.0, Op.add)
         ts(A("c4", 0, 256), A("T2", 0, 256), W - 1, Op.bitwise_and)
         ts(A("o4", 0, 256), A("c4", 0, 256), 16.0, Op.add)
 
+    peers = sorted([(rank + k) % N for k in range(1, N)],
+                   key=lambda b: topo.same_plane(topo.chip(core), topo.chip(T.cores[b])))
+    counts = ("p0", "p1", "p4", "p5")
+    pre_terms(0)
+
     for t in range(R):
         lo, B = S * t, W + S * t
         last = t == R - 1
-        c0, r0 = divmod(ST * (t + 1), 16)
+        c0 = ST * (t + 1) // 16
         xa = A("X", O + B, O + B + S)
         if t > 0:
             z0 = S * (t - 1)
-            for i, b in enumerate([rank] + peers):
-                src = A("zs" if b == rank else "Z", z0 + 64 * b, z0 + 64 * b + 64)
-                mm(A("p3", 64 * b, 64 * b + 64), A("Ih", 0, 128), src, False, i == N - 1, arr=t - 1 if i == 1 else None)
+            mm(A("p3", 64 * rank, 64 * rank + 64), Ih, A("zs", z0 + 64 * rank, z0 + 64 * rank + 64), False, False)
+            mms([(A("p3", 64 * b, 64 * b + 64), Ih, A("Z", z0 + 64 * b, z0 + 64 * b + 64), False, b == peers[-1]) for b in peers])
+            ops[-1]["arr"] = t - 1
         ts(xa, A("p3", 0, 256), MAGIC, Op.add, MAGIC, Op.subtract)
+        if t == 0:
+            who(0)
         wrap(A("p7", 0, 16), "WS1", lambda r: A("X", O + B + r, O + B + S, 16))
         act(A("uq", 0, 16), A("p7", 0, 16), Fn.Square)
         if t > 0:
-            ts(A("tq", 320, 336), A("p7", 0, 16), -2048.0, Op.add)
+            ts(A("uh", 0, 16), A("p7", 0, 16), -2048.0, Op.add)
         else:
             act(A("ua", 0, 16), A("p7", 0, 16), Fn.Identity)
-            places(0)
-            who(0)
-        for i, (e, k, n, bank) in enumerate(pieces):
-            a, m = O + lo + 16 * k, 16 * n
-            ed, got = A("Ed", 16 * k, 16 * k + m), IND(xa, A("who", k, k + n))
-            mm(A(bank, 0, m), A("Ip", 0, 128), A("cV" if e == "V" else "cS", 0, m), True, False)
-            known = min(m, O + B - S - a)
-            if t > 0 and known > 0:
-                mm(A(bank, 0, known), A("BD2", 0, 128), A("XA", a, a + known), False, False)
+        diffs = ["p2", "p3"]
+        for i, e in enumerate(CFG["own"]):
+            a, bank = O + lo + 512 * i, counts[i]
+            ed, got, old = A("Ed", 512 * i, 512 * i + 512), IND(xa, A("who", 32 * i, 32 * i + 32)), A("X", a, a + 512)
+            known = min(512, O + B - S - a)
+            mms([(A(bank, 0, 512), Ip, A("cV" if e == "V" else "cS", 0, 512), True, False)] +
+                ([(A(bank, 0, known), A("BD2", 0, 128), A("XA", a, a + known), False, False)] if t > 0 else []))
             if e == "V":
-                tt(ed, got, A("X", a, a + m), Op.is_ge)
+                tt(ed, got, old, Op.is_ge)
             else:
-                h, pb = (512, "p3") if i == 3 else (0, "p2")
-                act(A("Gd", h, h + m), got, Fn.Identity)
-                mm(A(pb, 0, m), A("In", 0, 128), A("X", a, a + m), True, False)
-                mm(A(pb, 0, m), A("Ip", 0, 128), A("Gd", h, h + m), False, True)
-                act(ed, A(pb, 0, m), Fn.Sign, bias=0.5)
-            mm(A(bank, 0, m), A("BDv" if e == "V" else "BDs", 0, 128), ed, False, True)
-            tt(A("XA", a, a + m), A(bank, 0, m), A("X", a, a + m), Op.min)
-        if t > 0:
-            places(t)
-        ov = CFG["ov"] if t > 0 else 62
+                pb = diffs.pop(0)
+                diffs.append(pb)
+                gd = A("Gd", 0, 512) if pb == "p2" else A("Gd", 512, 1024)
+                act(gd, got, Fn.Identity)
+                mm(A(pb, 0, 512), In, old, True, False)
+                mm(A(pb, 0, 512), Ip, gd, False, True)
+                act(ed, A(pb, 0, 512), Fn.Sign, bias=0.5)
+            mm(A(bank, 0, 512), A("BDv" if e == "V" else "BDs", 0, 128), ed, False, True)
+            tt(A("XA", a, a + 512), A(bank, 0, 512), old, Op.min)
+        places(t)
         wall = A("XA", 0, O + B)
         win = A("XA", lo + O - 16, O + B)
-        cut = 128 - ov
-        ts(A("Og", 16 * cut, 2064), IND(wall, A("lc", cut, 129)), 0.0, Op.min, -1.0, Op.max)
-        if CFG["pin2"]:
-            ops[-1]["r"] += [("T2", 0, 256) if CFG["pin2"] == 1 else ("o4", 0, 256)]
-        mid = min(CFG["mid"], cut - 2)
-        act(A("Og", 0, 16 * mid), IND(wall, A("lc", 0, mid)), Fn.Sign, bias=0.5)
-        chain("S")
-        act(A("Og", 16 * mid, 16 * cut), IND(wall, A("lc", mid, cut)), Fn.Sign, bias=0.5)
-        chain("S")
-        mm(A("p6", 0, 129), A("Ip", 0, 128), A("cH", 0, 129), True, False)
-        wrap(A("p6", 0, 128 - c0), "WS1", lambda r: A("XA", O + lo + 16 * c0 + r, O + B, 16), False, False)
-        wrap(A("p6", 128 - c0, 129), "WS1", lambda r: A("XA", O + lo + r, O + lo + 16 * c0 + 16, 16), False, False)
-        wrap(A("p6", 0, mid), "WSz", lambda r: A("Og", r, 16 * mid, 16), False, False)
-        wrap(A("p6", mid, 129), "WSz", lambda r: A("Og", 16 * mid + r, 2064, 16), False, True)
-        ts(A("F", 1, 130), A("p6", 0, 129), 6000.0, Op.is_ge)
-        mm(A("p6", 0, 129), A("BD", 0, 128), A("F", 1, 130), True, True)
-        mm(A("p7", 0, 129), A("TL", 0, 128), A("F", 1, 130), True, False)
-        mm(A("p7", 0, 129), A("TU", 0, 128), A("F", 0, 129), False, True)
-        scan(A("Sb", 0, 129), A("p6", 0, 129), A("cap", 0, 129), Op.add, Op.min)
-        wrap(A("p6", 0, 8), "WS1", lambda r: A("Sb", r, 128, 16))
-        scan(A("cum", 0, 129), A("one", 0, 129), A("p7", 0, 129), Op.mult, Op.add)
+        for i, e in enumerate(CFG["og"]):
+            got = IND(A("XA", 0, O + lo + 512 * i + 512), A("lc", 32 * i, 32 * i + 32))
+            if e == "V":
+                ts(A("Og", 512 * i, 512 * i + 512), got, 0.0, Op.min, -1.0, Op.max)
+            else:
+                act(A("Og", 512 * i, 512 * i + 512), got, Fn.Sign, bias=0.5)
+
+        def cyclic(a, b):
+            return A("p6", a - c0, b - c0) if a >= c0 else A("p6", a + 128 - c0, b + 128 - c0)
+        mm(A("p6", 0, 129), In, A("cF", 144 * t, 144 * t + 129), True, False)
+        if t == 0:
+            mms([(cyclic(a, b), In, A("cdm", a, b), False, False) for a, b in ((0, c0 + 1), (c0, 128))])
+        for a, b in ((0, c0 + 1), (c0, 128)):
+            wrap(cyclic(a, b), "WS1", lambda r: A("XA", O + lo + 16 * a + r, O + lo + 16 * b, 16), False, False)
+        for a, b in [(0, c0 + 1)] + ([(c0, 64), (64, 128)] if c0 < 32 else [(c0, 128)]):
+            wrap(cyclic(a, b), "WSz", lambda r: A("Og", 16 * a + r, 16 * b, 16), False, b == 128)
+        F = A("F", 0, 129)
+        ts(F, A("p6", 0, 129), 6000.0, Op.is_ge)
+        gfill(A("Tw", 0, S), 0)
+        mms([(A("p6", 0, 129), A("BD", 0, 128), F, True, True), (A("p6", 144, 288), If, A("cJb", 0, 144), True, False),
+             (A("p6", 144, 273), A("BDv", 0, 128), F, False, True)])
+        mms([(A("p7", 0, 129), Ip, A("s1", 0, 129), True, False), (A("p7", 0, 129), A("TLn", 0, 128), F, False, True)])
+        scan(A("Sb", 1, 130), A("p6", 0, 129), A("one", 0, 129), Op.add, Op.mult)
+        tt(A("off", 0, 144), A("p6", 144, 288), A("Sb", 0, 144), Op.max)
+        act(A("vv", 0, 129), A("p7", 0, 129), Fn.Identity, bias=1024.5 + 0.5 / 1024)
+        wrap(A("p6", 0, 9), "Wh", lambda r: A("off", r, 144, 16))
+        cp(A("lb", 0, 9), A("p6", 0, 9))
+        cp(SCT(A("Tw", 0, 2352), A("lb", 0, 9)), A("vv", 0, 144))
+        scan(A("E3", 0, 256), A("inc", 0, 256), A("Tw", 0, 256), Op.add, Op.max)
         base = float(O + lo + 16 * c0)
-        ts(A("Ub", 0, 16), A("sw", 0, 16), col("Sb", 128), Op.is_ge, -(base + 16.0), Op.mult)
-        ts(A("Ub", 16, 32), A("sw", 0, 16), col("Sb", 127 - c0), Op.is_ge, -2048.0, Op.mult)
-        act(col("U", 0), col("Sb", 128), Fn.Identity, scale=-1.0)
-        act(A("Ub", 32, 48), A("sw", 0, 16), Fn.Relu, bias=col("U", 0))
-        for h in range(2):
-            for b in range(4):
-                ts(view(T.IB[:, 64 * h + b:64 * h + 64:4, :], "IB", 1024 * h, 1024 * h + 1024, 256, b), s16,
-                   col("p6", 4 * h + b), Op.is_ge)
-                chain("IB")
-            wrap(A("p7", 0, 64), "WS1", lambda r: view(T.IB[:, 64 * h:64 * h + 64, r], "IB", 1024 * h, 1024 * h + 1024, 64),
-                 h == 0, h == 1)
-        scan(A("bs", 0, 64), A("seg8", 0, 64), A("p7", 0, 64), Op.mult, Op.add)
-        cp(A("lb", 0, 16), A("bs", 3, 64, 4))
-        tt(A("E3", 0, 256), IND(A("cum", 0, 129), A("lb", 0, 16)), A("s1", 0, 256), Op.is_le)
-        act(A("Ub", 48, 64), A("bs", 3, 64, 4), Fn.Identity, scale=16.0)
-        for i in range(4):
-            mm(A("p6", 0, 16), A("Ip", 0, 128), A("Ub", 16 * i, 16 * i + 16), i == 0, False)
-        wrap(A("p6", 0, 16), "WS1", lambda r: A("E3", r, 256, 16), False, True)
-        ts(A("lo1", 0, 16), A("p6", 0, 16), base, Op.add)
-        act(A("ou", 0, 16), A("p6", 0, 16), Fn.Identity, bias=base)
-        ts(A("dg", 0, 256), IND(A("D", 0, O + B), A("lo1", 0, 16)), float(-lo), Op.add, -1.0, Op.max)
-        act(A("y", 0, 256), IND(A("X", 0, O + B), A("lo1", 0, 16)), Fn.Identity)
+        ts(A("Ub", 0, 16), sw, col("Sb", 129), Op.is_ge, -(base + 16.0) / 16, Op.mult)
+        ts(A("Ub", 16, 32), sw, col("Sb", 128 - c0), Op.is_ge, -128.0, Op.mult)
+        act(col("U", 0), col("Sb", 129), Fn.Identity, scale=-1.0 / 16)
+        act(A("Ub", 32, 48), sw, Fn.Relu, bias=col("U", 0), scale=1.0 / 16)
+        mms([(A("p6", 0, 16), Ip, A("Ub", 16 * i, 16 * i + 16), i == 0, False) for i in range(3)])
+        wrap(A("p6", 0, 16), "Wh", lambda r: A("E3", r, 256, 16), False, True)
+        slots = A("lo1", 0, 16)
+        ts(slots, A("p6", 0, 16), 16.0, Op.mult, base - 16384.0, Op.add)
+        ts(A("dg", 0, 256), IND(A("D", 0, O + B), slots), float(-lo), Op.add, -1.0, Op.max)
+        yy = A("X", Y0, Y0 + S)
+        act(yy, IND(wall, slots), Fn.Identity)
         turn("p7", "dg", 256, "M0", 1)
         cp(A("ta", 0, 256), A("p7", 0, 256))
-        turn(lambda a: ("p6" if a < 2 else "p7", 64 * a), "ta", 256, "M1", 4)
-        ts(A("o5", 0, 128), A("p6", 0, 128), 16.0, Op.add)
-        ts(A("o5", 128, 256), A("p7", 128, 256), 16.0, Op.add)
-        act(A("c5", 0, 128), A("p6", 0, 128), Fn.Identity)
-        act(A("c5", 128, 256), A("p7", 128, 256), Fn.Identity)
+        for bank, h in (("p6", 0), ("p7", 128)):
+            turn(bank, "ta", 256, "M1", 4, range(h // 64, h // 64 + 2))
+            ts(A("o5", h, h + 128), A(bank, h, h + 128), 16.0, Op.add)
+            act(A("c5", h, h + 128), A(bank, h, h + 128), Fn.Identity)
         vrow, srows, const, count = judge_parts("E4", "o4", xa, win, "cJ4")
         const("p4", 0, 16)
         for k in range(nv4):
@@ -477,74 +467,57 @@ def build(T, rank, topo, core):
         cs = sorted(chunks(0, nv4) + chunks(nv4, 16), key=lambda x: CFG["v4"] * x[1] / nv4 if x[0] < nv4 else (x[1] - nv4) / ns4)
         for k0, k1 in cs:
             count("p4", k0, k1, "WSv" if k0 < nv4 else "WSs", (k0, k1) == cs[-1])
-        steps4, _ = tree("v4", "p4", "c4", 0, 16, "tr", 0, A("m4", 0, 16))
-        yy = A("y", 0, 256)
-        vrow, srows, const, count = judge_parts("E5", "o5", yy, win, "cJ5")
-        const("p5", 0, early)
-        const("p1", early, 16)
-        if CFG["at4"] < 0:
-            while steps4:
-                steps4.pop(0)()
-        for k in range(ns5, early):
-            vrow(k)
-            if k - ns5 >= CFG["at4"] and steps4:
-                steps4.pop(0)()
-                chain("V")
-        for step in steps4:
-            step()
-        spread("m4", 0, lo, "p4", A("CO" if last else "C", O + B, O + B + S))
+        m4 = tree("v4", "p4", "c4", 0, 16, "tr", 0, A("m4", 0, 16))
+        ts(A("mc", 0, 16), m4, float(-lo - 1), Op.max)
+        unwrap("p4", A("mc", 0, 16))
+        act(A("CO" if last else "C", O + B, O + B + S), A("p4", 0, 256), Fn.Identity, bias=float(lo if last else lo - 1024))
         if t == 0:
             ages()
         if not last:
+            act(A("XF", O + B, O + B + S), xa, Fn.Identity, scale=16.0)
             ts(A("lh", 0, 16), A("mc", 0, 16), float(lo + O), Op.add)
-            act(lane("cc", 64 * t + 1, 64 * t + 64, 4), A("m4", 0, 16), Fn.Identity, bias=float(lo))
+            act(lane("cc", 64 * t + 1, 64 * t + 64, 4), m4, Fn.Identity, bias=float(lo))
+            tt(lane("fl", 1, 64, 4), m4, A("th1", 16 * t, 16 * t + 16), Op.is_lt)
+        vrow, srows, const, count = judge_parts("E5", "o5", yy, win, "cJ5")
+        const("p5", 0, early)
+        const("p1", early, 16)
+        for k in range(ns5, 16):
+            vrow(k)
         srows(0, ns5)
         cs = sorted(chunks(0, ns5) + chunks(ns5, early), key=lambda x: x[1] / ns5 if x[0] < ns5 else (x[1] - ns5) / (16 - ns5))
         for k0, k1 in cs:
             count("p5", k0, k1, "WSs" if k0 < ns5 else "WSv", (k0, k1) == cs[-1])
-        steps5, top = tree("v5", "p5", "c5", 0, early, "tq", 0, None)
-        steps5.append(lambda: ts(A("tq", 240, 256), top, float(-lo - 1), Op.max))
-        for k in range(early, 16):
-            vrow(k)
-            if k >= early + CFG["at5"]:
-                steps5.pop(0)()
-                chain("V")
+        top = tree("v5", "p5", "c5", 0, early, "tq", 0, None)
+        tt(A("tq", 240, 256), top, A("fb", 16 * t, 16 * t + 16), Op.max)
         count("p1", early, 16, "WSv", True)
-        for step in steps5:
-            step()
-        steps5, top = tree("v5", "p1", "c5", early, 16, "tq", 256, None)
-        for step in steps5:
-            step()
+        top = tree("v5", "p1", "c5", early, 16, "tq", 256, None)
         tt(A("mc", 16, 32), A("tq", 240, 256), top, Op.max)
-        ts(A("lx", 0, 16), A("mc", 16, 32), 16.0, Op.add)
-        spread(None, 1, lo, "p6", A("cn", 0, 256))
-        mm(A("p7", 0, 256), A("Ih", 0, 128), yy, True, False)
-        mm(A("p7", 0, 256), A("Ih", 0, 128), A("cH", 0, 256), False, False)
-        act(A("xb", 0, 256), IND(win, A("lx", 0, 16)), Fn.Identity)
-        mm(A("p7", 0, 256), A("Ih", 0, 128), A("xb", 0, 256), False, True)
-        ts(A("U", 16, 32), A("mc", 16, 32), 0.0, Op.min, 8192.0, Op.mult)
-        tt(A("U", 32, 48), A("ou", 0, 16), A("U", 16, 32), Op.add)
-        tt(A("U", 48, 64), A("U", 32, 48), A("sv", 0, 16), Op.max)
-        cp(A("lo2", 0, 16), A("U", 48, 64))
+        ts(A("lx", 0, 16), A("mc", 16, 32), float(lo + O - Y0), Op.add)
+        xb = IND(A("X", Y0, O + B), A("lx", 0, 16))
+        unwrap("p6", A("mc", 16, 32))
         if last:
-            ts(A("av", 0, 256), A("p7", 0, 256), MAGIC, Op.add, MAGIC, Op.subtract)
-        else:
-            act(A("aw", 0, 256), A("p7", 0, 256), Fn.Identity, bias=MAGIC)
-            act(A("av", 0, 256), A("aw", 0, 256), Fn.Identity, bias=-MAGIC)
-        if last:
-            for r in range(16):
-                mm(A("p0", 0, 128), ws("WS1", r), A("XA", O + lo + 128 * r, O + lo + 128 * r + 128), r == 0, r == 15)
+            select(A("xb", 0, 256), yy, [[0, 256]], Op.is_ge, 0, 0)
+            tt(A("sm", 0, 256), xb, A("xb", 0, 256), Op.add)
+            ts(A("avi", 0, 256), A("sm", 0, 256), 0.5, Op.mult, -0.25, Op.add)
+            ts(A("cn", 0, 256), A("p6", 0, 256), float(lo), Op.add, -1.0, Op.max)
+            wrap(A("p0", 0, 128), "WS1", lambda r: A("XA", O + lo + 128 * r, O + lo + 128 * r + 128))
             ts(A("cdf", 0, 128), A("p0", 0, 128), 0.0, Op.is_ge)
             dma("Y", ext(T.ya[:, 0:W]), A("cdf", 0, 128), "dya", 64)
             dma("Y", ext(T.ya[:, W:W + S]), view(T.one[0:8, 0:256], "one", 0, 256, 256), "dyo", 8)
             dma("Y", ext(T.yx[:, W:W + S]), xa, "dyy", 64)
-            cp(SCT(A("X", 0, O + B), A("lo2", 0, 16)), A("av", 0, 256))
+            cp(SCT(A("X", 0, O + B), slots), A("avi", 0, 256))
             dma("Y", ext(T.yx[:, 0:W]), A("X", O + lo, O + B), "dyx", 512)
-            cp(SCT(A("CO", 0, O + B), A("lo1", 0, 16)), A("cn", 0, 256))
+            cp(SCT(A("CO", 0, O + B), slots), A("cn", 0, 256))
             dma("S", ext(T.yc[:]), view(T.CO[0:128:16, O + lo:PW], "CO", O + lo, PW, W + S), "dyc", 72)
             break
-        cp(SCT(A("C", 0, O + B), A("lo1", 0, 16)), A("cn", 0, 256))
-        cp(SCT(A("X", 0, O + B), A("lo2", 0, 16)), A("av", 0, 256))
+        ts(A("cn", 0, 256), A("p6", 0, 256), float(lo - 1024), Op.add, -1025.0, Op.max)
+        cp(SCT(A("C", 0, O + B), slots), A("cn", 0, 256))
+        mms([(A("p7", 0, 256), Ih, yy, True, False), (A("p7", 0, 256), Ih, A("cH", 0, 256), False, False)])
+        act(A("xb", 0, 256), xb, Fn.Identity)
+        mm(A("p7", 0, 256), Ih, A("xb", 0, 256), False, True)
+        act(A("aw", 0, 256), A("p7", 0, 256), Fn.Identity, bias=MAGIC)
+        act(A("ax", 0, 256), A("aw", 0, 256), Fn.Identity, bias=-16 * MAGIC, scale=16.0)
+        act(SCT(A("XF", 0, O + B), slots), A("ax", 0, 256), Fn.Silu)
         cw = A("C", 0, O + B + S)
         for h in range(2):
             hg, sc = A("hg", 256 * h, 256 * h + 256), A("sc", 256 * h, 256 * h + 256)
@@ -554,58 +527,64 @@ def build(T, rank, topo, core):
             if h == 0:
                 ts(A("lh", 16, 32), ends, float(O + 1024), Op.add)
             ts(lane("cc", 64 * t + 2 + h, 64 * t + 64, 4), ends, 1024.0, Op.add)
-        cc = A("cc", 64 * t, 64 * t + 64)
-        tt(A("fl", 0, 64), cc, A("th", 64 * t, 64 * t + 64), Op.is_lt)
-        scan(A("wq", 0, 64), A("fl", 0, 64), cc, Op.mult, Op.max)
-        ts(A("lw", 0, 16), A("wq", 3, 64, 4), float(O), Op.add)
-        cp(A("zs", lo, lo + S), IND(A("X", 0, O + B + S), A("lw", 0, 16)))
+            tt(lane("fl", 2 + h, 64, 4), ends, A("th2", 16 * t, 16 * t + 16), Op.is_lt)
+        scan(A("wq", 0, 64), A("fl", 0, 64), A("cc", 64 * t, 64 * t + 64), Op.mult, Op.max)
+        ts(A("lw", 0, 16), A("wq", 3, 64, 4), float(-lo), Op.add)
+        ts(A("zs", lo, lo + S), IND(A("XF", O + lo, O + B + S), A("lw", 0, 16)), 0.0625, Op.mult)
 
-        def send(q, t=t):
+        def send(q, to, t=t):
             trs = []
-            free = topo.engines(core, T.cores[peers[0]])
-            for i, b in enumerate(peers):
-                dst = T.cores[b]
-                ok = [e for e in topo.engines(core, dst) if e in free][:4 if i == 0 else 2]
-                free = [e for e in free if e not in ok]
-                rid, pid, _ = topo.addr(dst)
+            free = [e for e in topo.engines(core, T.cores[to[0]]) if all(e in topo.engines(core, T.cores[b]) for b in to)]
+            for i, b in enumerate(to):
+                k = len(free) // 2 if i < len(to) - 1 else len(free)
+                mine, free = free[:k], free[k:]
+                rid, pid, _ = topo.addr(T.cores[b])
                 trs.append(RemoteDMATransfer(
-                    dst_ids=[DstId(rid=rid, pnc=pid)], dma_engine_mask=sum(1 << e for e in ok),
+                    dst_ids=[DstId(rid=rid, pnc=pid)], dma_engine_mask=sum(1 << e for e in mine),
                     remote_sem=T.sem["arr%d" % t], src=T.zs[:, S * t + 64 * b:S * t + 64 * b + 64],
                     dst=T.Z[:, S * t + 64 * rank:S * t + 64 * rank + 64]))
             return q.remote_dma_fused(trs, local_sem=T.sem["snt%d" % t])
-        emit("G", send, ext(None), [A("zs", lo, lo + S)], 500.0)
+        for to in ([peers[:2], peers[2:]] if CFG["calls"] == 2 else [peers]):
+            sent = emit("G", lambda q, to=to, f=send: f(q, to), ext(None), [A("zs", lo, lo + S)], (400, 0, 0))
+            chain("send")
         ops[-1]["send"] = t
+        for h in range(lo + S, B, 512):
+            act(A("X", O + h, O + min(h + 512, B)), A("XF", O + h, O + min(h + 512, B)), Fn.Identity, scale=0.0625)
         who(t + 1)
-        for h in range(0, W, 1024):
-            select(A("Ch", h, h + 1024), A("C", O + lo + S + h, O + lo + S + h + 1024), [[0, 1024]], Op.is_ge, 0, 0)
-            wrap(A("p6", h // 16, h // 16 + 64), "Wh", lambda r: A("Ch", h + r, h + 1024, 16))
-        parent_list(t + 1, "p6")
+        for i in range(4):
+            a = O + lo + S + 512 * i
+            select(A("Ch", 512 * i, 512 * i + 512), A("C", a, a + 512), [[0, 512]], Op.is_ge, 0, 0)
+            if i >= CFG["pre"]:
+                after(sent)
+            if i % 2:
+                wrap(A("p6", 32 * i - 32, 32 * i + 32), "Wh", lambda r: A("Ch", 512 * i - 512 + r, 512 * i + 512, 16))
+        ts(A("lc", 0, 128), A("p6", 0, 128), float(O + 1024), Op.add)
         if t == R - 2:
             for h in range(0, W, 512):
                 a = O + lo + S + h
                 act(A("CO", a, a + 512), A("C", a, a + 512), Fn.Identity, bias=1024.0)
-        act(A("junk", 0, 256), A("XA", O + lo, O + lo + S), Fn.Sign, bias=0.5, acc=col("ac", 2))
-        ops[-1]["r"] += [("E5", 0, 256 * ns5)]
+        act(A("junk", 0, 256), A("XA", O + lo, O + lo + S), Fn.Sign, bias=0.5, acc=col("ac", 1))
         for i in range(2):
             a = S + 896 * i
-            act(A("junk", a, a + 896), A("XA", O + lo + a, O + lo + a + 896), Fn.Sign, bias=0.5, acc=col("ac", 8 + i))
-            ops[-1]["r"] += [("cn", 0, 256)]
-        act(col("ac", 4), col("ac", 8), Fn.Identity, bias=col("ac", 9))
-        act(col("ac", 3), col("ac", 2), Fn.Identity, bias=col("ac", 4))
-        act(col("ac", 0), col("ac", 3), Fn.Identity, bias=1024.0 if t == 0 else col("ac", 5), scale=-0.5)
-        act(col("ac", 5), col("ac", 4), Fn.Identity, bias=128.0, scale=0.5)
+            act(A("junk", a, a + 896), A("XA", O + lo + a, O + lo + a + 896), Fn.Sign, bias=0.5, acc=col("ac", 2 + i))
+        act(col("ac", 4), col("ac", 2), Fn.Identity, bias=col("ac", 3))
+        act(col("ac", 5), col("ac", 1), Fn.Identity, bias=1024.0 if t == 0 else col("ac", 6), scale=-0.5)
+        act(col("ac", 0), col("ac", 4), Fn.Identity, bias=col("ac", 5), scale=-0.5)
+        act(col("ac", 6), col("ac", 4), Fn.Identity, bias=128.0, scale=0.5)
         gfill(A("XA", O + lo, O + lo + S), -512)
+        after(sent)
         if t == 0:
             gfill(A("XA", O - 1, O), 0)
-        back("p0", "v4", "M1", 4)
-        cp(A("tb", 0, 256), A("p0", 0, 256))
-        back("p0", "tb", "M0", 1)
-        ts(A("D", O + B, O + B + S), A("p0", 0, 256), float(lo), Op.add)
-        back("p2", "v5", "M1", 4)
-        cp(A("tc", 0, 256), A("p2", 0, 256))
-        back("p2", "tc", "M0", 1)
-        act(A("dn", 0, 256), A("p2", 0, 256), Fn.Identity, bias=float(lo))
-        cp(SCT(A("D", 0, O + B), A("lo1", 0, 16)), A("dn", 0, 256))
+            after(sent)
+        back("p2", "v4", "M1", 4)
+        cp(A("tb", 0, 256), A("p2", 0, 256))
+        back("p2", "tb", "M0", 1)
+        ts(A("D", O + B, O + B + S), A("p2", 0, 256), float(lo), Op.add)
+        back("p3", "v5", "M1", 4)
+        cp(A("tc", 0, 256), A("p3", 0, 256))
+        back("p3", "tc", "M0", 1)
+        act(A("dn", 0, 256), A("p3", 0, 256), Fn.Identity, bias=float(lo))
+        cp(SCT(A("D", 0, O + B), slots), A("dn", 0, 256))
         pre_terms(t + 1)
     return ops
 
@@ -622,7 +601,7 @@ def hazards(ops):
         o["key"] = o["sem"] if o["sem"] is not None else o["e"]
         follow, wait = set(), set()
         for kind in ("r", "w"):
-            for reg in o[kind]:
+            for reg in set(o[kind]):
                 psum = SCRATCH[reg[0]][0] == "psum"
                 for (j, k2, reg2) in seen.get(reg[0], []):
                     other = ops[j]["key"] != o["key"]
@@ -636,7 +615,7 @@ def hazards(ops):
                         if other or o["sem"] is None:
                             wait.add(j)
         for kind in ("r", "w"):
-            for reg in o[kind]:
+            for reg in set(o[kind]):
                 old = seen.setdefault(reg[0], [])
                 if SCRATCH[reg[0]][0] == "psum" and o["e"] == "P":
                     old[:] = []
@@ -644,39 +623,55 @@ def hazards(ops):
         o["follow"], o["wait"] = follow, wait
 
 
+_ORDER = {}
+
+
 def schedule(ops):
+    if "order" in _ORDER:
+        return [ops[i] for i in _ORDER["order"]]
     hazards(ops)
-    n, wake = len(ops), CFG["wake"]
-    edges = [[] for _ in ops]
+    n = len(ops)
     sends = {o["send"]: i for i, o in enumerate(ops) if "send" in o}
-    dmas = {}
-    mix = CFG["mix"]
+    names, pre = {}, []
     for i, o in enumerate(ops):
-        mix = (mix * 1103515245 + 12345) % 2147483648
-        o["c"] *= 1 + CFG["spread"] * (mix / 2147483648 - 0.5)
-        pre = {j: (ops[j]["lat"] + wake if j in o["wait"] else 0.0) for j in o["follow"]}
+        p = {j: 1 if j in o["wait"] else 0 for j in o["follow"]}
+        for j in o["after"] + [j for j in range(min(i, 7)) if ops[j]["e"] == o["e"]]:
+            p.setdefault(j, 0)
         if o["arr"] is not None:
-            pre[sends[o["arr"]]] = CFG["far"]
+            p[sends[o["arr"]]] = 2
         name = "dma" + o["e"] if o["sem"] is not None else o.get("chain")
         if name is not None:
-            if name in dmas:
-                pre.setdefault(dmas[name], 0.0)
-            dmas[name] = i
-        o["pre"] = pre
-        for j, d in pre.items():
-            edges[j].append((i, d))
-    way = [0.0] * n
-    for i in range(n - 1, -1, -1):
-        way[i] = ops[i]["c"] + max([ops[i]["lat"]] + [d + way[j] for j, d in edges[i]])
-    before = [list(o["pre"].items()) for o in ops]
+            if name in names:
+                p.setdefault(names[name], 0)
+            names[name] = i
+        pre.append(p)
+    lat, zero, eng = [o["lat"] for o in ops], [0.0] * n, [o["e"] for o in ops]
 
-    def place(rank, links, head):
+    def paced(m):
+        unit = (m[0], m[0] * m[1], m[0] * m[2], m[3])
+        cost = [o["c"][0] + o["c"][1] * unit[o["c"][2]] for o in ops]
+        return cost, [[(j, (0.0, lat[j] + m[4], m[5])[k]) for j, k in p.items()] for p in pre]
+    paces = [paced(m) for m in PACE]
+
+    def replay(seq, cost, before):
+        end, free = [0.0] * n, {}
+        for i in seq:
+            at = free.get(eng[i], 0.0)
+            for j, d in before[i]:
+                if end[j] + d > at:
+                    at = end[j] + d
+            end[i] = free[eng[i]] = at + cost[i]
+        return max(end[i] + lat[i] for i in range(n))
+
+    def place(rank, cost, links, head):
         end = [0.0] * n
         busy = {e: ([], []) for e in "VSPGY"}
         for i in sorted(range(n), key=rank):
-            c = ops[i]["c"]
-            at = max([head[i]] + [end[j] + d for j, d in links[i]])
-            starts, ends = busy[ops[i]["e"]]
+            c, at = cost[i], head[i]
+            for j, d in links[i]:
+                if end[j] + d > at:
+                    at = end[j] + d
+            starts, ends = busy[eng[i]]
             a, b = 0, len(ends)
             while a < b:
                 mid = (a + b) // 2
@@ -692,17 +687,51 @@ def schedule(ops):
             end[i] = at + c
         return end
 
-    lat, zero = [o["lat"] for o in ops], [0.0] * n
-    end = place(lambda i: (-way[i], i), before, zero)
-    best = None
-    for _ in range(CFG["turns"]):
-        rev = place(lambda i: (-end[i], -i), edges, lat)
-        end = place(lambda i: (-rev[i], i), before, zero)
-        span = max(end[i] + lat[i] for i in range(n))
-        if best is None or span < best[0]:
-            best = (span, end)
-    end = best[1]
-    return [ops[i] for i in sorted(range(n), key=lambda i: (end[i] - ops[i]["c"], i))]
+    mix, best = CFG["mix"], None
+    for k in range(CFG["tries"]):
+        cost, before = paces[k % len(paces)]
+        edges = [[] for _ in ops]
+        for i in range(n):
+            for j, d in before[i]:
+                edges[j].append((i, d))
+        way = [0.0] * n
+        for i in range(n - 1, -1, -1):
+            mix = (mix * 1103515245 + 12345) % 2147483648
+            way[i] = cost[i] * (1 + CFG["spread"] * (mix / 2147483648 - 0.5)) + max([lat[i]] + [d + way[j] for j, d in edges[i]])
+        end = place(lambda i: (-way[i], i), cost, before, zero)
+        for turn in range(CFG["turns"] + 1):
+            if turn:
+                rev = place(lambda i: (-end[i], -i), cost, edges, lat)
+                end = place(lambda i: (-rev[i], i), cost, before, zero)
+            seq = sorted(range(n), key=lambda i: (end[i] - cost[i], i))
+            score = sum(replay(seq, c, b) / m[0] for (c, b), m in zip(paces, PACE))
+            if best is None or score < best[0]:
+                best = (score, seq, [end[i] - cost[i] for i in range(n)])
+    post = [[] for _ in ops]
+    for i in range(n):
+        for j in pre[i]:
+            post[j].append(i)
+    for k in range(CFG["shakes"]):
+        key = list(best[2])
+        mix = (mix * 1103515245 + 12345) % 2147483648
+        i = (mix >> 8) % n
+        mix = (mix * 1103515245 + 12345) % 2147483648
+        step = CFG["span"] * (mix / 1073741824 - 1)
+        key[i] += step
+        todo = [i]
+        while todo:
+            j = todo.pop()
+            for x in (pre[j] if step < 0 else post[j]):
+                if (key[x] > key[j]) if step < 0 else (key[x] < key[j]):
+                    key[x] = key[j]
+                    todo.append(x)
+        seq = sorted(range(n), key=lambda i: (key[i], i))
+        score = sum(replay(seq, c, b) / m[0] for (c, b), m in zip(paces, PACE))
+        if score <= best[0] + CFG["heat"] * (1 - k / CFG["shakes"]):
+            best = (score, seq, key)
+    _ORDER["order"] = best[1]
+    _ORDER["spans"] = [replay(best[1], c, b) for c, b in paces]
+    return [ops[i] for i in best[1]]
 
 
 def order(ops):
@@ -739,6 +768,7 @@ def rank_program(g, core, T, topo):
     ops = schedule(build(T, rank, topo, core))
     count = order(ops)
     queue = {"V": g.vector, "S": g.scalar, "P": g.tensor, "G": g, "Y": g.sync}
+    landed = 8 * CFG["calls"]
     raised = {}
     for o in ops:
         if o["sem"] is None and o.get("sig"):
@@ -753,7 +783,7 @@ def rank_program(g, core, T, topo):
             else:
                 q.wait_ge(T.sem[p["sem"]], 16 * count[p["sem"]])
         if o["arr"] is not None:
-            q.wait_ge(T.sem["arr%d" % o["arr"]], 8)
+            q.wait_ge(T.sem["arr%d" % o["arr"]], landed)
         ins = o["f"](q)
         if o["sem"] is not None:
             ins.then_inc(T.sem[o["sem"]], 16)
@@ -762,4 +792,4 @@ def rank_program(g, core, T, topo):
     for n in ("dya", "dyo", "dyy", "dyx", "dyc"):
         g.wait_ge(T.sem[n], 16)
     for t in range(R - 1):
-        g.wait_ge(T.sem["snt%d" % t], 8)
+        g.wait_ge(T.sem["snt%d" % t], landed)

@@ -3,43 +3,43 @@ from concourse.mybir import AluOpType as Op, ActivationFunctionType as Fn
 
 W, S, R, ST, N = 2048, 256, 4, 341, 4
 O = 528
-Y0 = 256
+Y0 = 0
 PW = O + W + R * S
 BF, F32, F16, I32, U16 = "bfloat16", "float32", "float16", "int32", "uint16"
 MAGIC = 12582912.0
 K3 = 65536.0
-CFG = {"ns4": 9, "ns5": 5, "late": 3, "own": "VVSS", "og": "SSSV", "v4": 0.9, "calls": 2, "pre": 2,
-       "tries": 12, "turns": 2, "spread": 0.3, "mix": 1, "shakes": 3000, "span": 2000.0, "heat": 100.0}
+CFG = {"rows4": "SSVVSSVVSSVVSSVV", "rows5": "SSVVWWWWSSWWSSWW", "own": "VVSS", "own0": "VSVS", "ov": 24, "ov3": 32, "step": 16, "early": 12,
+       "rows3": "SSVVSSVVSSVVSSSS", "post3": 12, "calls": 2, "pre": 2, "soon": "", "here": "L", "w4": 16, "c5": "S", "tries": 60, "turns": 2, "spread": 0.6, "mix": 1, "shakes": 20000, "span": 2000, "heat": 300.0}
 PACE = [(0.83, 1.56, 3.8, 0.42, 110.0, 4200.0), (1.15, 1.8, 5.0, 0.58, 90.0, 4200.0),
-        (0.88, 1.2, 2.5, 0.44, 190.0, 5500.0), (1.04, 1.5, 3.5, 0.52, 130.0, 3300.0)]
+        (0.88, 1.2, 2.5, 0.44, 190.0, 5500.0), (1.0, 1.5, 3.5, 0.55, 130.0, 2800.0)]
 
 SCRATCH = {}
 
 
 def _sb(name, cols, dtype):
-    SCRATCH[name] = ("sbuf", [128, cols], dtype)
+    SCRATCH[name] = ("sbuf", [128] + (cols if isinstance(cols, list) else [cols]), dtype)
 
 
 for _n, _c, _d in [
-    ("X", PW, BF), ("XA", PW, BF), ("XF", PW, F32), ("C", PW, F32), ("D", PW, I32), ("CM", R * S, BF),
+    ("X", PW + S, BF), ("XA", PW, BF), ("XF", PW, F32), ("C", PW, F32), ("D", PW, I32), ("CM", R * S, BF),
     ("cdi", 128, I32), ("cdf", 128, F32), ("cdh", 128, F16), ("agi", 48, I32), ("cdm", 128, BF),
-    ("jrow", 256, F32), ("pi", 1, I32), ("pt", 4, I32), ("pc", 16, F32), ("jg", 128, F32), ("jm", 256, F32),
-    ("WS1", 144, BF), ("WSv", 144, BF), ("WSs", 144, BF), ("WSz", 144, BF), ("Wh", 144, F16), ("Ch", W, F16), ("CO", PW, F32),
-    ("BD", 128, BF), ("BD2", 128, BF), ("BDv", 128, BF), ("BDs", 128, BF), ("TL", 128, BF), ("TLn", 128, BF), ("Ub", 48, BF),
+    ("jrow", 256, F32), ("pi", 1, I32), ("pt", 4, I32), ("pc", 16, F32), ("XR", 896, BF),
+    ("WS1", 144, BF), ("WSv", 144, BF), ("WSz", 144, BF), ("Wh", 144, F16), ("Ch", W, F16), ("CO", PW, F32),
+    ("BD", 128, BF), ("BD2", 128, BF), ("live", 129, BF), ("I8", 128, BF), ("BDv", 128, BF), ("BDs", 128, BF), ("TL", 128, BF), ("TLn", 128, BF), ("Ub", 48, BF),
     ("Ip", 128, BF), ("In", 128, BF), ("Ih", 128, BF), ("If", 128, F16),
     ("M0", 4 * 160, F16), ("M1", 4 * 160, F16), ("UWi", 2048, BF), ("UW", 2048, F16), ("KI", 2048, F16),
-    ("cV", 512, BF), ("cS", 512, BF), ("cH", 256, BF), ("cJ4", 256, BF), ("cJ5", 256, BF), ("cF", 144 * R, BF),
-    ("one", 256, F32), ("inc", 256, BF), ("cJb", 144, F16), ("vv", 144, F32), ("Tw", 2352, F32), ("off", 144, F16),
-    ("fb", 16 * R, F16), ("segn", 256, F16), ("aw", 256, F32), ("ax", 256, F32), ("mk", 256, F32),
+    ("cV", 512, BF), ("cS", 512, BF), ("cH", 256, BF), ("cJ3", 256, F16), ("cJ4", 256, F16), ("cJ5", 256, F16), ("cF", 2 * R, BF),
+    ("one", 256, F32), ("inc", 256, BF), ("cL", 9, BF), ("vv", 144, F32), ("Tw", 6672, F32), ("far", 9, BF), ("W32", 144, BF),
+    ("segn", 256, F16), ("aw", 256, F32), ("ax", 256, F32), ("mk", 256, F32),
     ("p32", 128, F32), ("Kc", 256, F32), ("s1", 144, BF), ("sw", 16, F32),
     ("L16", 16, U16), ("sq", 128, F32), ("wi", 128, I32), ("wj", 128, I32), ("who", 128, U16), ("lc", 128, U16),
-    ("Ed", W, BF), ("Gd", 1536, BF), ("Og", W, BF), ("E4", 4096, BF), ("E5", 4096, BF), ("junk", W, BF),
-    ("ua", 16, F32), ("uq", 16, F32), ("hi", 16, I32), ("hj", 16, I32), ("hA", 16, F32), ("uh", 32, F16),
-    ("T1", 256, F32), ("T2", 256, I32), ("c4", 256, I32), ("o4", 256, U16), ("c5", 256, F32), ("o5", 256, U16),
-    ("F", 130, BF), ("Sb", 144, F32), ("lb", 16, U16),
-    ("E3", 256, F16), ("U", 1, F32), ("lo1", 16, U16), ("lx", 16, U16), ("sm", 256, F16), ("avi", 256, I32),
+    ("Ed", W, BF), ("Gd", 1536, BF), ("Og", W, BF), ("E4", 4096, BF), ("E5", 4096, BF),
+    ("hi", 32, I32), ("hj", 32, I32), ("uh", 32, F16),
+    ("T1", 256, F32), ("T2", [16, 16], I32), ("c4", 256, I32), ("o4", 256, U16), ("c5", 256, F32), ("o5", 256, U16),
+    ("F", 144, BF), ("Sb", 144, F16), ("lb", 16, U16),
+    ("E3", 256, F16), ("U", 3, F32), ("lo1", 16, U16), ("lx", 16, U16), ("sm", 256, F16), ("avi", 256, I32),
     ("dg", 256, F16), ("ta", 256, F16), ("tb", 256, F16), ("tc", 256, F16),
-    ("v4", 256, F16), ("v5", 256, F16), ("tr", 256, F16), ("tq", 320, F16), ("m4", 16, F32), ("mc", 32, F16),
+    ("v4", [16, 16], F16), ("v50", 272, F16), ("v51", 272, F16), ("v52", 272, F16), ("v53", 272, F16), ("tr", 256, F16), ("tq", 320, F16), ("CMh", 3 * S, BF), ("mc", 32, F16),
     ("cn", 256, F32), ("xb", 256, BF), ("dn", 256, F32),
     ("th1", 48, F32), ("th2", 48, F32), ("cc", 192, F32), ("fl", 64, F32), ("wq", 64, F32),
     ("lh", 32, U16), ("hg", 512, F16), ("sc", 512, F16), ("lw", 16, U16),
@@ -49,7 +49,7 @@ for _n, _c, _d in [
 for _k in range(8):
     SCRATCH["p%d" % _k] = ("psum", [128, 512], F32)
 
-DMA_SEMS = ["dx", "dx2", "dc0", "dcm", "dcd", "dag", "ddl", "drep", "dya", "dyo", "dyx", "dyy", "dyc"]
+DMA_SEMS = ["dx", "dx2", "dc0", "dcm", "dcd", "dag", "ddl", "drep", "dya", "dyo", "dyx", "dyy", "dyc", "dyd"]
 SEMAPHORES = ["eV", "eS", "eP", "eG"] + DMA_SEMS + ["arr0", "arr1", "arr2", "snt0", "snt1", "snt2"]
 
 
@@ -68,6 +68,9 @@ def build(T, rank, topo, core):
 
     def lane(n, a, b, st):
         return view(T[n][:, a:b:st], n, a - a % st, b, (b - a + st - 1) // st, a % st)
+
+    def block(n, k0, k1, j0, j1):
+        return view(T[n][:, k0:k1, j0:j1], n, 16 * k0, 16 * k1, (k1 - k0) * (j1 - j0), None if j1 - j0 == 16 else j0)
 
     def ext(a):
         return {"ap": a, "regs": [], "rd": [], "n": 0, "two": False, "ps": False, "ind": False}
@@ -136,7 +139,8 @@ def build(T, rank, topo, core):
         def run(q):
             return [q.matmul(ap(o), ap(l), ap(r), a, z) for o, l, r, a, z in calls][-1]
         out = dict(calls[0][0], regs=sorted(set(c[0]["regs"][0] for c in calls)))
-        return emit("P", run, out, [x for c in calls for x in c[1:3]], (0, sum(max(64, c[2]["n"]) for c in calls), 3), 60.0)
+        return emit("P", run, out, [x for c in calls for x in c[1:3]],
+                    (0, sum(max(64, c[2]["n"]) * (1 if c[2]["two"] else 4) for c in calls), 3), 60.0)
 
     def mm(out, l, r, start, stop):
         return mms([(out, l, r, start, stop)])
@@ -165,11 +169,16 @@ def build(T, rank, topo, core):
     def ws(n, r):
         return A(n, 15 - r, 143 - r)
 
-    def wrap(out, n, rhs, start=True, stop=True):
-        return mms([(out, ws(n, r), rhs(r), start and r == 0, stop and r == 15) for r in range(16)])
+    def wrap(out, n, rhs, start=True, stop=True, step=16):
+        for h in range(0, 16, step):
+            mms([(out, ws(n, r), rhs(r), start and r == 0, stop and r == 15) for r in range(h, h + step)])
 
-    def unwrap(bank, src):
-        return mms([(A(bank, r, 256, 16), A("UW", 128 * r, 128 * r + 128), src, True, True) for r in range(16)])
+    def unwrap(bank, src, at=0):
+        return mms([(A(bank, at + r, at + 16 * src["n"], 16), A("UW", 128 * r, 128 * r + 128), src, True, True) for r in range(16)])
+
+    def runs(a, b):
+        cut = [a, b] if b - a == 64 else [a, S - first if a < S - first < b else 128, b]
+        return [(x, y, (x + first) % S) for x, y in zip(cut, cut[1:])]
 
     def mshift(n, a, d):
         return A(n, 160 * a + 16 - d, 160 * a + 144 - d)
@@ -179,54 +188,57 @@ def build(T, rank, topo, core):
         mms([(A(bank, k * a, k * a + k), mshift(m, a, d * (b - a)), A(src, b, n, 4), b == 0, b == 3)
              for a in part for b in range(4)])
 
-    def back(bank, src, m, d):
-        mms([(A(bank, b, 256, 4), mshift(m, b, d * (a - b)), A(src, 64 * a, 64 * a + 64), a == 0, a == 3)
+    def back(bank, src, m, d, at=0):
+        mms([(A(bank, b, 256, 4), mshift(m, b, d * (a - b)),
+              block(src, 4 * a, 4 * a + 4, 0, 16) if src == "v4" else A(src, at + 64 * a, at + 64 * a + 64), a == 0, a == 3)
              for b in range(4) for a in range(4)])
 
     def col(n, j):
         return A(n, j, j + 1)
 
-    ns4, ns5 = CFG["ns4"], CFG["ns5"]
-    early = 16 - CFG["late"]
-    nv4 = 16 - ns4
+    early, first = CFG["early"], 64 * (rank + 1) % S
     Ip, In, Ih, If = A("Ip", 0, 128), A("In", 0, 128), A("Ih", 0, 128), A("If", 0, 128)
     sw = A("sw", 0, 16)
-    dma("Y", A("X", O, O + W // 2), ext(T.x0[:, 0:W // 2]), "dx", 256)
-    dma("Y", A("X", O + W // 2, O + W), ext(T.x0[:, W // 2:W]), "dx2", 512)
-    dma("S", A("CM", 0, S), ext(T.come[:, 0:S]), "dc0", 64)
-    dma("S", A("cdi", 0, 128), ext(T.cd0[:]), "dcd", 64)
-    dma("S", A("agi", 0, 48), ext(T.age[:]), "dag", 24)
-    dma("Y", A("D", O, O + W), ext(T.dl0[:]), "ddl", 1536)
-    dma("Y", A("CM", S, R * S), ext(T.come[:, S:R * S]), "dcm", 1728)
+    dma("Y", A("X", O, O + W // 2), ext(T.x0[:, 0:W // 2]), "dx", 300)
+    dma("Y", A("X", O + W // 2, O + W), ext(T.x0[:, W // 2:W]), "dx2", 600)
+    dma("S", A("CM", 0, S), ext(T.come[:, 0:S]), "dc0", 300)
+    dma("S", A("cdi", 0, 128), ext(T.cd0[:]), "dcd", 450)
+    dma("Y", A("agi", 0, 48), ext(T.age[:]), "dag", 700)
+    dma("Y", A("D", O, O + W), ext(T.dl0[:]), "ddl", 1700)
+    dma("Y", A("CM", S, R * S), ext(T.come[:, S:R * S]), "dcm", 1900)
     iota(A("pi", 0, 1), [[0, 1]], 0, 1, False)
     iota(A("jrow", 0, 256), [[1, 256]], 0, 0)
-    iota(A("jg", 0, 128), [[16, 8], [0, 16]], 0, 0)
-    iota(A("Kc", 0, 256), [[61, 16], [0, 16]], 7, 0)
+    iota(A("ax", 0, 128), [[16, 8], [0, 16]], 0, 0)
+    iota(A("Kc", 0, 16 * CFG["w4"]), [[61, 16], [0, CFG["w4"]]], 7, 0)
+    if CFG["w4"] < 16:
+        iota(A("Kc", 192, 256), [[61, 16], [0, 4]], 7, 0)
     iota(A("s1", 0, 144), [[1, 144]], 0, 0)
-    iota(A("jm", 0, 256), [[0, 16], [1, 16]], 0, 0)
-    fill(A("UWi", 0, 2048), 1.0)
+    iota(A("aw", 0, 256), [[0, 16], [1, 16]], 0, 0)
+    iota(A("wq", 0, 12), [[0, 4], [4, 3]], 0, 0)
+    fill(A("UWi", 0, 512), 1.0)
     fill(A("cH", 0, 256), -0.5)
     fill(A("cV", 0, 512), 10.5 * K3)
     fill(A("cS", 0, 512), 2.5 * K3)
     gfill(A("XA", 0, O - 1), 0)
     gfill(A("XA", O - 1, O), -512)
-    gfill(A("X", 0, O), 0)
+    gfill(A("X", 2 * S, O), 0)
     gfill(A("C", 0, O), -1025)
     iota(A("D", 0, O), [[0, O]], -1, 0, False)
     gfill(A("one", 0, 256), 1)
-    gfill(A("Sb", 0, 144), 0)
-    gfill(A("cF", 0, 144 * R), 0)
-    gfill(A("fl", 0, 64), 0)
-    gfill(A("inc", 0, 256), 1)
-    act(A("inc", 0, 256), A("inc", 0, 256), Fn.Identity, scale=1.0 / 1024)
+    gfill(A("Sb", 0, 1), 0)
+    gfill(A("Sb", 130, 144), W)
+    gfill(lane("fl", 0, 64, 4), 0)
+    fill(A("inc", 0, 256), 1.0 / 1024)
     fill(A("vv", 129, 144), 1024 + 129.125)
-    iota(A("cJb", 0, 129), [[2, 129]], 2050, 0)
-    gfill(A("cJb", 129, 130), -1)
-    iota(A("cJb", 130, 144), [[2, 14]], 2310, 0)
-    gfill(A("cJ4", 0, 16 * nv4), -43008)
-    gfill(A("cJ4", 16 * nv4, 256), -10240)
-    gfill(A("cJ5", 0, 16 * ns5), -10240)
-    gfill(A("cJ5", 16 * ns5, 256), -43008)
+    gfill(A("F", 129, 130), 1)
+    gfill(A("F", 130, 144), 0)
+    for n, rows, w in (("cJ4", CFG["rows4"], CFG["w4"]), ("cJ5", CFG["rows5"], 16), ("cJ3", CFG["rows3"], 16)):
+        iota(A(n, 0, 16 * w), [[0, 4], [-18592, 2], [0, 2 * w]], -13504, 0)
+        for k in range(0, 16, 2):
+            if (rows[k] == "S") != (k % 4 == 0):
+                gfill(A(n, w * k, w * k + 2 * w), -13504 if rows[k] == "S" else -32096)
+    if CFG["w4"] < 16:
+        gfill(A("cJ4", 192, 256), -13504 if CFG["here"] == "L" else -32096)
     ts(col("pt", 0), col("pi", 0), 15, Op.bitwise_and)
     ts(col("pt", 1), col("pi", 0), 112, Op.bitwise_and)
     ts(col("pt", 2), col("pi", 0), 3, Op.bitwise_and)
@@ -236,19 +248,28 @@ def build(T, rank, topo, core):
     cp(A("pc", 1, 3), A("pt", 0, 2))
     ts(col("pc", 3), col("pt", 1), 15.0, Op.add)
     cp(A("pc", 5, 7), A("pt", 2, 4))
-    act(col("pc", 7), col("pc", 1), Fn.Identity, scale=32.0)
+    act(col("pc", 7), col("pc", 1), Fn.Identity, bias=32.0 * (S - first), scale=32.0)
     ts(A("WS1", 0, 144), A("jrow", 0, 144), col("pc", 3), Op.is_equal)
     ts(Ip, A("jrow", 0, 128), col("pc", 0), Op.is_equal)
-    ts(A("BD", 0, 128), A("jg", 0, 128), col("pc", 2), Op.is_equal)
+    ts(A("BD", 0, 128), A("ax", 0, 128), col("pc", 2), Op.is_equal)
     act(A("p32", 0, 128), A("jrow", 0, 128), Fn.Identity, bias=col("pc", 7), scale=512.0)
     act(sw, A("jrow", 0, 16), Fn.Identity, bias=col("pc", 1), scale=16.0)
     for n, src, k, v in (("Ih", "Ip", 128, 0.5), ("In", "Ip", 128, -1.0), ("BDv", "BD", 128, -K3), ("BDs", "BD", 128, -K3 / 2),
-                         ("BD2", "BD", 128, 2.0), ("WSz", "WS1", 144, -512.0), ("WSv", "WS1", 144, 4096.0),
-                         ("WSs", "WS1", 144, 2048.0), ("TLn", "TL", 128, -1.0 / 1024)):
+                         ("BD2", "BD", 128, 2.0), ("WSz", "WS1", 144, -512.0), ("WSv", "WS1", 144, 3104.0),
+                         ("W32", "WS1", 144, 32.0), ("I8", "Ip", 128, 16384.0), ("TLn", "TL", 128, -1.0 / 1024)):
         if n == "TLn":
             select(A("TL", 0, 128), A("BD", 0, 128), [[1, 128]], Op.is_ge, 0, -1)
         act(A(n, 0, k), A(src, 0, k), Fn.Identity, scale=v)
-    ts(A("L16", 0, 16), A("jrow", 0, 16), 0.0, Op.mult, col("pc", 1), Op.add)
+    act(A("cL", 0, 8), A("sw", 0, 8), Fn.Identity, bias=1032.0, scale=8.0)
+    act(col("cL", 8), col("pc", 1), Fn.Identity, bias=2064.0, scale=16.0)
+    if CFG["w4"] < 16:
+        act(A("wq", 16, 28), A("wq", 0, 12), Fn.Identity, bias=col("pc", 1))
+        ts(A("wq", 32, 44), A("wq", 16, 28), 12.0, Op.is_ge, -12.0, Op.mult)
+        tt(A("wq", 48, 60), A("wq", 32, 44), A("wq", 16, 28), Op.add)
+        cp(A("L16", 0, 12), A("wq", 48, 60))
+        ts(A("L16", 12, 16), A("one", 0, 4), 12.0, Op.mult, col("pc", 5), Op.add)
+    else:
+        ts(A("L16", 0, 16), A("jrow", 0, 16), 0.0, Op.mult, col("pc", 1), Op.add)
     ts(A("pc", 8, 12), A("jrow", 0, 4), col("pc", 5), Op.is_equal)
     ts(A("pc", 12, 16), A("jrow", 0, 16, 4), col("pc", 6), Op.is_equal)
     for a in range(4):
@@ -256,21 +277,25 @@ def build(T, rank, topo, core):
         ts(A("M1", 160 * a, 160 * a + 160), A("jrow", 0, 160), col("pc", 4), Op.is_equal, col("pc", 12 + a), Op.mult)
     for t in range(R):
         r0 = ST * (t + 1) % 16
-        ts(A("fb", 16 * t, 16 * t + 16), sw, float(Y0 - O - S * t), Op.add)
-        act(col("cF", 144 * t), col("pc", 1), Fn.Relu, bias=8192.0 * r0, scale=-8192.0)
-        act(col("cF", 144 * t + 128), col("pc", 1), Fn.Relu, bias=8192.0 * (1 - r0), scale=8192.0)
+        ts(A("v5%d" % t, 0, 16), sw, float(Y0 + S - O - S * t), Op.add)
+        act(col("cF", 2 * t), col("pc", 1), Fn.Relu, bias=8192.0 * r0, scale=-8192.0)
+        act(col("cF", 2 * t + 1), col("pc", 1), Fn.Relu, bias=8192.0 * (1 - r0), scale=8192.0)
     for h in range(0, W, 512):
         act(A("XF", O + h, O + h + 512), A("X", O + h, O + h + 512), Fn.Identity, scale=16.0)
-    select(A("segn", 0, 256), A("X", 0, 256), [[0, 16], [1, 16]], Op.not_equal, 0, 0, -60000.0)
-    ts(A("mk", 0, 256), A("jm", 0, 256), col("pc", 1), Op.not_equal, -48976.0, Op.mult)
+    select(A("segn", 0, 256), A("XA", 0, 256), [[0, 16], [1, 16]], Op.not_equal, 0, 0, -60000.0)
+    ts(A("mk", 0, 256), A("aw", 0, 256), col("pc", 1), Op.not_equal, -48976.0, Op.mult)
     ts(A("Wh", 0, 144), A("WS1", 0, 144), 0.0625, Op.mult)
     select(If, Ip, [[0, 128]], Op.is_ge, 0, 0)
     for h in range(0, W, 512):
+        select(A("UW", h, h + 512), A("UWi", 0, 512), [[1, 4], [16, 8], [0, 16]], Op.is_equal, h // 128, -1)
+        chain("wide")
+    for h in range(0, W, 512):
         iota(A("CO", h, h + 512), [[61, 4], [0, 128]], 7 + 61 * (h // 128), 0)
+        chain("wide")
         select(A("KI", h, h + 512), A("CO", h, h + 512), [[0, 4], [1, 128]], Op.is_equal, 0, -1)
-        select(A("UW", h, h + 512), A("UWi", h, h + 512), [[1, 4], [16, 8], [0, 16]], Op.is_equal, h // 128, -1)
     for t in range(R - 1):
-        act(lane("cc", 64 * t, 64 * t + 64, 4), sw, Fn.Identity, bias=float(W + S * t))
+        for a, b, i in runs(0, S):
+            act(lane("cc", 64 * t + a // 4, 64 * t + b // 4, 4), A("sw", i // 16, (i + b - a) // 16), Fn.Identity, bias=float(W + S * t))
     cp(A("cdh", 0, 128), A("cdi", 0, 128))
     ts(A("cdf", 0, 128), A("cdi", 0, 128), -1024.0, Op.add)
     for r in range(16):
@@ -289,7 +314,9 @@ def build(T, rank, topo, core):
         for t in range(R - 1):
             oldest = W + S * t + S - 1 - 1024
             for n, less in (("th1", S * t), ("th2", 1024)):
-                act(A(n, 16 * t, 16 * t + 16), A("p1", 16 * t, 16 * t + 16), Fn.Identity, bias=float(oldest - less), scale=-1.0)
+                for a, b, i in runs(0, S):
+                    act(A(n, 16 * t + a // 16, 16 * t + b // 16), A("p1", 16 * t + i // 16, 16 * t + (i + b - a) // 16),
+                        Fn.Identity, bias=float(oldest - less), scale=-1.0)
 
     def who(t):
         lo = S * t
@@ -302,72 +329,80 @@ def build(T, rank, topo, core):
 
     def pre_terms(t):
         lo = S * t
-        mms([(A("p3", 0, 256), Ih, A("CM", lo, lo + S), True, False), (A("p3", 0, 256), Ih, A("cH", 0, 256), False, t == 0)])
+        bank = "p7" if t else "p3"
+        mms([(A(bank, 0, 256), Ih, A("cH", 0, 256), True, False)] +
+            [(A(bank, a, b), Ih, A("CM", lo + i, lo + i + b - a), False, t == 0 and b == S) for a, b, i in runs(0, S)])
 
-    def judge_parts(E, off, yy, win, cj):
-        flip = [0]
+    def copy(out, a):
+        return select(out, a, [[0, a["n"]]], Op.is_ge, 0, 0)
 
-        def vrow(k):
-            tt(A(E, 256 * k, 256 * k + 256), IND(win, A(off, 16 * k, 16 * k + 16)), yy, Op.is_ge)
+    def judge_parts(E, off, ys, y, win, cj, w=16, at=0):
+        def vrow(k, n):
+            a, b = at + w * k, at + w * (k + n)
+            tt(A(E, 16 * a, 16 * b), IND(win, A(off, a, b)), A(ys, y, y + 16 * w * n), Op.is_ge)
             chain("V")
 
-        def srows(k0, k1):
-            todo = None
-            for k in list(range(k0, k1, 2)) + [None]:
-                if k is not None:
-                    n = min(2, k1 - k)
-                    h, pb = 512 * flip[0], ("p2", "p3", "p0")[flip[0]]
-                    flip[0] = (flip[0] + 1) % 3
-                    act(A("Gd", h, h + 256 * n), IND(win, A(off, 16 * k, 16 * (k + n))), Fn.Identity)
-                    chain("S")
-                    mms([(A(pb, 0, 256 * n), Ip, A("Gd", h, h + 256 * n), True, False)] +
-                        [(A(pb, 256 * i, 256 * i + 256), In, yy, False, i == n - 1) for i in range(n)])
-                if todo is not None:
-                    act(A(E, 256 * todo[0], 256 * (todo[0] + todo[1])), A(todo[2], 0, 256 * todo[1]), Fn.Sign, bias=0.5)
-                    chain("S")
-                todo = None if k is None else (k, n, pb)
+        def srows(k, n=2):
+            h, pb, a, b = 512 * flip[0], ("p2", "p3", "p0")[flip[0]], at + w * k, at + w * (k + n)
+            flip[0] = (flip[0] + 1) % 3
+            act(A("Gd", h, h + 16 * w * n), IND(win, A(off, a, b)), Fn.Identity)
+            chain("S")
+            mm(A(pb, 0, 16 * w * n), In, A(ys, y, y + 16 * w * n), True, False)
+            mm(A(pb, 0, 16 * w * n), Ip, A("Gd", h, h + 16 * w * n), False, True)
+            signs()
+            due.append((A(E, 16 * a, 16 * b), A(pb, 0, 16 * w * n)))
 
         def const(bank, k0, k1):
-            mm(A(bank, 16 * k0, 16 * k1), Ip, A(cj, 16 * k0, 16 * k1), True, False)
+            mm(A(bank, at + w * k0, at + w * k1), If, A(cj, at + w * k0, at + w * k1), True, False)
 
-        def count(bank, k0, k1, m, stop=False):
-            wrap(A(bank, 16 * k0, 16 * k1), m, lambda r: A(E, 256 * k0 + r, 256 * k1, 16), False, stop)
+        def count(bank, k0, k1, stop):
+            a, b = at + w * k0, at + w * k1
+            wrap(A(bank, a, b), "WSv", lambda r: A(E, 16 * a + r, 16 * b, 16), False, stop)
 
-        return vrow, srows, const, count
+        def rows(own, k0, k1):
+            for k in range(k0, k1):
+                if own[k] == "V":
+                    vrow(k, 1)
+                elif own[k] in "LM":
+                    if k % 8 == 0:
+                        srows(k, 8) if own[k] == "L" else vrow(k, 8)
+                elif k % 2 == 0:
+                    srows(k) if own[k] == "S" else vrow(k, 2)
 
-    def tree(v, bank, c, k0, k1, tmp, at, out):
-        tt(A(v, 16 * k0, 16 * k1), A(bank, 16 * k0, 16 * k1), A(c, 16 * k0, 16 * k1), Op.min)
-        src, a, n = v, 16 * k0, k1 - k0
-        top = A(src, a, a + 16)
+        return rows, const, count
+
+    flip, due = [0], []
+
+    def signs():
+        while due:
+            act(*due.pop(), Fn.Sign, bias=0.5)
+            chain("S")
+
+    def tree(v, bank, c, k0, k1, tmp, to, out, more=0, w=16, at=0):
+        a, b = at + w * k0, at + w * k1
+        tt(A(v, 16 + a, 16 + b), A(bank, a, b), A(c, a, b), Op.min)
+        src, a, n = v, 16 + a - w * more, k1 - k0 + more
         while n > 1:
             h = (n + 1) // 2
-            top = out if h == 1 and out is not None else A(tmp, at, at + 16 * h)
-            tt(top, A(src, a, a + 16 * h), A(src, a + 16 * (n - h), a + 16 * n), Op.max)
-            src, a, n, at = tmp, at, h, at + 16 * h
+            top = out if h == 1 and out is not None else A(tmp, to, to + w * h)
+            tt(top, A(src, a, a + w * h), A(src, a + w * (n - h), a + w * n), Op.max)
+            src, a, n, to = tmp, to, h, to + w * h
         return top
 
-    def chunks(a, b):
-        cut = list(range(a, max(b - 3, a + 1), 4)) + [b]
-        return list(zip(cut, cut[1:]))
-
-    def places(t):
-        cp(A("hi", 0, 16), A("uq", 0, 16))
-        ts(A("hj", 0, 16), A("hi", 0, 16), 5, Op.arith_shift_right, W - 1, Op.bitwise_and)
+    def places(t, j0, j1):
+        a, b = 16 * j0, 16 * j1
         if t == 0:
-            cp(A("hA", 0, 16), A("hj", 0, 16))
-            tt(A("T1", 0, 256), IND(A("ua", 0, 16), A("L16", 0, 16)), A("Kc", 0, 256), Op.mult)
-            tt(A("T2", 0, 256), IND(A("hA", 0, 16), A("L16", 0, 16)), A("T1", 0, 256), Op.add)
-        else:
-            ts(A("uh", 16, 32), A("hj", 0, 16), col("ac", 0), Op.add, -2048.0, Op.add)
-            mms([c for m in range(16) for c in (
-                (A("p7", 16 * m, 16 * m + 16), A("KI", 128 * m, 128 * m + 128), A("uh", 0, 16), True, False),
-                (A("p7", 16 * m, 16 * m + 16), If, A("uh", 16, 32), False, True))])
-            ts(A("T2", 0, 256), A("p7", 0, 256), 4194304.0, Op.add)
-        ts(A("c4", 0, 256), A("T2", 0, 256), W - 1, Op.bitwise_and)
-        ts(A("o4", 0, 256), A("c4", 0, 256), 16.0, Op.add)
+            tt(A("T1", 0, 256), IND(A("hj", 16, 32), A("L16", 0, 16)), A("Kc", 0, 256), Op.mult)
+            tt(A("avi", 0, 256), IND(A("hj", 0, 16), A("L16", 0, 16)), A("T1", 0, 256), Op.add)
+        elif j0 == 0:
+            for h in range(0, 16, 4):
+                mms([c for m in range(h, h + 4) for c in (
+                    (A("p7", 16 * m, 16 * m + 16), A("KI", 128 * m, 128 * m + 128), A("uh", 16, 32), True, False),
+                    (A("p7", 16 * m, 16 * m + 16), If, A("uh", 0, 16), False, True))])
+            ts(block("T2", 0, 16, 0, 16), A("p7", 0, 256), col("ac", 0), Op.add)
+        ts(A("c4", a, b), block("T2", 0, 16, j0, j1) if t else A("avi", a, b), W - 1, Op.bitwise_and)
+        ts(A("o4", a, b), A("c4", a, b), 16.0, Op.add)
 
-    peers = sorted([(rank + k) % N for k in range(1, N)],
-                   key=lambda b: topo.same_plane(topo.chip(core), topo.chip(T.cores[b])))
     counts = ("p0", "p1", "p4", "p5")
     pre_terms(0)
 
@@ -375,77 +410,100 @@ def build(T, rank, topo, core):
         lo, B = S * t, W + S * t
         last = t == R - 1
         c0 = ST * (t + 1) // 16
-        xa = A("X", O + B, O + B + S)
+        w4 = 16 if last else CFG["w4"]
+        xa = A("XR", 192, 448)
         if t > 0:
-            z0 = S * (t - 1)
-            mm(A("p3", 64 * rank, 64 * rank + 64), Ih, A("zs", z0 + 64 * rank, z0 + 64 * rank + 64), False, False)
-            mms([(A("p3", 64 * b, 64 * b + 64), Ih, A("Z", z0 + 64 * b, z0 + 64 * b + 64), False, b == peers[-1]) for b in peers])
+            mm(A("p7", 0, 256), In, A("Z", lo - S, lo), False, True)
             ops[-1]["arr"] = t - 1
-        ts(xa, A("p3", 0, 256), MAGIC, Op.add, MAGIC, Op.subtract)
+        ts(xa, A("p7" if t else "p3", 0, 256), MAGIC, Op.add, MAGIC, Op.subtract)
         if t == 0:
             who(0)
-        wrap(A("p7", 0, 16), "WS1", lambda r: A("X", O + B + r, O + B + S, 16))
-        act(A("uq", 0, 16), A("p7", 0, 16), Fn.Square)
+        wrap(A("p7", 16, 32), "W32", lambda r: A("XR", 192 + r, 448, 16))
+        act(A("p7", 0, 16), A("p7", 16, 32), Fn.Square, scale=1.0 / 32)
+        cp(A("hi", 0, 32), A("p7", 0, 32))
+        ts(A("hj", 0, 32), A("hi", 0, 32), 5, Op.arith_shift_right, W - 1, Op.bitwise_and)
         if t > 0:
-            ts(A("uh", 0, 16), A("p7", 0, 16), -2048.0, Op.add)
+            cp(A("uh", 0, 32), A("hj", 0, 32))
+        if w4 == 16:
+            copy(A("XR", 448, 704), xa)
         else:
-            act(A("ua", 0, 16), A("p7", 0, 16), Fn.Identity)
+            copy(A("XR", 0, 192), A("XR", 192, 384))
+            for h in (64, 128, 256):
+                copy(A("XR", 384 + h, 384 + 2 * h), A("XR", 384, 384 + h))
+        for a, b, i in runs(0, S):
+            copy(A("X", O + B + i, O + B + i + b - a), A("XR", 192 + a, 192 + b))
         diffs = ["p2", "p3"]
-        for i, e in enumerate(CFG["own"]):
+        for i, e in enumerate(CFG["own" if t else "own0"]):
             a, bank = O + lo + 512 * i, counts[i]
-            ed, got, old = A("Ed", 512 * i, 512 * i + 512), IND(xa, A("who", 32 * i, 32 * i + 32)), A("X", a, a + 512)
+            ed, names, old = A("Ed", 512 * i, 512 * i + 512), A("who", 32 * i, 32 * i + 32), A("X", a, a + 512)
             known = min(512, O + B - S - a)
             mms([(A(bank, 0, 512), Ip, A("cV" if e == "V" else "cS", 0, 512), True, False)] +
                 ([(A(bank, 0, known), A("BD2", 0, 128), A("XA", a, a + known), False, False)] if t > 0 else []))
+            soon = t and e in CFG["soon"]
+            got = IND(A("Z", lo - S, lo), names) if soon else IND(xa, names)
+            half = IND(A("CMh", lo - S, lo), names) if soon else None
             if e == "V":
                 tt(ed, got, old, Op.is_ge)
             else:
                 pb = diffs.pop(0)
                 diffs.append(pb)
                 gd = A("Gd", 0, 512) if pb == "p2" else A("Gd", 512, 1024)
-                act(gd, got, Fn.Identity)
                 mm(A(pb, 0, 512), In, old, True, False)
-                mm(A(pb, 0, 512), Ip, gd, False, True)
-                act(ed, A(pb, 0, 512), Fn.Sign, bias=0.5)
+                if soon:
+                    act(A("E5", 512 * i, 512 * i + 512), half, Fn.Identity)
+                    mm(A(pb, 0, 512), Ip, A("E5", 512 * i, 512 * i + 512), False, False)
+                act(gd, got, Fn.Identity)
+                ops[-1]["arr"] = t - 1 if soon else None
+                mm(A(pb, 0, 512), In if soon else Ip, gd, False, True)
+                act(ed, A(pb, 0, 512), Fn.Sign, bias=0.25)
             mm(A(bank, 0, 512), A("BDv" if e == "V" else "BDs", 0, 128), ed, False, True)
             tt(A("XA", a, a + 512), A(bank, 0, 512), old, Op.min)
-        places(t)
+        places(t, 0, w4 if t else 16)
         wall = A("XA", 0, O + B)
         win = A("XA", lo + O - 16, O + B)
-        for i, e in enumerate(CFG["og"]):
-            got = IND(A("XA", 0, O + lo + 512 * i + 512), A("lc", 32 * i, 32 * i + 32))
-            if e == "V":
-                ts(A("Og", 512 * i, 512 * i + 512), got, 0.0, Op.min, -1.0, Op.max)
+        ov = CFG["ov3" if last else "ov"]
+        cuts = sorted(set(range(0, 128 - ov, 32)) | {128 - ov, 128})
+        for a, b in zip(cuts, cuts[1:]):
+            got = IND(A("XA", 0, O + lo + 16 * b), A("lc", a, b))
+            if a >= 128 - ov:
+                ts(A("Og", 16 * a, 16 * b), got, 0.0, Op.min, -1.0, Op.max)
             else:
-                act(A("Og", 512 * i, 512 * i + 512), got, Fn.Sign, bias=0.5)
+                act(A("Og", 16 * a, 16 * b), got, Fn.Sign, bias=0.5)
 
-        def cyclic(a, b):
-            return A("p6", a - c0, b - c0) if a >= c0 else A("p6", a + 128 - c0, b + 128 - c0)
-        mm(A("p6", 0, 129), In, A("cF", 144 * t, 144 * t + 129), True, False)
+        def cyclic(a, b, bank="p6"):
+            return A(bank, a - c0, b - c0) if a >= c0 else A(bank, a + 128 - c0, b + 128 - c0)
+        mms([(A("p6", 0, 129), In, A("XA", 0, 129), True, False), (A("p6", 0, 129, 128), In, A("cF", 2 * t, 2 * t + 2), False, False)])
         if t == 0:
             mms([(cyclic(a, b), In, A("cdm", a, b), False, False) for a, b in ((0, c0 + 1), (c0, 128))])
         for a, b in ((0, c0 + 1), (c0, 128)):
-            wrap(cyclic(a, b), "WS1", lambda r: A("XA", O + lo + 16 * a + r, O + lo + 16 * b, 16), False, False)
+            wrap(cyclic(a, b, "p6" if last else "p0"), "WS1", lambda r: A("XA", O + lo + 16 * a + r, O + lo + 16 * b, 16),
+                 not last, not last)
+        if not last:
+            act(A("live", 0, 129), A("p0", 0, 129), Fn.Sign, bias=0.5)
+            mm(A("p6", 0, 129), A("I8", 0, 128), A("live", 0, 129), False, False)
         for a, b in [(0, c0 + 1)] + ([(c0, 64), (64, 128)] if c0 < 32 else [(c0, 128)]):
             wrap(cyclic(a, b), "WSz", lambda r: A("Og", 16 * a + r, 16 * b, 16), False, b == 128)
         F = A("F", 0, 129)
-        ts(F, A("p6", 0, 129), 6000.0, Op.is_ge)
+        ts(F, A("p6", 0, 129), 6000.0 if last else 20000.0, Op.is_ge)
         gfill(A("Tw", 0, S), 0)
-        mms([(A("p6", 0, 129), A("BD", 0, 128), F, True, True), (A("p6", 144, 288), If, A("cJb", 0, 144), True, False),
-             (A("p6", 144, 273), A("BDv", 0, 128), F, False, True)])
+        mm(A("p6", 0, 129), A("BD", 0, 128), F, True, True)
+        mm(A("p1", 0, 9), In, A("cL", 0, 9), True, False)
+        wrap(A("p1", 0, 9), "WSv", lambda r: A("F", r, 144, 16), False, True)
+        act(A("far", 0, 9), A("p1", 0, 9), Fn.Relu, scale=-2.0)
         mms([(A("p7", 0, 129), Ip, A("s1", 0, 129), True, False), (A("p7", 0, 129), A("TLn", 0, 128), F, False, True)])
         scan(A("Sb", 1, 130), A("p6", 0, 129), A("one", 0, 129), Op.add, Op.mult)
-        tt(A("off", 0, 144), A("p6", 144, 288), A("Sb", 0, 144), Op.max)
         act(A("vv", 0, 129), A("p7", 0, 129), Fn.Identity, bias=1024.5 + 0.5 / 1024)
-        wrap(A("p6", 0, 9), "Wh", lambda r: A("off", r, 144, 16))
+        wrap(A("p6", 0, 9), "Wh", lambda r: A("Sb", r, 144, 16), True, False)
+        mm(A("p6", 0, 9), Ip, A("far", 0, 9), False, True)
         cp(A("lb", 0, 9), A("p6", 0, 9))
-        cp(SCT(A("Tw", 0, 2352), A("lb", 0, 9)), A("vv", 0, 144))
+        cp(SCT(A("Tw", 0, 6672), A("lb", 0, 9)), A("vv", 0, 144))
         scan(A("E3", 0, 256), A("inc", 0, 256), A("Tw", 0, 256), Op.add, Op.max)
         base = float(O + lo + 16 * c0)
-        ts(A("Ub", 0, 16), sw, col("Sb", 129), Op.is_ge, -(base + 16.0) / 16, Op.mult)
-        ts(A("Ub", 16, 32), sw, col("Sb", 128 - c0), Op.is_ge, -128.0, Op.mult)
-        act(col("U", 0), col("Sb", 129), Fn.Identity, scale=-1.0 / 16)
-        act(A("Ub", 32, 48), sw, Fn.Relu, bias=col("U", 0), scale=1.0 / 16)
+        cp(A("U", 0, 2), A("Sb", 128 - c0, 130, c0 + 1))
+        ts(A("Ub", 0, 16), sw, col("U", 1), Op.is_ge, -(base + 16.0) / 16, Op.mult)
+        ts(A("Ub", 16, 32), sw, col("U", 0), Op.is_ge, -128.0, Op.mult)
+        act(col("U", 2), col("U", 1), Fn.Identity, scale=-1.0 / 16)
+        act(A("Ub", 32, 48), sw, Fn.Relu, bias=col("U", 2), scale=1.0 / 16)
         mms([(A("p6", 0, 16), Ip, A("Ub", 16 * i, 16 * i + 16), i == 0, False) for i in range(3)])
         wrap(A("p6", 0, 16), "Wh", lambda r: A("E3", r, 256, 16), False, True)
         slots = A("lo1", 0, 16)
@@ -453,62 +511,86 @@ def build(T, rank, topo, core):
         ts(A("dg", 0, 256), IND(A("D", 0, O + B), slots), float(-lo), Op.add, -1.0, Op.max)
         yy = A("X", Y0, Y0 + S)
         act(yy, IND(wall, slots), Fn.Identity)
+        copy(A("X", S, 2 * S), yy)
         turn("p7", "dg", 256, "M0", 1)
         cp(A("ta", 0, 256), A("p7", 0, 256))
         for bank, h in (("p6", 0), ("p7", 128)):
             turn(bank, "ta", 256, "M1", 4, range(h // 64, h // 64 + 2))
             ts(A("o5", h, h + 128), A(bank, h, h + 128), 16.0, Op.add)
-            act(A("c5", h, h + 128), A(bank, h, h + 128), Fn.Identity)
-        vrow, srows, const, count = judge_parts("E4", "o4", xa, win, "cJ4")
+            if CFG["c5"] == "S":
+                act(A("c5", h, h + 128), A(bank, h, h + 128), Fn.Identity)
+            else:
+                cp(A("c5", h, h + 128), A(bank, h, h + 128))
+        if t > 0 and w4 < 16:
+            places(t, 12, 16)
+        rows4, const, count = judge_parts("E4", "o4", "XR", 192 if w4 == 16 else 0, win, "cJ3" if last else "cJ4", w4)
+        rows5, const5, count5 = judge_parts("E5", "o5", "X", Y0, win, "cJ5")
         const("p4", 0, 16)
-        for k in range(nv4):
-            vrow(k)
-        srows(nv4, 16)
-        cs = sorted(chunks(0, nv4) + chunks(nv4, 16), key=lambda x: CFG["v4"] * x[1] / nv4 if x[0] < nv4 else (x[1] - nv4) / ns4)
-        for k0, k1 in cs:
-            count("p4", k0, k1, "WSv" if k0 < nv4 else "WSs", (k0, k1) == cs[-1])
-        m4 = tree("v4", "p4", "c4", 0, 16, "tr", 0, A("m4", 0, 16))
-        ts(A("mc", 0, 16), m4, float(-lo - 1), Op.max)
-        unwrap("p4", A("mc", 0, 16))
-        act(A("CO" if last else "C", O + B, O + B + S), A("p4", 0, 256), Fn.Identity, bias=float(lo if last else lo - 1024))
+        own, post = (CFG["rows3"], CFG["post3"]) if last else (CFG["rows4"], 16)
+        rows4(own, 0, post)
+        signs()
+        rows5(CFG["rows5"], 0, 16)
+        signs()
+        rows4(own, post, 16)
+        signs()
+        for k in range(0, 16, 4):
+            count("p4", k, k + 4, k == 12)
+
+        def parents(bank, j0, j1):
+            w, to, m4 = j1 - j0, 16 * j0, A("mc", j0, j1)
+            tt(block("v4", 0, 16, j0, j1), A(bank, to, to + 16 * w), A("c4", to, to + 16 * w), Op.min)
+            tt(A("tr", to, to + 8 * w), block("v4", 0, 8, j0, j1), block("v4", 8, 16, j0, j1), Op.max)
+            for n in (4 * w, 2 * w, w):
+                tt(m4 if n == w else A("tr", to + 2 * n, to + 3 * n), A("tr", to, to + n), A("tr", to + n, to + 2 * n), Op.max)
+                to += 2 * n
+            if not last:
+                ts(A("lh", j0, j1), m4, float(lo + O), Op.add)
+                ts(lane("cc", 64 * t + 4 * j0 + 1, 64 * t + 4 * j1, 4), m4, float(lo), Op.add)
+                tt(lane("fl", 4 * j0 + 1, 4 * j1, 4), m4, A("th1", 16 * t + j0, 16 * t + j1), Op.is_lt)
+            if j1 < 16:
+                return
+            unwrap(bank, A("mc", 0, 16))
+            if not last:
+                act(A("T1", 0, 256), A(bank, 0, 256), Fn.Relu, bias=float(lo + 1))
+            for a, b, i in runs(0, S):
+                if last:
+                    ts(A("CO", O + B + i, O + B + i + b - a), A(bank, a, b), float(lo), Op.add, -1.0, Op.max)
+                else:
+                    act(A("C", O + B + i, O + B + i + b - a), A("T1", a, b), Fn.Identity, bias=-1025.0)
         if t == 0:
             ages()
-        if not last:
-            act(A("XF", O + B, O + B + S), xa, Fn.Identity, scale=16.0)
-            ts(A("lh", 0, 16), A("mc", 0, 16), float(lo + O), Op.add)
-            act(lane("cc", 64 * t + 1, 64 * t + 64, 4), m4, Fn.Identity, bias=float(lo))
-            tt(lane("fl", 1, 64, 4), m4, A("th1", 16 * t, 16 * t + 16), Op.is_lt)
-        vrow, srows, const, count = judge_parts("E5", "o5", yy, win, "cJ5")
-        const("p5", 0, early)
-        const("p1", early, 16)
-        for k in range(ns5, 16):
-            vrow(k)
-        srows(0, ns5)
-        cs = sorted(chunks(0, ns5) + chunks(ns5, early), key=lambda x: x[1] / ns5 if x[0] < ns5 else (x[1] - ns5) / (16 - ns5))
-        for k0, k1 in cs:
-            count("p5", k0, k1, "WSs" if k0 < ns5 else "WSv", (k0, k1) == cs[-1])
-        top = tree("v5", "p5", "c5", 0, early, "tq", 0, None)
-        tt(A("tq", 240, 256), top, A("fb", 16 * t, 16 * t + 16), Op.max)
-        count("p1", early, 16, "WSv", True)
-        top = tree("v5", "p1", "c5", early, 16, "tq", 256, None)
-        tt(A("mc", 16, 32), A("tq", 240, 256), top, Op.max)
-        ts(A("lx", 0, 16), A("mc", 16, 32), float(lo + O - Y0), Op.add)
-        xb = IND(A("X", Y0, O + B), A("lx", 0, 16))
+        parents("p4", 0, w4)
+        const5("p5", 0, early)
+        const5("p1", early, 16)
+        for k in range(0, early, 4):
+            count5("p5", k, min(k + 4, early), k + 4 >= early)
+        v5 = "v5%d" % t
+        top = tree(v5, "p5", "c5", 0, early, "tq", 0, None, 1)
+        count5("p1", early, 16, True)
+        tt(A("mc", 16, 32), top, tree(v5, "p1", "c5", early, 16, "tq", 256, None), Op.max)
+        if w4 < 16:
+            rows4, const, count = judge_parts("E4", "o4", "XR", 384, win, "cJ4", 4, 192)
+            rows4(16 * CFG["here"], 0, 16)
+            signs()
+            const("p5", 0, 16)
+            count("p5", 0, 16, True)
+        ts(A("lx", 0, 16), A("mc", 16, 32), float(lo + O - S), Op.add)
+        xb = IND(A("X", S, O + B), A("lx", 0, 16))
         unwrap("p6", A("mc", 16, 32))
         if last:
-            select(A("xb", 0, 256), yy, [[0, 256]], Op.is_ge, 0, 0)
-            tt(A("sm", 0, 256), xb, A("xb", 0, 256), Op.add)
+            tt(A("sm", 0, 256), xb, yy, Op.add)
             ts(A("avi", 0, 256), A("sm", 0, 256), 0.5, Op.mult, -0.25, Op.add)
             ts(A("cn", 0, 256), A("p6", 0, 256), float(lo), Op.add, -1.0, Op.max)
             wrap(A("p0", 0, 128), "WS1", lambda r: A("XA", O + lo + 128 * r, O + lo + 128 * r + 128))
             ts(A("cdf", 0, 128), A("p0", 0, 128), 0.0, Op.is_ge)
             dma("Y", ext(T.ya[:, 0:W]), A("cdf", 0, 128), "dya", 64)
             dma("Y", ext(T.ya[:, W:W + S]), view(T.one[0:8, 0:256], "one", 0, 256, 256), "dyo", 8)
-            dma("Y", ext(T.yx[:, W:W + S]), xa, "dyy", 64)
+            dma("Y", ext(T.yx[:, W:W + S]), A("X", O + B, O + B + S), "dyy", 64)
             cp(SCT(A("X", 0, O + B), slots), A("avi", 0, 256))
             dma("Y", ext(T.yx[:, 0:W]), A("X", O + lo, O + B), "dyx", 512)
             cp(SCT(A("CO", 0, O + B), slots), A("cn", 0, 256))
-            dma("S", ext(T.yc[:]), view(T.CO[0:128:16, O + lo:PW], "CO", O + lo, PW, W + S), "dyc", 72)
+            dma("S", ext(T.yc[:, 0:W]), view(T.CO[0:128:16, O + lo:O + B], "CO", O + lo, O + B, W), "dyc", 72)
+            dma("S", ext(T.yc[:, W:W + S]), view(T.CO[0:128:16, O + B:PW], "CO", O + B, PW, S), "dyd", 16)
             break
         ts(A("cn", 0, 256), A("p6", 0, 256), float(lo - 1024), Op.add, -1025.0, Op.max)
         cp(SCT(A("C", 0, O + B), slots), A("cn", 0, 256))
@@ -518,36 +600,49 @@ def build(T, rank, topo, core):
         act(A("aw", 0, 256), A("p7", 0, 256), Fn.Identity, bias=MAGIC)
         act(A("ax", 0, 256), A("aw", 0, 256), Fn.Identity, bias=-16 * MAGIC, scale=16.0)
         act(SCT(A("XF", 0, O + B), slots), A("ax", 0, 256), Fn.Silu)
-        cw = A("C", 0, O + B + S)
-        for h in range(2):
-            hg, sc = A("hg", 256 * h, 256 * h + 256), A("sc", 256 * h, 256 * h + 256)
-            tt(hg, IND(cw, A("lh", 16 * h, 16 * h + 16)), A("mk", 0, 256), Op.add)
-            scan(sc, A("segn", 0, 256), hg, Op.add, Op.max)
-            ends = A("sc", 256 * h + 15, 256 * h + 256, 16)
-            if h == 0:
-                ts(A("lh", 16, 32), ends, float(O + 1024), Op.add)
-            ts(lane("cc", 64 * t + 2 + h, 64 * t + 64, 4), ends, 1024.0, Op.add)
-            tt(lane("fl", 2 + h, 64, 4), ends, A("th2", 16 * t, 16 * t + 16), Op.is_lt)
-        scan(A("wq", 0, 64), A("fl", 0, 64), A("cc", 64 * t, 64 * t + 64), Op.mult, Op.max)
-        ts(A("lw", 0, 16), A("wq", 3, 64, 4), float(-lo), Op.add)
-        ts(A("zs", lo, lo + S), IND(A("XF", O + lo, O + B + S), A("lw", 0, 16)), 0.0625, Op.mult)
+        ops[-1]["c"] = (65 if t else 1365, S, 2)
+        act(A("XF", O + B, O + B + S), A("X", O + B, O + B + S), Fn.Identity, scale=16.0)
 
-        def send(q, to, t=t):
-            trs = []
-            free = [e for e in topo.engines(core, T.cores[to[0]]) if all(e in topo.engines(core, T.cores[b]) for b in to)]
-            for i, b in enumerate(to):
-                k = len(free) // 2 if i < len(to) - 1 else len(free)
-                mine, free = free[:k], free[k:]
-                rid, pid, _ = topo.addr(T.cores[b])
+        def hops(j0, j1):
+            for h in range(2):
+                a, b = 256 * h + 16 * j0, 256 * h + 16 * j1
+                tt(A("hg", a, b), IND(A("C", 0, O + B), A("lh", 16 * h + j0, 16 * h + j1)), A("mk", 0, b - a), Op.add)
+                scan(A("sc", a, b), A("segn", 0, b - a), A("hg", a, b), Op.add, Op.max)
+                ends = A("sc", a + 15, b, 16)
+                if h == 0:
+                    ts(A("lh", 16 + j0, 16 + j1), ends, float(O + 1024), Op.add)
+                ts(lane("cc", 64 * t + 4 * j0 + 2 + h, 64 * t + 4 * j1, 4), ends, 1024.0, Op.add)
+                tt(lane("fl", 4 * j0 + 2 + h, 4 * j1, 4), ends, A("th2", 16 * t + j0, 16 * t + j1), Op.is_lt)
+            scan(A("wq", 4 * j0, 4 * j1), A("fl", 4 * j0, 4 * j1), A("cc", 64 * t + 4 * j0, 64 * t + 4 * j1), Op.mult, Op.max)
+            ts(A("lw", j0, j1), A("wq", 4 * j0 + 3, 4 * j1, 4), float(-lo), Op.add)
+
+        def reached(out, j0, j1):
+            ts(A(out, lo + 16 * j0, lo + 16 * j1), IND(A("XF", O + lo, O + B + S), A("lw", j0, j1)), -1.0 / 32, Op.mult)
+
+        def send(q, pieces, t=t):
+            trs, to = [], [T.cores[(rank + 1 + k) % N] for k in pieces]
+            free = [e for e in topo.engines(core, to[0]) if all(e in topo.engines(core, c) for c in to)]
+            share = len(free) // len(to)
+            for i, k in enumerate(pieces):
+                rid, pid, _ = topo.addr(to[i])
                 trs.append(RemoteDMATransfer(
-                    dst_ids=[DstId(rid=rid, pnc=pid)], dma_engine_mask=sum(1 << e for e in mine),
-                    remote_sem=T.sem["arr%d" % t], src=T.zs[:, S * t + 64 * b:S * t + 64 * b + 64],
-                    dst=T.Z[:, S * t + 64 * rank:S * t + 64 * rank + 64]))
+                    dst_ids=[DstId(rid=rid, pnc=pid)], dma_engine_mask=sum(1 << e for e in free[share * i:share * i + share]),
+                    remote_sem=T.sem["arr%d" % t], src=T.zs[:, S * t + 64 * k:S * t + 64 * k + 64],
+                    dst=T.Z[:, S * t + 64 * (2 - k):S * t + 64 * (3 - k)]))
             return q.remote_dma_fused(trs, local_sem=T.sem["snt%d" % t])
-        for to in ([peers[:2], peers[2:]] if CFG["calls"] == 2 else [peers]):
-            sent = emit("G", lambda q, to=to, f=send: f(q, to), ext(None), [A("zs", lo, lo + S)], (400, 0, 0))
+        hops(0, 12)
+        for pieces in ((0, 1), (2,)):
+            reached("zs", 4 * pieces[0], 4 * pieces[-1] + 4)
+            sent = emit("G", lambda q, p=pieces, f=send: f(q, p), ext(None), [A("zs", lo + 64 * pieces[0], lo + 64 * pieces[-1] + 64)],
+                        (2700 if t == 0 and len(pieces) == 2 else 400, 0, 0))
             chain("send")
         ops[-1]["send"] = t
+        if w4 < 16:
+            parents("p5", 12, 16)
+        hops(12, 16)
+        reached("Z", 12, 16)
+        for a, b, i in runs(0, S):
+            act(A("CMh", lo + a, lo + b), A("CM", lo + S + i, lo + S + i + b - a), Fn.Identity, scale=0.5)
         for h in range(lo + S, B, 512):
             act(A("X", O + h, O + min(h + 512, B)), A("XF", O + h, O + min(h + 512, B)), Fn.Identity, scale=0.0625)
         who(t + 1)
@@ -558,19 +653,16 @@ def build(T, rank, topo, core):
                 after(sent)
             if i % 2:
                 wrap(A("p6", 32 * i - 32, 32 * i + 32), "Wh", lambda r: A("Ch", 512 * i - 512 + r, 512 * i + 512, 16))
-        ts(A("lc", 0, 128), A("p6", 0, 128), float(O + 1024), Op.add)
+                ts(A("lc", 32 * i - 32, 32 * i + 32), A("p6", 32 * i - 32, 32 * i + 32), float(O + 1024), Op.add)
         if t == R - 2:
             for h in range(0, W, 512):
                 a = O + lo + S + h
                 act(A("CO", a, a + 512), A("C", a, a + 512), Fn.Identity, bias=1024.0)
-        act(A("junk", 0, 256), A("XA", O + lo, O + lo + S), Fn.Sign, bias=0.5, acc=col("ac", 1))
-        for i in range(2):
-            a = S + 896 * i
-            act(A("junk", a, a + 896), A("XA", O + lo + a, O + lo + a + 896), Fn.Sign, bias=0.5, acc=col("ac", 2 + i))
-        act(col("ac", 4), col("ac", 2), Fn.Identity, bias=col("ac", 3))
-        act(col("ac", 5), col("ac", 1), Fn.Identity, bias=1024.0 if t == 0 else col("ac", 6), scale=-0.5)
-        act(col("ac", 0), col("ac", 4), Fn.Identity, bias=col("ac", 5), scale=-0.5)
-        act(col("ac", 6), col("ac", 4), Fn.Identity, bias=128.0, scale=0.5)
+        mm(A("p0", 0, 128), A("BD", 0, 128), A("live", 0, 128), True, True)
+        act(A("UWi", 512, 640), A("p0", 0, 128), Fn.Identity, scale=-0.5, acc=col("ac", 1))
+        act(A("UWi", 640, 656), A("p0", 128 - c0, 144 - c0), Fn.Identity, bias=8.0, scale=-0.5, acc=col("ac", 3))
+        act(col("ac", 0), col("ac", 1), Fn.Identity, bias=1024.0 if t == 0 else col("ac", 2))
+        act(col("ac", 2), col("ac", 1), Fn.Identity, bias=col("ac", 3), scale=-1.0)
         gfill(A("XA", O + lo, O + lo + S), -512)
         after(sent)
         if t == 0:
@@ -579,8 +671,9 @@ def build(T, rank, topo, core):
         back("p2", "v4", "M1", 4)
         cp(A("tb", 0, 256), A("p2", 0, 256))
         back("p2", "tb", "M0", 1)
-        ts(A("D", O + B, O + B + S), A("p2", 0, 256), float(lo), Op.add)
-        back("p3", "v5", "M1", 4)
+        for a, b, i in runs(0, S):
+            ts(A("D", O + B + i, O + B + i + b - a), A("p2", a, b), float(lo), Op.add)
+        back("p3", v5, "M1", 4, 16)
         cp(A("tc", 0, 256), A("p3", 0, 256))
         back("p3", "tc", "M0", 1)
         act(A("dn", 0, 256), A("p3", 0, 256), Fn.Identity, bias=float(lo))
@@ -632,7 +725,7 @@ def schedule(ops):
     hazards(ops)
     n = len(ops)
     sends = {o["send"]: i for i, o in enumerate(ops) if "send" in o}
-    names, pre = {}, []
+    names, pre, older = {}, [], []
     for i, o in enumerate(ops):
         p = {j: 1 if j in o["wait"] else 0 for j in o["follow"]}
         for j in o["after"] + [j for j in range(min(i, 7)) if ops[j]["e"] == o["e"]]:
@@ -644,7 +737,11 @@ def schedule(ops):
             if name in names:
                 p.setdefault(names[name], 0)
             names[name] = i
-        pre.append(p)
+        cover = 0
+        for j in p:
+            cover |= older[j]
+        older.append(cover | sum(1 << j for j in p))
+        pre.append({j: k for j, k in p.items() if k == 2 or ops[j]["sem"] is not None or not cover >> j & 1})
     lat, zero, eng = [o["lat"] for o in ops], [0.0] * n, [o["e"] for o in ops]
 
     def paced(m):
@@ -711,24 +808,79 @@ def schedule(ops):
     for i in range(n):
         for j in pre[i]:
             post[j].append(i)
+    tail = [i for i in range(n) if not post[i]]
+
+    def held(seq, cost, before):
+        end, why, last = [0.0] * n, [None] * n, {}
+        for i in seq:
+            w = last.get(eng[i])
+            at = 0.0 if w is None else end[w]
+            for j, d in before[i]:
+                if end[j] + d > at:
+                    at, w = end[j] + d, j
+            end[i], why[i], last[eng[i]] = at + cost[i], w, i
+        i, pairs = max(tail, key=lambda x: end[x] + lat[x]), []
+        while why[i] is not None:
+            if not older[i] >> why[i] & 1:
+                pairs.append((why[i], i))
+            i = why[i]
+        return end, pairs
+
+    def again(seq, p, q, cost, before, was):
+        end, free, last = list(was), {}, q
+        for x in range(p - 1, -1, -1):
+            free.setdefault(eng[seq[x]], end[seq[x]])
+            if len(free) == 4 or x < p - 200:
+                break
+        for x in range(p, n):
+            i = seq[x]
+            at = free.get(eng[i], 0.0)
+            for j, d in before[i]:
+                if end[j] + d > at:
+                    at = end[j] + d
+            at += cost[i]
+            free[eng[i]] = at
+            if x > q + 60 and ops[i]["arr"] is not None:
+                return at - end[i]
+            if at != end[i]:
+                end[i], last = at, max(last, x)
+            elif x > last + 120:
+                return 0.0
+        return max(end[i] + lat[i] for i in tail) - max(was[i] + lat[i] for i in tail)
+
+    now, fresh, ends = best[:2], True, [held(best[1], c, b) for c, b in paces]
     for k in range(CFG["shakes"]):
-        key = list(best[2])
+        if fresh:
+            seq = sorted(now[1], key=lambda i: ends[0][0][i] - paces[0][0][i])
+            at = {x: p for p, x in enumerate(seq)}
+            best = min(best, now, key=lambda x: x[0])
         mix = (mix * 1103515245 + 12345) % 2147483648
-        i = (mix >> 8) % n
+        pairs = ends[k % len(paces)][1]
+        a, b = pairs[(mix >> 8) % len(pairs)]
         mix = (mix * 1103515245 + 12345) % 2147483648
-        step = CFG["span"] * (mix / 1073741824 - 1)
-        key[i] += step
-        todo = [i]
-        while todo:
-            j = todo.pop()
-            for x in (pre[j] if step < 0 else post[j]):
-                if (key[x] > key[j]) if step < 0 else (key[x] < key[j]):
-                    key[x] = key[j]
-                    todo.append(x)
-        seq = sorted(range(n), key=lambda i: (key[i], i))
-        score = sum(replay(seq, c, b) / m[0] for (c, b), m in zip(paces, PACE))
-        if score <= best[0] + CFG["heat"] * (1 - k / CFG["shakes"]):
-            best = (score, seq, key)
+        how, far = (mix >> 8) % 4, 1 + (mix >> 12 & 31) ** 3 // CFG["span"]
+        i, early = (b, True) if how == 0 else (a, how == 1)
+        if how == 3:
+            i, early = (mix >> 3) % n, mix >> 11 & 1
+        p = q = at[i]
+        while far and (p > 0 if early else q < n - 1):
+            p, q = (p - 1, q) if early else (p, q + 1)
+            far -= eng[seq[p if early else q]] == eng[i]
+        part = seq[p:q + 1]
+        tied = [x == i or (older[i] >> x & 1 if early else older[x] >> i & 1) for x in part]
+        new = seq[:p] + [x for x, y in zip(part, tied) if y == early] + [x for x, y in zip(part, tied) if y != early] + seq[q + 1:]
+        room, worse, fresh = CFG["heat"] * (1 - k / CFG["shakes"]) * (mix >> 20 & 7) / 4, 0.0, False
+        if [x for x in new[p:q + 1] if eng[x] == eng[i]] == [x for x in part if eng[x] == eng[i]]:
+            continue
+        for (c, b), m, (e, _) in zip(paces, PACE, ends):
+            worse += again(new, p, q, c, b, e) / m[0]
+            if worse > room + 200:
+                break
+        if worse <= room:
+            tried = [held(new, c, b) for c, b in paces]
+            score = sum(max(e[i] + lat[i] for i in tail) / m[0] for (e, _), m in zip(tried, PACE))
+            if score <= now[0] + room:
+                now, ends, fresh = (score, new), tried, True
     _ORDER["order"] = best[1]
     _ORDER["spans"] = [replay(best[1], c, b) for c, b in paces]
     return [ops[i] for i in best[1]]
@@ -789,7 +941,7 @@ def rank_program(g, core, T, topo):
             ins.then_inc(T.sem[o["sem"]], 16)
         elif o.get("sig"):
             ins.then_inc(T.sem["e" + o["e"]], 1)
-    for n in ("dya", "dyo", "dyy", "dyx", "dyc"):
+    for n in ("dya", "dyo", "dyy", "dyx", "dyc", "dyd"):
         g.wait_ge(T.sem[n], 16)
     for t in range(R - 1):
         g.wait_ge(T.sem["snt%d" % t], landed)

from concourse.bass import DstId, RemoteDMATransfer
from concourse.mybir import AluOpType as Op, ActivationFunctionType as Fn

W, S, R, ST, N = 2048, 256, 4, 341, 4
O = 528
Y0 = 0
PW = O + W + R * S
BF, F32, F16, I32, U16 = "bfloat16", "float32", "float16", "int32", "uint16"
MAGIC = 12582912.0
K3 = 65536.0
CFG = {"rows4": "SSVVSSVVSSVVSSVV", "rows5": "SSVVWWWWSSWWSSWW", "own": "VVSS", "own0": "VSVS", "ov": 24, "ov3": 32, "step": 16, "early": 12,
       "rows3": "SSVVSSVVSSVVSSSS", "post3": 12, "calls": 2, "pre": 2, "soon": "", "here": "L", "w4": 16, "c5": "S", "tries": 60, "turns": 2, "spread": 0.6, "mix": 1, "shakes": 20000, "span": 2000, "heat": 300.0}
PACE = [(0.83, 1.56, 3.8, 0.42, 110.0, 4200.0), (1.15, 1.8, 5.0, 0.58, 90.0, 4200.0),
        (0.88, 1.2, 2.5, 0.44, 190.0, 5500.0), (1.0, 1.5, 3.5, 0.55, 130.0, 2800.0)]

SCRATCH = {}


def _sb(name, cols, dtype):
    SCRATCH[name] = ("sbuf", [128] + (cols if isinstance(cols, list) else [cols]), dtype)


for _n, _c, _d in [
    ("X", PW + S, BF), ("XA", PW, BF), ("XF", PW, F32), ("C", PW, F32), ("D", PW, I32), ("CM", R * S, BF),
    ("cdi", 128, I32), ("cdf", 128, F32), ("cdh", 128, F16), ("agi", 48, I32), ("cdm", 128, BF),
    ("jrow", 256, F32), ("pi", 1, I32), ("pt", 4, I32), ("pc", 16, F32), ("XR", 896, BF),
    ("WS1", 144, BF), ("WSv", 144, BF), ("WSz", 144, BF), ("Wh", 144, F16), ("Ch", W, F16), ("CO", PW, F32),
    ("BD", 128, BF), ("BD2", 128, BF), ("live", 129, BF), ("I8", 128, BF), ("BDv", 128, BF), ("BDs", 128, BF), ("TL", 128, BF), ("TLn", 128, BF), ("Ub", 48, BF),
    ("Ip", 128, BF), ("In", 128, BF), ("Ih", 128, BF), ("If", 128, F16),
    ("M0", 4 * 160, F16), ("M1", 4 * 160, F16), ("UWi", 2048, BF), ("UW", 2048, F16), ("KI", 2048, F16),
    ("cV", 512, BF), ("cS", 512, BF), ("cH", 256, BF), ("cJ3", 256, F16), ("cJ4", 256, F16), ("cJ5", 256, F16), ("cF", 2 * R, BF),
    ("one", 256, F32), ("inc", 256, BF), ("cL", 9, BF), ("vv", 144, F32), ("Tw", 6672, F32), ("far", 9, BF), ("W32", 144, BF),
    ("segn", 256, F16), ("aw", 256, F32), ("ax", 256, F32), ("mk", 256, F32),
    ("p32", 128, F32), ("Kc", 256, F32), ("s1", 144, BF), ("sw", 16, F32),
    ("L16", 16, U16), ("sq", 128, F32), ("wi", 128, I32), ("wj", 128, I32), ("who", 128, U16), ("lc", 128, U16),
    ("Ed", W, BF), ("Gd", 1536, BF), ("Og", W, BF), ("E4", 4096, BF), ("E5", 4096, BF),
    ("hi", 32, I32), ("hj", 32, I32), ("uh", 32, F16),
    ("T1", 256, F32), ("T2", [16, 16], I32), ("c4", 256, I32), ("o4", 256, U16), ("c5", 256, F32), ("o5", 256, U16),
    ("F", 144, BF), ("Sb", 144, F16), ("lb", 16, U16),
    ("E3", 256, F16), ("U", 3, F32), ("lo1", 16, U16), ("lx", 16, U16), ("sm", 256, F16), ("avi", 256, I32),
    ("dg", 256, F16), ("ta", 256, F16), ("tb", 256, F16), ("tc", 256, F16),
    ("v4", [16, 16], F16), ("v50", 272, F16), ("v51", 272, F16), ("v52", 272, F16), ("v53", 272, F16), ("tr", 256, F16), ("tq", 320, F16), ("CMh", 3 * S, BF), ("mc", 32, F16),
    ("cn", 256, F32), ("xb", 256, BF), ("dn", 256, F32),
    ("th1", 48, F32), ("th2", 48, F32), ("cc", 192, F32), ("fl", 64, F32), ("wq", 64, F32),
    ("lh", 32, U16), ("hg", 512, F16), ("sc", 512, F16), ("lw", 16, U16),
    ("zs", 3 * S, BF), ("Z", 3 * S, BF), ("ac", 8, F32),
]:
    _sb(_n, _c, _d)
for _k in range(8):
    SCRATCH["p%d" % _k] = ("psum", [128, 512], F32)

DMA_SEMS = ["dx", "dx2", "dc0", "dcm", "dcd", "dag", "ddl", "drep", "dya", "dyo", "dyx", "dyy", "dyc", "dyd"]
SEMAPHORES = ["eV", "eS", "eP", "eG"] + DMA_SEMS + ["arr0", "arr1", "arr2", "snt0", "snt1", "snt2"]


def build(T, rank, topo, core):
    ops = []

    def view(a, name, lo, hi, n, tag=None):
        where, _, dtype = SCRATCH[name]
        return {"ap": a, "regs": [(name, lo, hi) if tag is None else (name, lo, hi, tag)], "rd": [], "n": n,
                "two": dtype in (BF, F16, U16), "ps": where == "psum", "ind": False}

    def A(n, a, b, st=1):
        if st == 1:
            return view(T[n][:, a:b], n, a, b, b - a)
        return view(T[n][:, a:b:st], n, a, b, (b - a + st - 1) // st)

    def lane(n, a, b, st):
        return view(T[n][:, a:b:st], n, a - a % st, b, (b - a + st - 1) // st, a % st)

    def block(n, k0, k1, j0, j1):
        return view(T[n][:, k0:k1, j0:j1], n, 16 * k0, 16 * k1, (k1 - k0) * (j1 - j0), None if j1 - j0 == 16 else j0)

    def ext(a):
        return {"ap": a, "regs": [], "rd": [], "n": 0, "two": False, "ps": False, "ind": False}

    def IND(w, o):
        return dict(w, ap=w["ap"].indirect(o["ap"]), regs=w["regs"] + o["regs"], n=16 * o["n"], ind=True)

    def SCT(w, o):
        return dict(w, ap=w["ap"].indirect(o["ap"]), rd=o["regs"], n=16 * o["n"], ind=True)

    def ap(x):
        return x["ap"] if isinstance(x, dict) else x

    def emit(e, f, out, ins, cost, lat=0.0, sem=None):
        rd = list(out["rd"])
        for x in ins:
            if isinstance(x, dict):
                rd += x["regs"]
        ops.append({"e": e, "f": f, "w": list(out["regs"]), "r": rd, "sem": sem, "arr": None, "c": cost, "lat": lat,
                    "after": []})
        return len(ops) - 1

    def vcost(out, full, both=False):
        if out["ind"]:
            return (50, out["n"], 2)
        if full and full[0]["ind"]:
            return (50, out["n"], 1)
        k = 0.5 if out["two"] and all(x["two"] for x in full) else 1.0
        if both and not any(x["ps"] for x in full):
            k *= 2
        return (40, max(64, out["n"] * k), 0)

    def ts(out, a, s1, op0, s2=None, op1=None):
        if op1 is None:
            return emit("V", lambda q: q.tensor_scalar(ap(out), ap(a), ap(s1), None, op0), out, [a, s1], vcost(out, [a]))
        return emit("V", lambda q: q.tensor_scalar(ap(out), ap(a), ap(s1), ap(s2), op0, op1), out, [a, s1, s2],
                    vcost(out, [a]))

    def tt(out, a, b, op):
        return emit("V", lambda q: q.tensor_tensor(ap(out), ap(a), ap(b), op), out, [a, b], vcost(out, [a, b], True))

    def cp(out, a):
        return emit("V", lambda q: q.tensor_copy(ap(out), ap(a)), out, [a], vcost(out, [a]))

    def fill(out, v):
        return emit("V", lambda q: q.memset(ap(out), v), out, [], vcost(out, []))

    def scan(out, d0, d1, op0, op1):
        return emit("V", lambda q: q.tensor_tensor_scan(ap(out), ap(d0), ap(d1), 0.0, op0, op1), out, [d0, d1],
                    vcost(out, [d0, d1]))

    def act(out, a, fn, bias=None, scale=None, acc=None):
        kw = {}
        if bias is not None:
            kw["bias"] = ap(bias)
        if scale is not None:
            kw["scale"] = ap(scale)
        o = out
        if acc is not None:
            kw["accum_out"] = ap(acc)
            o = dict(out, regs=out["regs"] + acc["regs"])
        cost = (65, out["n"], 2) if out["ind"] else (65, out["n"], 1) if a["ind"] else (60, max(64, out["n"]), 0)
        return emit("S", lambda q: q.activation(ap(out), ap(a), fn, **kw), o, [a, bias, scale], cost)

    def mms(calls):
        def run(q):
            return [q.matmul(ap(o), ap(l), ap(r), a, z) for o, l, r, a, z in calls][-1]
        out = dict(calls[0][0], regs=sorted(set(c[0]["regs"][0] for c in calls)))
        return emit("P", run, out, [x for c in calls for x in c[1:3]],
                    (0, sum(max(64, c[2]["n"]) * (1 if c[2]["two"] else 4) for c in calls), 3), 60.0)

    def mm(out, l, r, start, stop):
        return mms([(out, l, r, start, stop)])

    def iota(out, pat, base, cm, flag=True):
        cost = (130, 2 * out["n"], 0)
        if flag:
            return emit("G", lambda q: q.iota(ap(out), pat, base, cm, allow_small_or_imprecise_dtypes=True), out, [], cost)
        return emit("G", lambda q: q.iota(ap(out), pat, base, cm), out, [], cost)

    def gfill(out, v):
        return iota(out, [[0, out["n"]]], v, 0)

    def select(out, a, pat, op, base, cm, other=0.0):
        return emit("G", lambda q: q.affine_select(ap(out), ap(a), pat, op, other, base, cm), out, [a], (170, 2 * out["n"], 0))

    def dma(e, out, a, sem, kib):
        return emit(e, lambda q: q.dma_start(ap(out), ap(a)), out, [a], (60, 0, 0), 2000.0 + 5.6 * kib, sem=sem)

    def chain(name):
        ops[-1]["chain"] = name

    def after(i):
        ops[-1]["after"].append(i)

    def ws(n, r):
        return A(n, 15 - r, 143 - r)

    def wrap(out, n, rhs, start=True, stop=True, step=16):
        for h in range(0, 16, step):
            mms([(out, ws(n, r), rhs(r), start and r == 0, stop and r == 15) for r in range(h, h + step)])

    def unwrap(bank, src, at=0):
        return mms([(A(bank, at + r, at + 16 * src["n"], 16), A("UW", 128 * r, 128 * r + 128), src, True, True) for r in range(16)])

    def runs(a, b):
        cut = [a, b] if b - a == 64 else [a, S - first if a < S - first < b else 128, b]
        return [(x, y, (x + first) % S) for x, y in zip(cut, cut[1:])]

    def mshift(n, a, d):
        return A(n, 160 * a + 16 - d, 160 * a + 144 - d)

    def turn(bank, src, n, m, d, part=range(4)):
        k = n // 4
        mms([(A(bank, k * a, k * a + k), mshift(m, a, d * (b - a)), A(src, b, n, 4), b == 0, b == 3)
             for a in part for b in range(4)])

    def back(bank, src, m, d, at=0):
        mms([(A(bank, b, 256, 4), mshift(m, b, d * (a - b)),
              block(src, 4 * a, 4 * a + 4, 0, 16) if src == "v4" else A(src, at + 64 * a, at + 64 * a + 64), a == 0, a == 3)
             for b in range(4) for a in range(4)])

    def col(n, j):
        return A(n, j, j + 1)

    early, first = CFG["early"], 64 * (rank + 1) % S
    Ip, In, Ih, If = A("Ip", 0, 128), A("In", 0, 128), A("Ih", 0, 128), A("If", 0, 128)
    sw = A("sw", 0, 16)
    dma("Y", A("X", O, O + W // 2), ext(T.x0[:, 0:W // 2]), "dx", 300)
    dma("Y", A("X", O + W // 2, O + W), ext(T.x0[:, W // 2:W]), "dx2", 600)
    dma("S", A("CM", 0, S), ext(T.come[:, 0:S]), "dc0", 300)
    dma("S", A("cdi", 0, 128), ext(T.cd0[:]), "dcd", 450)
    dma("Y", A("agi", 0, 48), ext(T.age[:]), "dag", 700)
    dma("Y", A("D", O, O + W), ext(T.dl0[:]), "ddl", 1700)
    dma("Y", A("CM", S, R * S), ext(T.come[:, S:R * S]), "dcm", 1900)
    iota(A("pi", 0, 1), [[0, 1]], 0, 1, False)
    iota(A("jrow", 0, 256), [[1, 256]], 0, 0)
    iota(A("ax", 0, 128), [[16, 8], [0, 16]], 0, 0)
    iota(A("Kc", 0, 16 * CFG["w4"]), [[61, 16], [0, CFG["w4"]]], 7, 0)
    if CFG["w4"] < 16:
        iota(A("Kc", 192, 256), [[61, 16], [0, 4]], 7, 0)
    iota(A("s1", 0, 144), [[1, 144]], 0, 0)
    iota(A("aw", 0, 256), [[0, 16], [1, 16]], 0, 0)
    iota(A("wq", 0, 12), [[0, 4], [4, 3]], 0, 0)
    fill(A("UWi", 0, 512), 1.0)
    fill(A("cH", 0, 256), -0.5)
    fill(A("cV", 0, 512), 10.5 * K3)
    fill(A("cS", 0, 512), 2.5 * K3)
    gfill(A("XA", 0, O - 1), 0)
    gfill(A("XA", O - 1, O), -512)
    gfill(A("X", 2 * S, O), 0)
    gfill(A("C", 0, O), -1025)
    iota(A("D", 0, O), [[0, O]], -1, 0, False)
    gfill(A("one", 0, 256), 1)
    gfill(A("Sb", 0, 1), 0)
    gfill(A("Sb", 130, 144), W)
    gfill(lane("fl", 0, 64, 4), 0)
    fill(A("inc", 0, 256), 1.0 / 1024)
    fill(A("vv", 129, 144), 1024 + 129.125)
    gfill(A("F", 129, 130), 1)
    gfill(A("F", 130, 144), 0)
    for n, rows, w in (("cJ4", CFG["rows4"], CFG["w4"]), ("cJ5", CFG["rows5"], 16), ("cJ3", CFG["rows3"], 16)):
        iota(A(n, 0, 16 * w), [[0, 4], [-18592, 2], [0, 2 * w]], -13504, 0)
        for k in range(0, 16, 2):
            if (rows[k] == "S") != (k % 4 == 0):
                gfill(A(n, w * k, w * k + 2 * w), -13504 if rows[k] == "S" else -32096)
    if CFG["w4"] < 16:
        gfill(A("cJ4", 192, 256), -13504 if CFG["here"] == "L" else -32096)
    ts(col("pt", 0), col("pi", 0), 15, Op.bitwise_and)
    ts(col("pt", 1), col("pi", 0), 112, Op.bitwise_and)
    ts(col("pt", 2), col("pi", 0), 3, Op.bitwise_and)
    ts(col("pt", 3), col("pi", 0), 12, Op.bitwise_and)
    cp(col("pc", 0), col("pi", 0))
    ts(col("pc", 4), col("pi", 0), 16.0, Op.add)
    cp(A("pc", 1, 3), A("pt", 0, 2))
    ts(col("pc", 3), col("pt", 1), 15.0, Op.add)
    cp(A("pc", 5, 7), A("pt", 2, 4))
    act(col("pc", 7), col("pc", 1), Fn.Identity, bias=32.0 * (S - first), scale=32.0)
    ts(A("WS1", 0, 144), A("jrow", 0, 144), col("pc", 3), Op.is_equal)
    ts(Ip, A("jrow", 0, 128), col("pc", 0), Op.is_equal)
    ts(A("BD", 0, 128), A("ax", 0, 128), col("pc", 2), Op.is_equal)
    act(A("p32", 0, 128), A("jrow", 0, 128), Fn.Identity, bias=col("pc", 7), scale=512.0)
    act(sw, A("jrow", 0, 16), Fn.Identity, bias=col("pc", 1), scale=16.0)
    for n, src, k, v in (("Ih", "Ip", 128, 0.5), ("In", "Ip", 128, -1.0), ("BDv", "BD", 128, -K3), ("BDs", "BD", 128, -K3 / 2),
                         ("BD2", "BD", 128, 2.0), ("WSz", "WS1", 144, -512.0), ("WSv", "WS1", 144, 3104.0),
                         ("W32", "WS1", 144, 32.0), ("I8", "Ip", 128, 16384.0), ("TLn", "TL", 128, -1.0 / 1024)):
        if n == "TLn":
            select(A("TL", 0, 128), A("BD", 0, 128), [[1, 128]], Op.is_ge, 0, -1)
        act(A(n, 0, k), A(src, 0, k), Fn.Identity, scale=v)
    act(A("cL", 0, 8), A("sw", 0, 8), Fn.Identity, bias=1032.0, scale=8.0)
    act(col("cL", 8), col("pc", 1), Fn.Identity, bias=2064.0, scale=16.0)
    if CFG["w4"] < 16:
        act(A("wq", 16, 28), A("wq", 0, 12), Fn.Identity, bias=col("pc", 1))
        ts(A("wq", 32, 44), A("wq", 16, 28), 12.0, Op.is_ge, -12.0, Op.mult)
        tt(A("wq", 48, 60), A("wq", 32, 44), A("wq", 16, 28), Op.add)
        cp(A("L16", 0, 12), A("wq", 48, 60))
        ts(A("L16", 12, 16), A("one", 0, 4), 12.0, Op.mult, col("pc", 5), Op.add)
    else:
        ts(A("L16", 0, 16), A("jrow", 0, 16), 0.0, Op.mult, col("pc", 1), Op.add)
    ts(A("pc", 8, 12), A("jrow", 0, 4), col("pc", 5), Op.is_equal)
    ts(A("pc", 12, 16), A("jrow", 0, 16, 4), col("pc", 6), Op.is_equal)
    for a in range(4):
        ts(A("M0", 160 * a, 160 * a + 160), A("jrow", 0, 160), col("pc", 4), Op.is_equal, col("pc", 8 + a), Op.mult)
        ts(A("M1", 160 * a, 160 * a + 160), A("jrow", 0, 160), col("pc", 4), Op.is_equal, col("pc", 12 + a), Op.mult)
    for t in range(R):
        r0 = ST * (t + 1) % 16
        ts(A("v5%d" % t, 0, 16), sw, float(Y0 + S - O - S * t), Op.add)
        act(col("cF", 2 * t), col("pc", 1), Fn.Relu, bias=8192.0 * r0, scale=-8192.0)
        act(col("cF", 2 * t + 1), col("pc", 1), Fn.Relu, bias=8192.0 * (1 - r0), scale=8192.0)
    for h in range(0, W, 512):
        act(A("XF", O + h, O + h + 512), A("X", O + h, O + h + 512), Fn.Identity, scale=16.0)
    select(A("segn", 0, 256), A("XA", 0, 256), [[0, 16], [1, 16]], Op.not_equal, 0, 0, -60000.0)
    ts(A("mk", 0, 256), A("aw", 0, 256), col("pc", 1), Op.not_equal, -48976.0, Op.mult)
    ts(A("Wh", 0, 144), A("WS1", 0, 144), 0.0625, Op.mult)
    select(If, Ip, [[0, 128]], Op.is_ge, 0, 0)
    for h in range(0, W, 512):
        select(A("UW", h, h + 512), A("UWi", 0, 512), [[1, 4], [16, 8], [0, 16]], Op.is_equal, h // 128, -1)
        chain("wide")
    for h in range(0, W, 512):
        iota(A("CO", h, h + 512), [[61, 4], [0, 128]], 7 + 61 * (h // 128), 0)
        chain("wide")
        select(A("KI", h, h + 512), A("CO", h, h + 512), [[0, 4], [1, 128]], Op.is_equal, 0, -1)
    for t in range(R - 1):
        for a, b, i in runs(0, S):
            act(lane("cc", 64 * t + a // 4, 64 * t + b // 4, 4), A("sw", i // 16, (i + b - a) // 16), Fn.Identity, bias=float(W + S * t))
    cp(A("cdh", 0, 128), A("cdi", 0, 128))
    ts(A("cdf", 0, 128), A("cdi", 0, 128), -1024.0, Op.add)
    for r in range(16):
        dma("Y", view(T.C[r:128:16, O:O + W], "C", O, O + W, W, r), A("cdf", 0, 128), "drep", 64)
    turn("p6", "cdh", 128, "M0", 1)
    cp(A("ta", 0, 128), A("p6", 0, 128))
    turn("p6", "ta", 128, "M1", 4)
    ts(A("lc", 0, 128), A("p6", 0, 128), float(O), Op.add)
    ts(A("cdm", 0, 128), A("p6", 0, 128), 0.0, Op.is_lt, 32768.0, Op.mult)

    def ages():
        ts(A("tc", 0, 48), A("agi", 0, 48), -1024.0, Op.add)
        turn("p1", "tc", 48, "M0", 1)
        cp(A("tb", 0, 48), A("p1", 0, 48))
        turn("p1", "tb", 48, "M1", 4)
        for t in range(R - 1):
            oldest = W + S * t + S - 1 - 1024
            for n, less in (("th1", S * t), ("th2", 1024)):
                for a, b, i in runs(0, S):
                    act(A(n, 16 * t + a // 16, 16 * t + b // 16), A("p1", 16 * t + i // 16, 16 * t + (i + b - a) // 16),
                        Fn.Identity, bias=float(oldest - less), scale=-1.0)

    def who(t):
        lo = S * t
        for a, b, bank in ([(0, 64, "p7"), (64, 128, "p2")] if t == 0 else [(0, 128, "p7")]):
            wrap(A(bank, a, b), "WS1", lambda r: A("X", O + lo + 16 * a + r, O + lo + 16 * b, 16))
            act(A("sq", a, b), A(bank, a, b), Fn.Square)
            tt(A("wi", a, b), A("sq", a, b), A("p32", a, b), Op.add)
            ts(A("wj", a, b), A("wi", a, b), 5, Op.arith_shift_right, S - 1, Op.bitwise_and)
            cp(A("who", a, b), A("wj", a, b))

    def pre_terms(t):
        lo = S * t
        bank = "p7" if t else "p3"
        mms([(A(bank, 0, 256), Ih, A("cH", 0, 256), True, False)] +
            [(A(bank, a, b), Ih, A("CM", lo + i, lo + i + b - a), False, t == 0 and b == S) for a, b, i in runs(0, S)])

    def copy(out, a):
        return select(out, a, [[0, a["n"]]], Op.is_ge, 0, 0)

    def judge_parts(E, off, ys, y, win, cj, w=16, at=0):
        def vrow(k, n):
            a, b = at + w * k, at + w * (k + n)
            tt(A(E, 16 * a, 16 * b), IND(win, A(off, a, b)), A(ys, y, y + 16 * w * n), Op.is_ge)
            chain("V")

        def srows(k, n=2):
            h, pb, a, b = 512 * flip[0], ("p2", "p3", "p0")[flip[0]], at + w * k, at + w * (k + n)
            flip[0] = (flip[0] + 1) % 3
            act(A("Gd", h, h + 16 * w * n), IND(win, A(off, a, b)), Fn.Identity)
            chain("S")
            mm(A(pb, 0, 16 * w * n), In, A(ys, y, y + 16 * w * n), True, False)
            mm(A(pb, 0, 16 * w * n), Ip, A("Gd", h, h + 16 * w * n), False, True)
            signs()
            due.append((A(E, 16 * a, 16 * b), A(pb, 0, 16 * w * n)))

        def const(bank, k0, k1):
            mm(A(bank, at + w * k0, at + w * k1), If, A(cj, at + w * k0, at + w * k1), True, False)

        def count(bank, k0, k1, stop):
            a, b = at + w * k0, at + w * k1
            wrap(A(bank, a, b), "WSv", lambda r: A(E, 16 * a + r, 16 * b, 16), False, stop)

        def rows(own, k0, k1):
            for k in range(k0, k1):
                if own[k] == "V":
                    vrow(k, 1)
                elif own[k] in "LM":
                    if k % 8 == 0:
                        srows(k, 8) if own[k] == "L" else vrow(k, 8)
                elif k % 2 == 0:
                    srows(k) if own[k] == "S" else vrow(k, 2)

        return rows, const, count

    flip, due = [0], []

    def signs():
        while due:
            act(*due.pop(), Fn.Sign, bias=0.5)
            chain("S")

    def tree(v, bank, c, k0, k1, tmp, to, out, more=0, w=16, at=0):
        a, b = at + w * k0, at + w * k1
        tt(A(v, 16 + a, 16 + b), A(bank, a, b), A(c, a, b), Op.min)
        src, a, n = v, 16 + a - w * more, k1 - k0 + more
        while n > 1:
            h = (n + 1) // 2
            top = out if h == 1 and out is not None else A(tmp, to, to + w * h)
            tt(top, A(src, a, a + w * h), A(src, a + w * (n - h), a + w * n), Op.max)
            src, a, n, to = tmp, to, h, to + w * h
        return top

    def places(t, j0, j1):
        a, b = 16 * j0, 16 * j1
        if t == 0:
            tt(A("T1", 0, 256), IND(A("hj", 16, 32), A("L16", 0, 16)), A("Kc", 0, 256), Op.mult)
            tt(A("avi", 0, 256), IND(A("hj", 0, 16), A("L16", 0, 16)), A("T1", 0, 256), Op.add)
        elif j0 == 0:
            for h in range(0, 16, 4):
                mms([c for m in range(h, h + 4) for c in (
                    (A("p7", 16 * m, 16 * m + 16), A("KI", 128 * m, 128 * m + 128), A("uh", 16, 32), True, False),
                    (A("p7", 16 * m, 16 * m + 16), If, A("uh", 0, 16), False, True))])
            ts(block("T2", 0, 16, 0, 16), A("p7", 0, 256), col("ac", 0), Op.add)
        ts(A("c4", a, b), block("T2", 0, 16, j0, j1) if t else A("avi", a, b), W - 1, Op.bitwise_and)
        ts(A("o4", a, b), A("c4", a, b), 16.0, Op.add)

    counts = ("p0", "p1", "p4", "p5")
    pre_terms(0)

    for t in range(R):
        lo, B = S * t, W + S * t
        last = t == R - 1
        c0 = ST * (t + 1) // 16
        w4 = 16 if last else CFG["w4"]
        xa = A("XR", 192, 448)
        if t > 0:
            mm(A("p7", 0, 256), In, A("Z", lo - S, lo), False, True)
            ops[-1]["arr"] = t - 1
        ts(xa, A("p7" if t else "p3", 0, 256), MAGIC, Op.add, MAGIC, Op.subtract)
        if t == 0:
            who(0)
        wrap(A("p7", 16, 32), "W32", lambda r: A("XR", 192 + r, 448, 16))
        act(A("p7", 0, 16), A("p7", 16, 32), Fn.Square, scale=1.0 / 32)
        cp(A("hi", 0, 32), A("p7", 0, 32))
        ts(A("hj", 0, 32), A("hi", 0, 32), 5, Op.arith_shift_right, W - 1, Op.bitwise_and)
        if t > 0:
            cp(A("uh", 0, 32), A("hj", 0, 32))
        if w4 == 16:
            copy(A("XR", 448, 704), xa)
        else:
            copy(A("XR", 0, 192), A("XR", 192, 384))
            for h in (64, 128, 256):
                copy(A("XR", 384 + h, 384 + 2 * h), A("XR", 384, 384 + h))
        for a, b, i in runs(0, S):
            copy(A("X", O + B + i, O + B + i + b - a), A("XR", 192 + a, 192 + b))
        diffs = ["p2", "p3"]
        for i, e in enumerate(CFG["own" if t else "own0"]):
            a, bank = O + lo + 512 * i, counts[i]
            ed, names, old = A("Ed", 512 * i, 512 * i + 512), A("who", 32 * i, 32 * i + 32), A("X", a, a + 512)
            known = min(512, O + B - S - a)
            mms([(A(bank, 0, 512), Ip, A("cV" if e == "V" else "cS", 0, 512), True, False)] +
                ([(A(bank, 0, known), A("BD2", 0, 128), A("XA", a, a + known), False, False)] if t > 0 else []))
            soon = t and e in CFG["soon"]
            got = IND(A("Z", lo - S, lo), names) if soon else IND(xa, names)
            half = IND(A("CMh", lo - S, lo), names) if soon else None
            if e == "V":
                tt(ed, got, old, Op.is_ge)
            else:
                pb = diffs.pop(0)
                diffs.append(pb)
                gd = A("Gd", 0, 512) if pb == "p2" else A("Gd", 512, 1024)
                mm(A(pb, 0, 512), In, old, True, False)
                if soon:
                    act(A("E5", 512 * i, 512 * i + 512), half, Fn.Identity)
                    mm(A(pb, 0, 512), Ip, A("E5", 512 * i, 512 * i + 512), False, False)
                act(gd, got, Fn.Identity)
                ops[-1]["arr"] = t - 1 if soon else None
                mm(A(pb, 0, 512), In if soon else Ip, gd, False, True)
                act(ed, A(pb, 0, 512), Fn.Sign, bias=0.25)
            mm(A(bank, 0, 512), A("BDv" if e == "V" else "BDs", 0, 128), ed, False, True)
            tt(A("XA", a, a + 512), A(bank, 0, 512), old, Op.min)
        places(t, 0, w4 if t else 16)
        wall = A("XA", 0, O + B)
        win = A("XA", lo + O - 16, O + B)
        ov = CFG["ov3" if last else "ov"]
        cuts = sorted(set(range(0, 128 - ov, 32)) | {128 - ov, 128})
        for a, b in zip(cuts, cuts[1:]):
            got = IND(A("XA", 0, O + lo + 16 * b), A("lc", a, b))
            if a >= 128 - ov:
                ts(A("Og", 16 * a, 16 * b), got, 0.0, Op.min, -1.0, Op.max)
            else:
                act(A("Og", 16 * a, 16 * b), got, Fn.Sign, bias=0.5)

        def cyclic(a, b, bank="p6"):
            return A(bank, a - c0, b - c0) if a >= c0 else A(bank, a + 128 - c0, b + 128 - c0)
        mms([(A("p6", 0, 129), In, A("XA", 0, 129), True, False), (A("p6", 0, 129, 128), In, A("cF", 2 * t, 2 * t + 2), False, False)])
        if t == 0:
            mms([(cyclic(a, b), In, A("cdm", a, b), False, False) for a, b in ((0, c0 + 1), (c0, 128))])
        for a, b in ((0, c0 + 1), (c0, 128)):
            wrap(cyclic(a, b, "p6" if last else "p0"), "WS1", lambda r: A("XA", O + lo + 16 * a + r, O + lo + 16 * b, 16),
                 not last, not last)
        if not last:
            act(A("live", 0, 129), A("p0", 0, 129), Fn.Sign, bias=0.5)
            mm(A("p6", 0, 129), A("I8", 0, 128), A("live", 0, 129), False, False)
        for a, b in [(0, c0 + 1)] + ([(c0, 64), (64, 128)] if c0 < 32 else [(c0, 128)]):
            wrap(cyclic(a, b), "WSz", lambda r: A("Og", 16 * a + r, 16 * b, 16), False, b == 128)
        F = A("F", 0, 129)
        ts(F, A("p6", 0, 129), 6000.0 if last else 20000.0, Op.is_ge)
        gfill(A("Tw", 0, S), 0)
        mm(A("p6", 0, 129), A("BD", 0, 128), F, True, True)
        mm(A("p1", 0, 9), In, A("cL", 0, 9), True, False)
        wrap(A("p1", 0, 9), "WSv", lambda r: A("F", r, 144, 16), False, True)
        act(A("far", 0, 9), A("p1", 0, 9), Fn.Relu, scale=-2.0)
        mms([(A("p7", 0, 129), Ip, A("s1", 0, 129), True, False), (A("p7", 0, 129), A("TLn", 0, 128), F, False, True)])
        scan(A("Sb", 1, 130), A("p6", 0, 129), A("one", 0, 129), Op.add, Op.mult)
        act(A("vv", 0, 129), A("p7", 0, 129), Fn.Identity, bias=1024.5 + 0.5 / 1024)
        wrap(A("p6", 0, 9), "Wh", lambda r: A("Sb", r, 144, 16), True, False)
        mm(A("p6", 0, 9), Ip, A("far", 0, 9), False, True)
        cp(A("lb", 0, 9), A("p6", 0, 9))
        cp(SCT(A("Tw", 0, 6672), A("lb", 0, 9)), A("vv", 0, 144))
        scan(A("E3", 0, 256), A("inc", 0, 256), A("Tw", 0, 256), Op.add, Op.max)
        base = float(O + lo + 16 * c0)
        cp(A("U", 0, 2), A("Sb", 128 - c0, 130, c0 + 1))
        ts(A("Ub", 0, 16), sw, col("U", 1), Op.is_ge, -(base + 16.0) / 16, Op.mult)
        ts(A("Ub", 16, 32), sw, col("U", 0), Op.is_ge, -128.0, Op.mult)
        act(col("U", 2), col("U", 1), Fn.Identity, scale=-1.0 / 16)
        act(A("Ub", 32, 48), sw, Fn.Relu, bias=col("U", 2), scale=1.0 / 16)
        mms([(A("p6", 0, 16), Ip, A("Ub", 16 * i, 16 * i + 16), i == 0, False) for i in range(3)])
        wrap(A("p6", 0, 16), "Wh", lambda r: A("E3", r, 256, 16), False, True)
        slots = A("lo1", 0, 16)
        ts(slots, A("p6", 0, 16), 16.0, Op.mult, base - 16384.0, Op.add)
        ts(A("dg", 0, 256), IND(A("D", 0, O + B), slots), float(-lo), Op.add, -1.0, Op.max)
        yy = A("X", Y0, Y0 + S)
        act(yy, IND(wall, slots), Fn.Identity)
        copy(A("X", S, 2 * S), yy)
        turn("p7", "dg", 256, "M0", 1)
        cp(A("ta", 0, 256), A("p7", 0, 256))
        for bank, h in (("p6", 0), ("p7", 128)):
            turn(bank, "ta", 256, "M1", 4, range(h // 64, h // 64 + 2))
            ts(A("o5", h, h + 128), A(bank, h, h + 128), 16.0, Op.add)
            if CFG["c5"] == "S":
                act(A("c5", h, h + 128), A(bank, h, h + 128), Fn.Identity)
            else:
                cp(A("c5", h, h + 128), A(bank, h, h + 128))
        if t > 0 and w4 < 16:
            places(t, 12, 16)
        rows4, const, count = judge_parts("E4", "o4", "XR", 192 if w4 == 16 else 0, win, "cJ3" if last else "cJ4", w4)
        rows5, const5, count5 = judge_parts("E5", "o5", "X", Y0, win, "cJ5")
        const("p4", 0, 16)
        own, post = (CFG["rows3"], CFG["post3"]) if last else (CFG["rows4"], 16)
        rows4(own, 0, post)
        signs()
        rows5(CFG["rows5"], 0, 16)
        signs()
        rows4(own, post, 16)
        signs()
        for k in range(0, 16, 4):
            count("p4", k, k + 4, k == 12)

        def parents(bank, j0, j1):
            w, to, m4 = j1 - j0, 16 * j0, A("mc", j0, j1)
            tt(block("v4", 0, 16, j0, j1), A(bank, to, to + 16 * w), A("c4", to, to + 16 * w), Op.min)
            tt(A("tr", to, to + 8 * w), block("v4", 0, 8, j0, j1), block("v4", 8, 16, j0, j1), Op.max)
            for n in (4 * w, 2 * w, w):
                tt(m4 if n == w else A("tr", to + 2 * n, to + 3 * n), A("tr", to, to + n), A("tr", to + n, to + 2 * n), Op.max)
                to += 2 * n
            if not last:
                ts(A("lh", j0, j1), m4, float(lo + O), Op.add)
                ts(lane("cc", 64 * t + 4 * j0 + 1, 64 * t + 4 * j1, 4), m4, float(lo), Op.add)
                tt(lane("fl", 4 * j0 + 1, 4 * j1, 4), m4, A("th1", 16 * t + j0, 16 * t + j1), Op.is_lt)
            if j1 < 16:
                return
            unwrap(bank, A("mc", 0, 16))
            if not last:
                act(A("T1", 0, 256), A(bank, 0, 256), Fn.Relu, bias=float(lo + 1))
            for a, b, i in runs(0, S):
                if last:
                    ts(A("CO", O + B + i, O + B + i + b - a), A(bank, a, b), float(lo), Op.add, -1.0, Op.max)
                else:
                    act(A("C", O + B + i, O + B + i + b - a), A("T1", a, b), Fn.Identity, bias=-1025.0)
        if t == 0:
            ages()
        parents("p4", 0, w4)
        const5("p5", 0, early)
        const5("p1", early, 16)
        for k in range(0, early, 4):
            count5("p5", k, min(k + 4, early), k + 4 >= early)
        v5 = "v5%d" % t
        top = tree(v5, "p5", "c5", 0, early, "tq", 0, None, 1)
        count5("p1", early, 16, True)
        tt(A("mc", 16, 32), top, tree(v5, "p1", "c5", early, 16, "tq", 256, None), Op.max)
        if w4 < 16:
            rows4, const, count = judge_parts("E4", "o4", "XR", 384, win, "cJ4", 4, 192)
            rows4(16 * CFG["here"], 0, 16)
            signs()
            const("p5", 0, 16)
            count("p5", 0, 16, True)
        ts(A("lx", 0, 16), A("mc", 16, 32), float(lo + O - S), Op.add)
        xb = IND(A("X", S, O + B), A("lx", 0, 16))
        unwrap("p6", A("mc", 16, 32))
        if last:
            tt(A("sm", 0, 256), xb, yy, Op.add)
            ts(A("avi", 0, 256), A("sm", 0, 256), 0.5, Op.mult, -0.25, Op.add)
            ts(A("cn", 0, 256), A("p6", 0, 256), float(lo), Op.add, -1.0, Op.max)
            wrap(A("p0", 0, 128), "WS1", lambda r: A("XA", O + lo + 128 * r, O + lo + 128 * r + 128))
            ts(A("cdf", 0, 128), A("p0", 0, 128), 0.0, Op.is_ge)
            dma("Y", ext(T.ya[:, 0:W]), A("cdf", 0, 128), "dya", 64)
            dma("Y", ext(T.ya[:, W:W + S]), view(T.one[0:8, 0:256], "one", 0, 256, 256), "dyo", 8)
            dma("Y", ext(T.yx[:, W:W + S]), A("X", O + B, O + B + S), "dyy", 64)
            cp(SCT(A("X", 0, O + B), slots), A("avi", 0, 256))
            dma("Y", ext(T.yx[:, 0:W]), A("X", O + lo, O + B), "dyx", 512)
            cp(SCT(A("CO", 0, O + B), slots), A("cn", 0, 256))
            dma("S", ext(T.yc[:, 0:W]), view(T.CO[0:128:16, O + lo:O + B], "CO", O + lo, O + B, W), "dyc", 72)
            dma("S", ext(T.yc[:, W:W + S]), view(T.CO[0:128:16, O + B:PW], "CO", O + B, PW, S), "dyd", 16)
            break
        ts(A("cn", 0, 256), A("p6", 0, 256), float(lo - 1024), Op.add, -1025.0, Op.max)
        cp(SCT(A("C", 0, O + B), slots), A("cn", 0, 256))
        mms([(A("p7", 0, 256), Ih, yy, True, False), (A("p7", 0, 256), Ih, A("cH", 0, 256), False, False)])
        act(A("xb", 0, 256), xb, Fn.Identity)
        mm(A("p7", 0, 256), Ih, A("xb", 0, 256), False, True)
        act(A("aw", 0, 256), A("p7", 0, 256), Fn.Identity, bias=MAGIC)
        act(A("ax", 0, 256), A("aw", 0, 256), Fn.Identity, bias=-16 * MAGIC, scale=16.0)
        act(SCT(A("XF", 0, O + B), slots), A("ax", 0, 256), Fn.Silu)
        ops[-1]["c"] = (65 if t else 1365, S, 2)
        act(A("XF", O + B, O + B + S), A("X", O + B, O + B + S), Fn.Identity, scale=16.0)

        def hops(j0, j1):
            for h in range(2):
                a, b = 256 * h + 16 * j0, 256 * h + 16 * j1
                tt(A("hg", a, b), IND(A("C", 0, O + B), A("lh", 16 * h + j0, 16 * h + j1)), A("mk", 0, b - a), Op.add)
                scan(A("sc", a, b), A("segn", 0, b - a), A("hg", a, b), Op.add, Op.max)
                ends = A("sc", a + 15, b, 16)
                if h == 0:
                    ts(A("lh", 16 + j0, 16 + j1), ends, float(O + 1024), Op.add)
                ts(lane("cc", 64 * t + 4 * j0 + 2 + h, 64 * t + 4 * j1, 4), ends, 1024.0, Op.add)
                tt(lane("fl", 4 * j0 + 2 + h, 4 * j1, 4), ends, A("th2", 16 * t + j0, 16 * t + j1), Op.is_lt)
            scan(A("wq", 4 * j0, 4 * j1), A("fl", 4 * j0, 4 * j1), A("cc", 64 * t + 4 * j0, 64 * t + 4 * j1), Op.mult, Op.max)
            ts(A("lw", j0, j1), A("wq", 4 * j0 + 3, 4 * j1, 4), float(-lo), Op.add)

        def reached(out, j0, j1):
            ts(A(out, lo + 16 * j0, lo + 16 * j1), IND(A("XF", O + lo, O + B + S), A("lw", j0, j1)), -1.0 / 32, Op.mult)

        def send(q, pieces, t=t):
            trs, to = [], [T.cores[(rank + 1 + k) % N] for k in pieces]
            free = [e for e in topo.engines(core, to[0]) if all(e in topo.engines(core, c) for c in to)]
            share = len(free) // len(to)
            for i, k in enumerate(pieces):
                rid, pid, _ = topo.addr(to[i])
                trs.append(RemoteDMATransfer(
                    dst_ids=[DstId(rid=rid, pnc=pid)], dma_engine_mask=sum(1 << e for e in free[share * i:share * i + share]),
                    remote_sem=T.sem["arr%d" % t], src=T.zs[:, S * t + 64 * k:S * t + 64 * k + 64],
                    dst=T.Z[:, S * t + 64 * (2 - k):S * t + 64 * (3 - k)]))
            return q.remote_dma_fused(trs, local_sem=T.sem["snt%d" % t])
        hops(0, 12)
        for pieces in ((0, 1), (2,)):
            reached("zs", 4 * pieces[0], 4 * pieces[-1] + 4)
            sent = emit("G", lambda q, p=pieces, f=send: f(q, p), ext(None), [A("zs", lo + 64 * pieces[0], lo + 64 * pieces[-1] + 64)],
                        (2700 if t == 0 and len(pieces) == 2 else 400, 0, 0))
            chain("send")
        ops[-1]["send"] = t
        if w4 < 16:
            parents("p5", 12, 16)
        hops(12, 16)
        reached("Z", 12, 16)
        for a, b, i in runs(0, S):
            act(A("CMh", lo + a, lo + b), A("CM", lo + S + i, lo + S + i + b - a), Fn.Identity, scale=0.5)
        for h in range(lo + S, B, 512):
            act(A("X", O + h, O + min(h + 512, B)), A("XF", O + h, O + min(h + 512, B)), Fn.Identity, scale=0.0625)
        who(t + 1)
        for i in range(4):
            a = O + lo + S + 512 * i
            select(A("Ch", 512 * i, 512 * i + 512), A("C", a, a + 512), [[0, 512]], Op.is_ge, 0, 0)
            if i >= CFG["pre"]:
                after(sent)
            if i % 2:
                wrap(A("p6", 32 * i - 32, 32 * i + 32), "Wh", lambda r: A("Ch", 512 * i - 512 + r, 512 * i + 512, 16))
                ts(A("lc", 32 * i - 32, 32 * i + 32), A("p6", 32 * i - 32, 32 * i + 32), float(O + 1024), Op.add)
        if t == R - 2:
            for h in range(0, W, 512):
                a = O + lo + S + h
                act(A("CO", a, a + 512), A("C", a, a + 512), Fn.Identity, bias=1024.0)
        mm(A("p0", 0, 128), A("BD", 0, 128), A("live", 0, 128), True, True)
        act(A("UWi", 512, 640), A("p0", 0, 128), Fn.Identity, scale=-0.5, acc=col("ac", 1))
        act(A("UWi", 640, 656), A("p0", 128 - c0, 144 - c0), Fn.Identity, bias=8.0, scale=-0.5, acc=col("ac", 3))
        act(col("ac", 0), col("ac", 1), Fn.Identity, bias=1024.0 if t == 0 else col("ac", 2))
        act(col("ac", 2), col("ac", 1), Fn.Identity, bias=col("ac", 3), scale=-1.0)
        gfill(A("XA", O + lo, O + lo + S), -512)
        after(sent)
        if t == 0:
            gfill(A("XA", O - 1, O), 0)
            after(sent)
        back("p2", "v4", "M1", 4)
        cp(A("tb", 0, 256), A("p2", 0, 256))
        back("p2", "tb", "M0", 1)
        for a, b, i in runs(0, S):
            ts(A("D", O + B + i, O + B + i + b - a), A("p2", a, b), float(lo), Op.add)
        back("p3", v5, "M1", 4, 16)
        cp(A("tc", 0, 256), A("p3", 0, 256))
        back("p3", "tc", "M0", 1)
        act(A("dn", 0, 256), A("p3", 0, 256), Fn.Identity, bias=float(lo))
        cp(SCT(A("D", 0, O + B), slots), A("dn", 0, 256))
        pre_terms(t + 1)
    return ops


def _meet(a, b):
    if a[2] <= b[1] or b[2] <= a[1]:
        return False
    return len(a) < 4 or len(b) < 4 or a[3] == b[3]


def hazards(ops):
    seen = {}
    for i, o in enumerate(ops):
        o["key"] = o["sem"] if o["sem"] is not None else o["e"]
        follow, wait = set(), set()
        for kind in ("r", "w"):
            for reg in set(o[kind]):
                psum = SCRATCH[reg[0]][0] == "psum"
                for (j, k2, reg2) in seen.get(reg[0], []):
                    other = ops[j]["key"] != o["key"]
                    if psum:
                        if other or o["e"] == "P":
                            follow.add(j)
                        if other:
                            wait.add(j)
                    elif (kind == "w" or k2 == "w") and _meet(reg, reg2):
                        follow.add(j)
                        if other or o["sem"] is None:
                            wait.add(j)
        for kind in ("r", "w"):
            for reg in set(o[kind]):
                old = seen.setdefault(reg[0], [])
                if SCRATCH[reg[0]][0] == "psum" and o["e"] == "P":
                    old[:] = []
                old.append((i, kind, reg))
        o["follow"], o["wait"] = follow, wait


_ORDER = {}


def schedule(ops):
    if "order" in _ORDER:
        return [ops[i] for i in _ORDER["order"]]
    hazards(ops)
    n = len(ops)
    sends = {o["send"]: i for i, o in enumerate(ops) if "send" in o}
    names, pre, older = {}, [], []
    for i, o in enumerate(ops):
        p = {j: 1 if j in o["wait"] else 0 for j in o["follow"]}
        for j in o["after"] + [j for j in range(min(i, 7)) if ops[j]["e"] == o["e"]]:
            p.setdefault(j, 0)
        if o["arr"] is not None:
            p[sends[o["arr"]]] = 2
        name = "dma" + o["e"] if o["sem"] is not None else o.get("chain")
        if name is not None:
            if name in names:
                p.setdefault(names[name], 0)
            names[name] = i
        cover = 0
        for j in p:
            cover |= older[j]
        older.append(cover | sum(1 << j for j in p))
        pre.append({j: k for j, k in p.items() if k == 2 or ops[j]["sem"] is not None or not cover >> j & 1})
    lat, zero, eng = [o["lat"] for o in ops], [0.0] * n, [o["e"] for o in ops]

    def paced(m):
        unit = (m[0], m[0] * m[1], m[0] * m[2], m[3])
        cost = [o["c"][0] + o["c"][1] * unit[o["c"][2]] for o in ops]
        return cost, [[(j, (0.0, lat[j] + m[4], m[5])[k]) for j, k in p.items()] for p in pre]
    paces = [paced(m) for m in PACE]

    def replay(seq, cost, before):
        end, free = [0.0] * n, {}
        for i in seq:
            at = free.get(eng[i], 0.0)
            for j, d in before[i]:
                if end[j] + d > at:
                    at = end[j] + d
            end[i] = free[eng[i]] = at + cost[i]
        return max(end[i] + lat[i] for i in range(n))

    def place(rank, cost, links, head):
        end = [0.0] * n
        busy = {e: ([], []) for e in "VSPGY"}
        for i in sorted(range(n), key=rank):
            c, at = cost[i], head[i]
            for j, d in links[i]:
                if end[j] + d > at:
                    at = end[j] + d
            starts, ends = busy[eng[i]]
            a, b = 0, len(ends)
            while a < b:
                mid = (a + b) // 2
                if ends[mid] <= at:
                    a = mid + 1
                else:
                    b = mid
            while a < len(starts) and starts[a] < at + c:
                at = max(at, ends[a])
                a += 1
            starts.insert(a, at)
            ends.insert(a, at + c)
            end[i] = at + c
        return end

    mix, best = CFG["mix"], None
    for k in range(CFG["tries"]):
        cost, before = paces[k % len(paces)]
        edges = [[] for _ in ops]
        for i in range(n):
            for j, d in before[i]:
                edges[j].append((i, d))
        way = [0.0] * n
        for i in range(n - 1, -1, -1):
            mix = (mix * 1103515245 + 12345) % 2147483648
            way[i] = cost[i] * (1 + CFG["spread"] * (mix / 2147483648 - 0.5)) + max([lat[i]] + [d + way[j] for j, d in edges[i]])
        end = place(lambda i: (-way[i], i), cost, before, zero)
        for turn in range(CFG["turns"] + 1):
            if turn:
                rev = place(lambda i: (-end[i], -i), cost, edges, lat)
                end = place(lambda i: (-rev[i], i), cost, before, zero)
            seq = sorted(range(n), key=lambda i: (end[i] - cost[i], i))
            score = sum(replay(seq, c, b) / m[0] for (c, b), m in zip(paces, PACE))
            if best is None or score < best[0]:
                best = (score, seq, [end[i] - cost[i] for i in range(n)])
    post = [[] for _ in ops]
    for i in range(n):
        for j in pre[i]:
            post[j].append(i)
    tail = [i for i in range(n) if not post[i]]

    def held(seq, cost, before):
        end, why, last = [0.0] * n, [None] * n, {}
        for i in seq:
            w = last.get(eng[i])
            at = 0.0 if w is None else end[w]
            for j, d in before[i]:
                if end[j] + d > at:
                    at, w = end[j] + d, j
            end[i], why[i], last[eng[i]] = at + cost[i], w, i
        i, pairs = max(tail, key=lambda x: end[x] + lat[x]), []
        while why[i] is not None:
            if not older[i] >> why[i] & 1:
                pairs.append((why[i], i))
            i = why[i]
        return end, pairs

    def again(seq, p, q, cost, before, was):
        end, free, last = list(was), {}, q
        for x in range(p - 1, -1, -1):
            free.setdefault(eng[seq[x]], end[seq[x]])
            if len(free) == 4 or x < p - 200:
                break
        for x in range(p, n):
            i = seq[x]
            at = free.get(eng[i], 0.0)
            for j, d in before[i]:
                if end[j] + d > at:
                    at = end[j] + d
            at += cost[i]
            free[eng[i]] = at
            if x > q + 60 and ops[i]["arr"] is not None:
                return at - end[i]
            if at != end[i]:
                end[i], last = at, max(last, x)
            elif x > last + 120:
                return 0.0
        return max(end[i] + lat[i] for i in tail) - max(was[i] + lat[i] for i in tail)

    now, fresh, ends = best[:2], True, [held(best[1], c, b) for c, b in paces]
    for k in range(CFG["shakes"]):
        if fresh:
            seq = sorted(now[1], key=lambda i: ends[0][0][i] - paces[0][0][i])
            at = {x: p for p, x in enumerate(seq)}
            best = min(best, now, key=lambda x: x[0])
        mix = (mix * 1103515245 + 12345) % 2147483648
        pairs = ends[k % len(paces)][1]
        a, b = pairs[(mix >> 8) % len(pairs)]
        mix = (mix * 1103515245 + 12345) % 2147483648
        how, far = (mix >> 8) % 4, 1 + (mix >> 12 & 31) ** 3 // CFG["span"]
        i, early = (b, True) if how == 0 else (a, how == 1)
        if how == 3:
            i, early = (mix >> 3) % n, mix >> 11 & 1
        p = q = at[i]
        while far and (p > 0 if early else q < n - 1):
            p, q = (p - 1, q) if early else (p, q + 1)
            far -= eng[seq[p if early else q]] == eng[i]
        part = seq[p:q + 1]
        tied = [x == i or (older[i] >> x & 1 if early else older[x] >> i & 1) for x in part]
        new = seq[:p] + [x for x, y in zip(part, tied) if y == early] + [x for x, y in zip(part, tied) if y != early] + seq[q + 1:]
        room, worse, fresh = CFG["heat"] * (1 - k / CFG["shakes"]) * (mix >> 20 & 7) / 4, 0.0, False
        if [x for x in new[p:q + 1] if eng[x] == eng[i]] == [x for x in part if eng[x] == eng[i]]:
            continue
        for (c, b), m, (e, _) in zip(paces, PACE, ends):
            worse += again(new, p, q, c, b, e) / m[0]
            if worse > room + 200:
                break
        if worse <= room:
            tried = [held(new, c, b) for c, b in paces]
            score = sum(max(e[i] + lat[i] for i in tail) / m[0] for (e, _), m in zip(tried, PACE))
            if score <= now[0] + room:
                now, ends, fresh = (score, new), tried, True
    _ORDER["order"] = best[1]
    _ORDER["spans"] = [replay(best[1], c, b) for c, b in paces]
    return [ops[i] for i in best[1]]


def order(ops):
    hazards(ops)
    known, count = {}, {}
    for o in ops:
        count[o["key"]] = count.get(o["key"], 0) + 1
        o["idx"] = count[o["key"]]
        kn = known.setdefault(o["e"], {})
        need = {}
        for j in o["wait"]:
            p = ops[j]
            if p["idx"] > kn.get(p["key"], 0) and p["idx"] > need.get(p["key"], (0, 0))[0]:
                need[p["key"]] = (p["idx"], j)
        waits = []
        for key in sorted(need, key=lambda k: -need[k][1]):
            idx, j = need[key]
            if idx > kn.get(key, 0):
                waits.append(j)
                ops[j]["sig"] = True
                kn[key] = idx if ops[j]["sem"] is None else 10 ** 6
                for k2, v2 in ops[j]["vc"].items():
                    if v2 > kn.get(k2, 0):
                        kn[k2] = v2
        o["waits"] = waits
        o["vc"] = dict(kn)
    return count


def rank_program(g, core, T, topo):
    rank = T.rank_of(core)
    if rank is None:
        return
    ops = schedule(build(T, rank, topo, core))
    count = order(ops)
    queue = {"V": g.vector, "S": g.scalar, "P": g.tensor, "G": g, "Y": g.sync}
    landed = 8 * CFG["calls"]
    raised = {}
    for o in ops:
        if o["sem"] is None and o.get("sig"):
            raised[o["e"]] = raised.get(o["e"], 0) + 1
            o["val"] = raised[o["e"]]
    for o in ops:
        q = queue[o["e"]]
        for j in o["waits"]:
            p = ops[j]
            if p["sem"] is None:
                q.wait_ge(T.sem["e" + p["e"]], p["val"])
            else:
                q.wait_ge(T.sem[p["sem"]], 16 * count[p["sem"]])
        if o["arr"] is not None:
            q.wait_ge(T.sem["arr%d" % o["arr"]], landed)
        ins = o["f"](q)
        if o["sem"] is not None:
            ins.then_inc(T.sem[o["sem"]], 16)
        elif o.get("sig"):
            ins.then_inc(T.sem["e" + o["e"]], 1)
    for n in ("dya", "dyo", "dyy", "dyx", "dyc", "dyd"):
        g.wait_ge(T.sem[n], 16)
    for t in range(R - 1):
        g.wait_ge(T.sem["snt%d" % t], landed)
